import numpy as np
import ml_dtypes


def mxq(x, axis, fmt="e4m3"):
    dtype, down = {"e4m3": (ml_dtypes.float8_e4m3fn, 7), "e5m2": (ml_dtypes.float8_e5m2, 14)}[fmt]
    v = np.moveaxis(np.asarray(x, np.float32).astype(ml_dtypes.bfloat16).astype(np.float64), axis, -1)
    blocks = v.reshape(v.shape[:-1] + (-1, 32))
    amax = np.abs(blocks).max(-1, keepdims=True)
    byte = np.maximum(np.where(amax > 0, np.frexp(amax)[1] - 1 + 127, 0) - down, 1)
    scale = np.exp2(byte - 127.0)
    codes = (blocks / scale).astype(np.float32).astype(dtype).astype(np.float64)
    return np.moveaxis((codes * scale).reshape(v.shape), -1, axis)


WIDE = False


def mx_kscale(k):
    if not WIDE:
        return np.ones(k)
    levels = np.array([10, -10, 5, -5, 0])
    if k % 512:
        return np.exp2(np.random.permutation(np.resize(levels, k // 32))).repeat(32)
    a = np.empty((k // 512, 16))
    for p in range(k // 512):
        a[p, :8] = np.random.permutation(np.resize(levels, 8))
        for g in range(8):
            far = levels[np.abs(levels - a[p, g]) >= 10]
            a[p, g + 8] = far[np.random.randint(len(far))]
    return np.exp2(a.ravel()).repeat(32)


def f64(x):
    return np.asarray(x).astype(np.float64)


def striped(idx):
    return np.tile(idx.reshape(-1, 16).T, (8, 1)).astype(np.uint16)


def unstriped(offs):
    return offs[:16].T.reshape(-1).astype(np.int64)


def relu(v):
    return np.maximum(v, 0.0)


K, T, D, S, V, N = 1024, 2048, 4, 512, 256, 512


def setup_inputs():
    n = np.random.standard_normal
    s = mx_kscale(K)[:, None]
    return {
        "xT": (n((K, T)) * s).astype(np.float32),
        "w": (n((K, N)) / np.sqrt(K) / s).astype(np.float32),
        "b": (0.3 * n((N, 1))).astype(np.float32),
        "gate": np.tile(np.random.uniform(0.2, 1.0, (D, 1, V)) / np.sqrt(D), (1, N, 1)).astype(np.float32),
        "offs": striped(np.random.permutation(T)[:S]),
        "pos1": striped(np.random.permutation(S)[:V]),
        "pos2": striped(np.random.permutation(S)[:V]),
        "pos3": striped(np.random.permutation(S)[:V]),
        "pos4": striped(np.random.permutation(S)[:V]),
    }


def reference(xT, w, b, gate, offs, pos1, pos2, pos3, pos4):
    idx = unstriped(offs)
    xq = mxq(f64(xT)[:, idx], 0, "e4m3")
    y = mxq(f64(w), 0, "e4m3").T @ xq
    y = relu(y + f64(b))
    return sum(f64(gate[d]) * y[:, unstriped(p)] for d, p in enumerate((pos1, pos2, pos3, pos4)))

@@ -1,0 +1,187 @@
+from contextlib import ExitStack
+
+import concourse.mybir as mybir
+from concourse.masks import make_identity
+
+F32 = mybir.dt.float32
+BF16 = mybir.dt.bfloat16
+U32 = mybir.dt.uint32
+U16 = mybir.dt.uint16
+U8 = mybir.dt.uint8
+FP8X4 = mybir.dt.float8_e4m3fn_x4
+MULT = mybir.AluOpType.mult
+ADD = mybir.AluOpType.add
+RELU = mybir.ActivationFunctionType.Relu
+
+K, T, D, S, V, N = 1024, 2048, 4, 512, 256, 512
+P = 128
+PACK = 4
+PASSES = K // (P * PACK)
+BLOCKS = N // P
+HALF = S // 2
+FLOPS = 2 * N * K * S
+
+
+def tile_picked_sub_lin_relu_sub_e_kernel(tc, xT, w, b, gate, offs, pos1, pos2, pos3, pos4, out):
+    nc = tc.nc
+    positions = (pos1, pos2, pos3, pos4)
+    with ExitStack() as ctx:
+        lists = ctx.enter_context(tc.tile_pool(name="lists", bufs=1))
+        keep = ctx.enter_context(tc.tile_pool(name="keep", bufs=1))
+        work = ctx.enter_context(tc.tile_pool(name="work", bufs=2))
+        psum = ctx.enter_context(tc.psum_pool(name="psum", bufs=1))
+
+        xv = xT.rearrange("(a p j) t -> a j p t", a=PASSES, j=PACK)
+        wv = w.rearrange("(a p j) n -> a p j n", a=PASSES, j=PACK)
+        gv = gate.rearrange("d (c p) v -> c p d v", c=BLOCKS)
+        ov = out.rearrange("(c p) v -> c p v", c=BLOCKS)
+
+        offs_sb = lists.tile([P, S // 16], U16, name="offs_sb")
+        pos_sb = [lists.tile([P, V // 16], U16, name=f"pos_sb{d}") for d in range(D)]
+        w_raw = [keep.tile([P, PACK, N], F32, name=f"w_raw{a}") for a in range(PASSES)]
+        x_sb = [[keep.tile([P, T], F32, name=f"x_sb{a}{j}", tag=f"x_sb{a}{j}", align_bytes=64) for j in range(PACK)] for a in range(PASSES)]
+        gate_sb = [keep.tile([P, D, V], F32, name=f"gate_sb{c}") for c in range(BLOCKS)]
+        b_cols = keep.tile([P, BLOCKS], F32, name="b_cols")
+
+        b_rows = keep.tile([P, P], F32, name="b_rows")
+        nc.vector.memset(b_rows[:], 0.0)
+        nc.scalar.dma_start(b_rows[0:BLOCKS, :], b.rearrange("(c p) o -> c (p o)", c=BLOCKS))
+        nc.sync.dma_start(offs_sb[:], offs)
+        nc.sync.dma_start(w_raw[0][:], wv[0])
+        for a in range(PASSES):
+            for j in range(PACK):
+                nc.sync.dma_start(x_sb[a][j][:], xv[a, j])
+        nc.sync.dma_start(w_raw[1][:], wv[1])
+        nc.sync.dma_start(gate_sb[0][:], gv[0])
+        for d in range(D):
+            nc.sync.dma_start(pos_sb[d][:], positions[d])
+        for c in range(1, BLOCKS):
+            nc.sync.dma_start(gate_sb[c][:], gv[c])
+
+        ident = keep.tile([P, P], F32, name="ident")
+        make_identity(nc, ident[:])
+        b_turned = psum.tile([P, V], F32, name="back")
+        nc.tensor.transpose(b_turned[:, 0:P], b_rows[:], ident[:])
+        nc.scalar.copy(b_cols[:], b_turned[:, 0:BLOCKS])
+        b_held = keep.tile([P, 1], F32, name="b_held", tag="w_grp_last", align_bytes=64)
+        nc.scalar.copy(b_held[:], b_turned[:, 0:1])
+
+        w_codes = [keep.tile([P, N], U32, name=f"w_codes{a}", align_bytes=64) for a in range(PASSES)]
+        w_scales = [keep.tile([P, N], U8, name=f"w_scales{a}", align_bytes=64) for a in range(PASSES)]
+
+        def interleave_w(copy, grouped, a, c):
+            copy(grouped, w_raw[a][:, :, c * P : (c + 1) * P].rearrange("p j m -> p m j"))
+
+        def quantize_w(grouped, a, n0, n1):
+            nc.vector.quantize_mx(
+                out=w_codes[a][:, n0:n1].bitcast(FP8X4),
+                scales=w_scales[a][:, n0:n1],
+                in_=grouped.rearrange("p n j -> p (n j)"),
+            )
+
+        w_grp0 = keep.tile([P, N, PACK], BF16, name="w_grp0", align_bytes=64)
+        for c in range(BLOCKS):
+            interleave_w(nc.scalar.copy, w_grp0[:, c * P : (c + 1) * P, :], 0, c)
+        quantize_w(w_grp0[:], 0, 0, N)
+
+        x_grp = [keep.tile([P, S, PACK], BF16, name=f"x_grp{a}", align_bytes=64) for a in range(PASSES)]
+        x_codes = [keep.tile([P, S], U32, name=f"x_codes{a}", align_bytes=64) for a in range(PASSES)]
+        x_scales = [keep.tile([P, S], U8, name=f"x_scales{a}", align_bytes=64) for a in range(PASSES)]
+        y_sb = [keep.tile([P, S], F32, name=f"y_sb{c}") for c in range(BLOCKS)]
+
+        def gather_x(a, j, s0, s1):
+            nc.vector.tensor_copy(x_grp[a][:, s0:s1, j], x_sb[a][j][:].indirect(offs_sb[:, s0 // 16 : s1 // 16]))
+
+        def quantize_x(a, s0, s1):
+            nc.vector.quantize_mx(
+                out=x_codes[a][:, s0:s1].bitcast(FP8X4),
+                scales=x_scales[a][:, s0:s1],
+                in_=x_grp[a][:, s0:s1, :].rearrange("p s j -> p (s j)"),
+            )
+
+        def multiply(acc, c, a, s0, s1):
+            nc.tensor.matmul_mx(
+                out=acc[:],
+                lhsT=w_codes[a][:, c * P : (c + 1) * P].bitcast(FP8X4),
+                lhsT_scale=w_scales[a][:, c * P : (c + 1) * P],
+                rhs=x_codes[a][:, s0:s1].bitcast(FP8X4),
+                rhs_scale=x_scales[a][:, s0:s1],
+                start=(a == 0),
+                stop=(a == PASSES - 1),
+            )
+
+        def finish(acc, c, s0, s1):
+            bias = b_held[:] if c == 0 else b_cols[:, c : c + 1]
+            nc.scalar.activation(y_sb[c][:, s0:s1], acc[:], RELU, bias=bias)
+
+        for j in range(PACK):
+            gather_x(0, j, 0, S)
+        quantize_x(0, 0, S)
+        pieces = [(0, 0, HALF), (0, HALF, S)] + [(c, 0, S) for c in range(1, BLOCKS)]
+        accs = [psum.tile([P, s1 - s0], F32, name=f"acc{i}") for i, (c, s0, s1) in enumerate(pieces)]
+        for acc, (c, s0, s1) in zip(accs, pieces):
+            multiply(acc, c, 0, s0, s1)
+        for j in range(PACK):
+            gather_x(1, j, 0, S)
+        quantize_x(1, 0, S)
+
+        def late_weights(c, grouped):
+            interleave_w(nc.vector.tensor_copy if c == 0 else nc.scalar.copy, grouped, 1, c)
+            quantize_w(grouped, 1, c * P, (c + 1) * P)
+
+        def close(c):
+            for acc, (block, s0, s1) in zip(accs, pieces):
+                if block == c:
+                    multiply(acc, c, 1, s0, s1)
+                    finish(acc, c, s0, s1)
+
+        w_grp1 = keep.tile([P, 2 * P, PACK], BF16, name="w_grp1", tag="x_sb13", align_bytes=64)
+        late_weights(0, w_grp1[:, 0:P, :])
+        close(0)
+        late_weights(1, w_grp1[:, P : 2 * P, :])
+        close(1)
+
+        prods = [[keep.tile([P, V], F32, name=f"prod{c}{d}") for d in range(D)] for c in range(BLOCKS)]
+
+        def neighbour(c, d):
+            nc.vector.tensor_tensor(prods[c][d][:], y_sb[c][:].indirect(pos_sb[d][:]), gate_sb[c][:, d, :], MULT)
+
+        def add_up(c, count):
+            banks = [psum.tile([P, P], F32, name=f"sum_t{h}") for h in range(V // P)]
+            for d in range(count):
+                for h in range(V // P):
+                    nc.tensor.matmul(
+                        banks[h][:],
+                        prods[c][d][:, h * P : (h + 1) * P],
+                        ident[:],
+                        start=(d == 0),
+                        stop=(d == count - 1),
+                        is_transpose=True,
+                    )
+            turned = work.tile([P, V], F32, name="turned")
+            for h in range(V // P):
+                nc.scalar.copy(turned[:, h * P : (h + 1) * P], banks[h][:])
+            back = psum.tile([P, V], F32, name="back")
+            for h in range(V // P):
+                nc.tensor.transpose(back[:, h * P : (h + 1) * P], turned[:, h * P : (h + 1) * P], ident[:])
+            return back
+
+        def store(c, total):
+            nc.sync.dma_start(ov[c], total[:])
+
+        w_grp_last = keep.tile([P, 2 * P, PACK], BF16, name="w_grp_last", tag="w_grp_last", align_bytes=64)
+        for c in range(BLOCKS):
+            for d in range(D):
+                neighbour(c, d)
+                if c == 0 and d in (1, 2):
+                    late_weights(d + 1, w_grp_last[:, (d - 1) * P : d * P, :])
+                    close(d + 1)
+            total = keep.tile([P, V], F32, name=f"total{c}")
+            if c < BLOCKS - 1:
+                nc.scalar.copy(total[:], add_up(c, D)[:])
+            else:
+                back = add_up(c, 2)
+                pair = keep.tile([P, V], F32, name="pair")
+                nc.vector.tensor_tensor(pair[:], prods[c][2][:], prods[c][3][:], ADD)
+                nc.vector.tensor_tensor(total[:], pair[:], back[:], ADD)
+            store(c, total)

@@ -11,6 +11,7 @@ U8 = mybir.dt.uint8
 FP8X4 = mybir.dt.float8_e4m3fn_x4
 MULT = mybir.AluOpType.mult
 ADD = mybir.AluOpType.add
+MAX = mybir.AluOpType.max
 RELU = mybir.ActivationFunctionType.Relu
 
 K, T, D, S, V, N = 1024, 2048, 4, 512, 256, 512
@@ -19,7 +20,9 @@ PACK = 4
 PASSES = K // (P * PACK)
 BLOCKS = N // P
 HALF = S // 2
+VH = V // P
 FLOPS = 2 * N * K * S
+BYTES = 4 * (K * T + K * N + N + D * V + N * V) + 2 * P * (S + D * V) // 16
 
 
 def tile_picked_sub_lin_relu_sub_e_kernel(tc, xT, w, b, gate, offs, pos1, pos2, pos3, pos4, out):
@@ -30,59 +33,81 @@ def tile_picked_sub_lin_relu_sub_e_kernel(tc, xT, w, b, gate, offs, pos1, pos2, 
         keep = ctx.enter_context(tc.tile_pool(name="keep", bufs=1))
         work = ctx.enter_context(tc.tile_pool(name="work", bufs=2))
         psum = ctx.enter_context(tc.psum_pool(name="psum", bufs=1))
+        psum2 = ctx.enter_context(tc.psum_pool(name="psum2", bufs=2))
 
         xv = xT.rearrange("(a p j) t -> a j p t", a=PASSES, j=PACK)
-        wv = w.rearrange("(a p j) n -> a p j n", a=PASSES, j=PACK)
-        gv = gate.rearrange("d (c p) v -> c p d v", c=BLOCKS)
+        wv = w.rearrange("(a p j) (c m) -> a c p j m", a=PASSES, j=PACK, c=BLOCKS)
         ov = out.rearrange("(c p) v -> c p v", c=BLOCKS)
 
         offs_sb = lists.tile([P, S // 16], U16, name="offs_sb")
         pos_sb = [lists.tile([P, V // 16], U16, name=f"pos_sb{d}") for d in range(D)]
-        w_raw = [keep.tile([P, PACK, N], F32, name=f"w_raw{a}") for a in range(PASSES)]
+        w_raw = [[keep.tile([P, PACK, P], F32, name=f"w_raw{a}{c}") for c in range(BLOCKS)] for a in range(PASSES)]
         x_sb = [[keep.tile([P, T], F32, name=f"x_sb{a}{j}", tag=f"x_sb{a}{j}", align_bytes=64) for j in range(PACK)] for a in range(PASSES)]
-        gate_sb = [keep.tile([P, D, V], F32, name=f"gate_sb{c}") for c in range(BLOCKS)]
-        b_cols = keep.tile([P, BLOCKS], F32, name="b_cols")
 
-        b_rows = keep.tile([P, P], F32, name="b_rows")
-        nc.vector.memset(b_rows[:], 0.0)
-        nc.scalar.dma_start(b_rows[0:BLOCKS, :], b.rearrange("(c p) o -> c (p o)", c=BLOCKS))
-        nc.sync.dma_start(offs_sb[:], offs)
-        nc.sync.dma_start(w_raw[0][:], wv[0])
-        for a in range(PASSES):
-            for j in range(PACK):
-                nc.sync.dma_start(x_sb[a][j][:], xv[a, j])
-        nc.sync.dma_start(w_raw[1][:], wv[1])
-        nc.sync.dma_start(gate_sb[0][:], gv[0])
-        for d in range(D):
-            nc.sync.dma_start(pos_sb[d][:], positions[d])
-        for c in range(1, BLOCKS):
-            nc.sync.dma_start(gate_sb[c][:], gv[c])
+        rows = keep.tile([P, V], F32, name="rows")
+        nc.vector.memset(rows[:], 0.0)
+        nc.scalar.dma_start(rows[0:D, :], gate[:, 0, :])
+        nc.scalar.dma_start(rows[D : D + BLOCKS, 0:P], b.rearrange("(c p) o -> c (p o)", c=BLOCKS))
+        planes = [(a, j) for a in range(PASSES) for j in range(PACK)]
+        for i, (a, j) in enumerate(planes):
+            nc.sync.dma_start(x_sb[a][j][:], xv[a, j])
+            if i == 0:
+                nc.sync.dma_start(offs_sb[:], offs)
+        for c in range(BLOCKS):
+            for a in range(PASSES):
+                nc.sync.dma_start(w_raw[a][c][:], wv[a, c])
+            if c == 0:
+                for d in range(D):
+                    nc.sync.dma_start(pos_sb[d][:], positions[d])
 
         ident = keep.tile([P, P], F32, name="ident")
         make_identity(nc, ident[:])
-        b_turned = psum.tile([P, V], F32, name="back")
-        nc.tensor.transpose(b_turned[:, 0:P], b_rows[:], ident[:])
-        nc.scalar.copy(b_cols[:], b_turned[:, 0:BLOCKS])
-        b_held = keep.tile([P, 1], F32, name="b_held", tag="w_grp_last", align_bytes=64)
-        nc.scalar.copy(b_held[:], b_turned[:, 0:1])
+        cols_ps = psum2.tile([P, VH, P], F32, name="back")
+        for h in range(VH):
+            nc.tensor.transpose(cols_ps[:, h, :], rows[:, h * P : (h + 1) * P], ident[:])
+        cols = keep.tile([P, VH, D + BLOCKS], F32, name="cols")
+        nc.scalar.copy(cols[:], cols_ps[:, :, 0 : D + BLOCKS])
+        gate_sb = keep.tile([P, D, V], F32, name="gate_sb")
+        for pair_of_turns in range(D // 2):
+            spread = psum2.tile([P, 2, V], F32, name="acc")
+            for e in range(2):
+                d = 2 * pair_of_turns + e
+                for h in range(VH):
+                    nc.tensor.transpose(spread[:, e, h * P : (h + 1) * P], cols[:, h, d : d + 1].to_broadcast([P, P]), ident[:])
+            nc.scalar.copy(gate_sb[:, 2 * pair_of_turns : 2 * pair_of_turns + 2, :], spread[:])
 
-        w_codes = [keep.tile([P, N], U32, name=f"w_codes{a}", align_bytes=64) for a in range(PASSES)]
-        w_scales = [keep.tile([P, N], U8, name=f"w_scales{a}", align_bytes=64) for a in range(PASSES)]
+        bias_held = []
+        for c, tag in enumerate(("late_scales", "slot3")):
+            one = keep.tile([P, 1], F32, name=f"bias{c}", tag=tag, align_bytes=64)
+            nc.scalar.copy(one[:], cols_ps[:, 0, D + c : D + c + 1])
+            bias_held.append(one)
 
-        def interleave_w(copy, grouped, a, c):
-            copy(grouped, w_raw[a][:, :, c * P : (c + 1) * P].rearrange("p j m -> p m j"))
+        def bias(c):
+            return bias_held[c][:] if c < len(bias_held) else cols[:, 0, D + c : D + c + 1]
 
-        def quantize_w(grouped, a, n0, n1):
-            nc.vector.quantize_mx(
-                out=w_codes[a][:, n0:n1].bitcast(FP8X4),
-                scales=w_scales[a][:, n0:n1],
-                in_=grouped.rearrange("p n j -> p (n j)"),
+        w_grp = {}
+        w_codes = {}
+        w_scales = {}
+
+        def interleave_w(a, c):
+            if c < BLOCKS - 1:
+                grouped = keep.tile([P, P, PACK], BF16, name=f"w_grp{a}{c}", tag=f"slot{a}{c}", align_bytes=64)
+                w_grp[a, c] = grouped[:]
+            elif a == 0:
+                both = keep.tile([P, PASSES * P, PACK], BF16, name="w_grp_last", tag="slot3", align_bytes=64)
+                for e in range(PASSES):
+                    w_grp[e, c] = both[:, e * P : (e + 1) * P, :]
+            nc.scalar.copy(
+                w_grp[a, c].rearrange("p (g i) j -> p g j i", i=4),
+                w_raw[a][c][:].rearrange("p j (g i) -> p g j i", i=4),
             )
 
-        w_grp0 = keep.tile([P, N, PACK], BF16, name="w_grp0", align_bytes=64)
-        for c in range(BLOCKS):
-            interleave_w(nc.scalar.copy, w_grp0[:, c * P : (c + 1) * P, :], 0, c)
-        quantize_w(w_grp0[:], 0, 0, N)
+        def quantize_w(a, c):
+            nc.vector.quantize_mx(
+                out=w_codes[a, c].bitcast(FP8X4),
+                scales=w_scales[a, c],
+                in_=w_grp[a, c].rearrange("p m j -> p (m j)"),
+            )
 
         x_grp = [keep.tile([P, S, PACK], BF16, name=f"x_grp{a}", align_bytes=64) for a in range(PASSES)]
         x_codes = [keep.tile([P, S], U32, name=f"x_codes{a}", align_bytes=64) for a in range(PASSES)]
@@ -102,86 +127,122 @@ def tile_picked_sub_lin_relu_sub_e_kernel(tc, xT, w, b, gate, offs, pos1, pos2, 
         def multiply(acc, c, a, s0, s1):
             nc.tensor.matmul_mx(
                 out=acc[:],
-                lhsT=w_codes[a][:, c * P : (c + 1) * P].bitcast(FP8X4),
-                lhsT_scale=w_scales[a][:, c * P : (c + 1) * P],
+                lhsT=w_codes[a, c].bitcast(FP8X4),
+                lhsT_scale=w_scales[a, c],
                 rhs=x_codes[a][:, s0:s1].bitcast(FP8X4),
                 rhs_scale=x_scales[a][:, s0:s1],
                 start=(a == 0),
                 stop=(a == PASSES - 1),
             )
 
-        def finish(acc, c, s0, s1):
-            bias = b_held[:] if c == 0 else b_cols[:, c : c + 1]
-            nc.scalar.activation(y_sb[c][:, s0:s1], acc[:], RELU, bias=bias)
-
+        halves = [(0, HALF), (HALF, S)]
         for j in range(PACK):
             gather_x(0, j, 0, S)
         quantize_x(0, 0, S)
-        pieces = [(0, 0, HALF), (0, HALF, S)] + [(c, 0, S) for c in range(1, BLOCKS)]
-        accs = [psum.tile([P, s1 - s0], F32, name=f"acc{i}") for i, (c, s0, s1) in enumerate(pieces)]
-        for acc, (c, s0, s1) in zip(accs, pieces):
-            multiply(acc, c, 0, s0, s1)
-        for j in range(PACK):
+        for j in range(PACK - 1):
             gather_x(1, j, 0, S)
-        quantize_x(1, 0, S)
+        for s0, s1 in halves:
+            gather_x(1, PACK - 1, s0, s1)
 
-        def late_weights(c, grouped):
-            interleave_w(nc.vector.tensor_copy if c == 0 else nc.scalar.copy, grouped, 1, c)
-            quantize_w(grouped, 1, c * P, (c + 1) * P)
+        pieces = [(a, c) for c in range(BLOCKS) for a in range(PASSES)]
+        early = 3
+        codes_all = keep.tile([P, len(pieces) * P], U32, name="codes_all", tag="x_sb13", align_bytes=64)
+        scales_early = keep.tile([P, early * P], U8, name="scales_early", align_bytes=64)
+        for i, piece in enumerate(pieces):
+            w_codes[piece] = codes_all[:, i * P : (i + 1) * P]
+        for i, piece in enumerate(pieces[:early]):
+            w_scales[piece] = scales_early[:, i * P : (i + 1) * P]
 
-        def close(c):
-            for acc, (block, s0, s1) in zip(accs, pieces):
-                if block == c:
-                    multiply(acc, c, 1, s0, s1)
-                    finish(acc, c, s0, s1)
+        def weights(a, c):
+            interleave_w(a, c)
+            quantize_w(a, c)
 
-        w_grp1 = keep.tile([P, 2 * P, PACK], BF16, name="w_grp1", tag="x_sb13", align_bytes=64)
-        late_weights(0, w_grp1[:, 0:P, :])
-        close(0)
-        late_weights(1, w_grp1[:, P : 2 * P, :])
-        close(1)
+        first = [psum.tile([P, HALF], F32, name=f"first{i}") for i in range(2)]
+        interleave_w(0, 0)
+        interleave_w(1, 0)
+        quantize_w(0, 0)
+        for acc, (s0, s1) in zip(first, halves):
+            multiply(acc, 0, 0, s0, s1)
+        for s0, s1 in halves:
+            quantize_x(1, s0, s1)
+        quantize_w(1, 0)
+        for acc, (s0, s1) in zip(first, halves):
+            multiply(acc, 0, 1, s0, s1)
+        accs = {1: psum2.tile([P, S], F32, name="acc")}
+        weights(0, 1)
+        for acc, (s0, s1) in zip(first, halves):
+            nc.vector.tensor_scalar(y_sb[0][:, s0:s1], acc[:], bias(0), 0.0, ADD, MAX)
+        multiply(accs[1], 1, 0, 0, S)
 
-        prods = [[keep.tile([P, V], F32, name=f"prod{c}{d}") for d in range(D)] for c in range(BLOCKS)]
+        scales_late = keep.tile([P, (len(pieces) - early) * P], U8, name="scales_late", tag="late_scales", align_bytes=64)
+        for i, piece in enumerate(pieces[early:]):
+            w_scales[piece] = scales_late[:, i * P : (i + 1) * P]
+
+        def layer(a, c):
+            if a == 0:
+                accs[c] = psum2.tile([P, S], F32, name="acc")
+            weights(a, c)
+            multiply(accs[c], c, a, 0, S)
+            if a == PASSES - 1:
+                nc.scalar.activation(y_sb[c][:], accs[c][:], RELU, bias=bias(c))
+
+        prods = {}
+        held = {0: "slot11", 1: "slot12", 2: "slot3", 3: "rest3"}
+        after = {(0, 0): (1, 1), (0, 1): (0, 2), (0, 3): (1, 2), (1, 1): (0, 3), (1, 2): (1, 3)}
 
         def neighbour(c, d):
-            nc.vector.tensor_tensor(prods[c][d][:], y_sb[c][:].indirect(pos_sb[d][:]), gate_sb[c][:, d, :], MULT)
+            if d == 0:
+                lead = keep.tile([P, V], F32, name=f"lead{c}")
+                prods[c, d] = lead[:]
+            elif d == 1:
+                rest = keep.tile([P, (D - 1) * V], F32, name=f"rest{c}", tag=held[c], align_bytes=64)
+                for e in range(1, D):
+                    prods[c, e] = rest[:, (e - 1) * V : e * V]
+            cuts = VH if (c, d) == (BLOCKS - 1, D - 1) else 1
+            width = V // cuts
+            for v0 in range(0, V, width):
+                nc.vector.tensor_tensor(
+                    prods[c, d][:, v0 : v0 + width],
+                    y_sb[c][:].indirect(pos_sb[d][:, v0 // 16 : (v0 + width) // 16]),
+                    gate_sb[:, d, v0 : v0 + width],
+                    MULT,
+                )
+            if (c, d) in after:
+                layer(*after[c, d])
 
         def add_up(c, count):
-            banks = [psum.tile([P, P], F32, name=f"sum_t{h}") for h in range(V // P)]
+            banks = [psum.tile([P, P], F32, name=f"sum_t{h}") for h in range(VH)]
             for d in range(count):
-                for h in range(V // P):
+                for h in range(VH):
                     nc.tensor.matmul(
                         banks[h][:],
-                        prods[c][d][:, h * P : (h + 1) * P],
+                        prods[c, d][:, h * P : (h + 1) * P],
                         ident[:],
                         start=(d == 0),
                         stop=(d == count - 1),
                         is_transpose=True,
                     )
             turned = work.tile([P, V], F32, name="turned")
-            for h in range(V // P):
+            for h in range(VH):
                 nc.scalar.copy(turned[:, h * P : (h + 1) * P], banks[h][:])
-            back = psum.tile([P, V], F32, name="back")
-            for h in range(V // P):
+            back = psum2.tile([P, V], F32, name="back")
+            for h in range(VH):
                 nc.tensor.transpose(back[:, h * P : (h + 1) * P], turned[:, h * P : (h + 1) * P], ident[:])
             return back
 
-        def store(c, total):
-            nc.sync.dma_start(ov[c], total[:])
-
-        w_grp_last = keep.tile([P, 2 * P, PACK], BF16, name="w_grp_last", tag="w_grp_last", align_bytes=64)
         for c in range(BLOCKS):
             for d in range(D):
                 neighbour(c, d)
-                if c == 0 and d in (1, 2):
-                    late_weights(d + 1, w_grp_last[:, (d - 1) * P : d * P, :])
-                    close(d + 1)
             total = keep.tile([P, V], F32, name=f"total{c}")
             if c < BLOCKS - 1:
                 nc.scalar.copy(total[:], add_up(c, D)[:])
+                nc.sync.dma_start(ov[c], total[:])
             else:
                 back = add_up(c, 2)
                 pair = keep.tile([P, V], F32, name="pair")
-                nc.vector.tensor_tensor(pair[:], prods[c][2][:], prods[c][3][:], ADD)
-                nc.vector.tensor_tensor(total[:], pair[:], back[:], ADD)
-            store(c, total)
+                parts = [slice(h * P, (h + 1) * P) for h in range(VH)]
+                for part in parts:
+                    nc.vector.tensor_tensor(pair[:, part], prods[c, 2][:, part], prods[c, 3][:, part], ADD)
+                for part, queue in zip(parts, (nc.scalar, nc.sync)):
+                    nc.vector.tensor_tensor(total[:, part], pair[:, part], back[:, part], ADD)
+                    queue.dma_start(ov[c][:, part], total[:, part])

@@ -36,12 +36,14 @@ def tile_picked_sub_lin_relu_sub_e_kernel(tc, xT, w, b, gate, offs, pos1, pos2, 
         psum2 = ctx.enter_context(tc.psum_pool(name="psum2", bufs=2))
 
         xv = xT.rearrange("(a p j) t -> a j p t", a=PASSES, j=PACK)
-        wv = w.rearrange("(a p j) (c m) -> a c p j m", a=PASSES, j=PACK, c=BLOCKS)
+        wv = w.rearrange("(a p j) n -> a p j n", a=PASSES, j=PACK)
         ov = out.rearrange("(c p) v -> c p v", c=BLOCKS)
 
         offs_sb = lists.tile([P, S // 16], U16, name="offs_sb")
         pos_sb = [lists.tile([P, V // 16], U16, name=f"pos_sb{d}") for d in range(D)]
-        w_raw = [[keep.tile([P, PACK, P], F32, name=f"w_raw{a}{c}") for c in range(BLOCKS)] for a in range(PASSES)]
+        w_loads = [(0, 1), (1, 2), (2, 4)]
+        w_tiles = {(a, c0): keep.tile([P, PACK, (c1 - c0) * P], F32, name=f"w_raw{a}{c0}") for c0, c1 in w_loads for a in range(PASSES)}
+        w_raw = {(a, c): w_tiles[a, c0][:, :, (c - c0) * P : (c - c0 + 1) * P] for c0, c1 in w_loads for c in range(c0, c1) for a in range(PASSES)}
         x_sb = [[keep.tile([P, T], F32, name=f"x_sb{a}{j}", tag=f"x_sb{a}{j}", align_bytes=64) for j in range(PACK)] for a in range(PASSES)]
 
         rows = keep.tile([P, V], F32, name="rows")
@@ -53,11 +55,11 @@ def tile_picked_sub_lin_relu_sub_e_kernel(tc, xT, w, b, gate, offs, pos1, pos2, 
             nc.sync.dma_start(x_sb[a][j][:], xv[a, j])
             if i == 0:
                 nc.sync.dma_start(offs_sb[:], offs)
-        for c in range(BLOCKS):
+        lists_behind = {(1, 0): (0,), (0, 1): (1,), (1, 1): (2, 3)}
+        for c0, c1 in w_loads:
             for a in range(PASSES):
-                nc.sync.dma_start(w_raw[a][c][:], wv[a, c])
-            if c == 0:
-                for d in range(D):
+                nc.sync.dma_start(w_tiles[a, c0][:], wv[a][:, :, c0 * P : c1 * P])
+                for d in lists_behind.get((a, c0), ()):
                     nc.sync.dma_start(pos_sb[d][:], positions[d])
 
         ident = keep.tile([P, P], F32, name="ident")
@@ -76,14 +78,14 @@ def tile_picked_sub_lin_relu_sub_e_kernel(tc, xT, w, b, gate, offs, pos1, pos2, 
                     nc.tensor.transpose(spread[:, e, h * P : (h + 1) * P], cols[:, h, d : d + 1].to_broadcast([P, P]), ident[:])
             nc.scalar.copy(gate_sb[:, 2 * pair_of_turns : 2 * pair_of_turns + 2, :], spread[:])
 
-        bias_held = []
-        for c, tag in enumerate(("late_scales", "slot3")):
-            one = keep.tile([P, 1], F32, name=f"bias{c}", tag=tag, align_bytes=64)
-            nc.scalar.copy(one[:], cols_ps[:, 0, D + c : D + c + 1])
-            bias_held.append(one)
-
-        def bias(c):
-            return bias_held[c][:] if c < len(bias_held) else cols[:, 0, D + c : D + c + 1]
+        bias_tags = {0: ("late_scales",), 1: ("slot12", "slot3"), 3: ("turn01",)}
+        biases = {2: [cols[:, 0, D + 2 : D + 3]]}
+        for c, tags in bias_tags.items():
+            biases[c] = []
+            for tag in tags:
+                one = keep.tile([P, 1], F32, name=f"bias_{tag}", tag=tag, align_bytes=64)
+                nc.scalar.copy(one[:], cols_ps[:, 0, D + c : D + c + 1])
+                biases[c].append(one[:])
 
         w_grp = {}
         w_codes = {}
@@ -98,8 +100,8 @@ def tile_picked_sub_lin_relu_sub_e_kernel(tc, xT, w, b, gate, offs, pos1, pos2, 
                 for e in range(PASSES):
                     w_grp[e, c] = both[:, e * P : (e + 1) * P, :]
             nc.scalar.copy(
-                w_grp[a, c].rearrange("p (g i) j -> p g j i", i=4),
-                w_raw[a][c][:].rearrange("p j (g i) -> p g j i", i=4),
+                w_grp[a, c].rearrange("p (g i) j -> p g j i", i=2),
+                w_raw[a, c].rearrange("p j (g i) -> p g j i", i=2),
             )
 
         def quantize_w(a, c):
@@ -171,7 +173,7 @@ def tile_picked_sub_lin_relu_sub_e_kernel(tc, xT, w, b, gate, offs, pos1, pos2, 
         accs = {1: psum2.tile([P, S], F32, name="acc")}
         weights(0, 1)
         for acc, (s0, s1) in zip(first, halves):
-            nc.vector.tensor_scalar(y_sb[0][:, s0:s1], acc[:], bias(0), 0.0, ADD, MAX)
+            nc.vector.tensor_scalar(y_sb[0][:, s0:s1], acc[:], biases[0][0], 0.0, ADD, MAX)
         multiply(accs[1], 1, 0, 0, S)
 
         scales_late = keep.tile([P, (len(pieces) - early) * P], U8, name="scales_late", tag="late_scales", align_bytes=64)
@@ -184,11 +186,14 @@ def tile_picked_sub_lin_relu_sub_e_kernel(tc, xT, w, b, gate, offs, pos1, pos2, 
             weights(a, c)
             multiply(accs[c], c, a, 0, S)
             if a == PASSES - 1:
-                nc.scalar.activation(y_sb[c][:], accs[c][:], RELU, bias=bias(c))
+                width = S // len(biases[c])
+                for i, one in enumerate(biases[c]):
+                    part = slice(i * width, (i + 1) * width)
+                    nc.scalar.activation(y_sb[c][:, part], accs[c][:, part], RELU, bias=one)
 
         prods = {}
         held = {0: "slot11", 1: "slot12", 2: "slot3", 3: "rest3"}
-        after = {(0, 0): (1, 1), (0, 1): (0, 2), (0, 3): (1, 2), (1, 1): (0, 3), (1, 2): (1, 3)}
+        after = {(0, 0): (1, 1), (0, 2): (0, 2), (1, 0): (1, 2), (1, 1): (0, 3), (1, 2): (1, 3)}
 
         def neighbour(c, d):
             if d == 0:
@@ -210,8 +215,10 @@ def tile_picked_sub_lin_relu_sub_e_kernel(tc, xT, w, b, gate, offs, pos1, pos2, 
             if (c, d) in after:
                 layer(*after[c, d])
 
+        turned_of = {}
+
         def add_up(c, count):
-            banks = [psum.tile([P, P], F32, name=f"sum_t{h}") for h in range(VH)]
+            banks = [psum.tile([P, P], F32, name=f"sum_t{h}", tag=f"first{h}" if c % 2 else f"sum_t{h}") for h in range(VH)]
             for d in range(count):
                 for h in range(VH):
                     nc.tensor.matmul(
@@ -222,7 +229,13 @@ def tile_picked_sub_lin_relu_sub_e_kernel(tc, xT, w, b, gate, offs, pos1, pos2, 
                         stop=(d == count - 1),
                         is_transpose=True,
                     )
-            turned = work.tile([P, V], F32, name="turned")
+            if c == 0:
+                two = keep.tile([P, 2 * V], F32, name="turned01", tag="turn01", align_bytes=64)
+                turned_of[0] = two[:, 0:V]
+                turned_of[1] = two[:, V : 2 * V]
+            elif c > 1:
+                turned_of[c] = work.tile([P, V], F32, name="turned")[:]
+            turned = turned_of[c]
             for h in range(VH):
                 nc.scalar.copy(turned[:, h * P : (h + 1) * P], banks[h][:])
             back = psum2.tile([P, V], F32, name="back")
@@ -230,19 +243,25 @@ def tile_picked_sub_lin_relu_sub_e_kernel(tc, xT, w, b, gate, offs, pos1, pos2, 
                 nc.tensor.transpose(back[:, h * P : (h + 1) * P], turned[:, h * P : (h + 1) * P], ident[:])
             return back
 
+        def finish(c):
+            total = keep.tile([P, V], F32, name=f"total{c}")
+            nc.scalar.copy(total[:], add_up(c, D)[:])
+            nc.sync.dma_start(ov[c], total[:])
+
         for c in range(BLOCKS):
             for d in range(D):
                 neighbour(c, d)
-            total = keep.tile([P, V], F32, name=f"total{c}")
-            if c < BLOCKS - 1:
-                nc.scalar.copy(total[:], add_up(c, D)[:])
-                nc.sync.dma_start(ov[c], total[:])
-            else:
-                back = add_up(c, 2)
-                pair = keep.tile([P, V], F32, name="pair")
-                parts = [slice(h * P, (h + 1) * P) for h in range(VH)]
-                for part in parts:
-                    nc.vector.tensor_tensor(pair[:, part], prods[c, 2][:, part], prods[c, 3][:, part], ADD)
-                for part, queue in zip(parts, (nc.scalar, nc.sync)):
-                    nc.vector.tensor_tensor(total[:, part], pair[:, part], back[:, part], ADD)
-                    queue.dma_start(ov[c][:, part], total[:, part])
+            if c == 1:
+                finish(0)
+            if c in (1, 2):
+                finish(c)
+        c = BLOCKS - 1
+        total = keep.tile([P, V], F32, name="total_last")
+        back = add_up(c, 2)
+        pair = keep.tile([P, V], F32, name="pair")
+        parts = [slice(h * P, (h + 1) * P) for h in range(VH)]
+        for part in parts:
+            nc.vector.tensor_tensor(pair[:, part], prods[c, 2][:, part], prods[c, 3][:, part], ADD)
+        for part, queue in zip(parts, (nc.scalar, nc.sync)):
+            nc.vector.tensor_tensor(total[:, part], pair[:, part], back[:, part], ADD)
+            queue.dma_start(ov[c][:, part], total[:, part])

@@ -41,7 +41,7 @@ def tile_picked_sub_lin_relu_sub_e_kernel(tc, xT, w, b, gate, offs, pos1, pos2, 
 
         offs_sb = lists.tile([P, S // 16], U16, name="offs_sb")
         pos_sb = [lists.tile([P, V // 16], U16, name=f"pos_sb{d}") for d in range(D)]
-        w_loads = [(0, 1), (1, 2), (2, 4)]
+        w_loads = [(c, c + 1) for c in range(BLOCKS)]
         w_tiles = {(a, c0): keep.tile([P, PACK, (c1 - c0) * P], F32, name=f"w_raw{a}{c0}") for c0, c1 in w_loads for a in range(PASSES)}
         w_raw = {(a, c): w_tiles[a, c0][:, :, (c - c0) * P : (c - c0 + 1) * P] for c0, c1 in w_loads for c in range(c0, c1) for a in range(PASSES)}
         x_sb = [[keep.tile([P, T], F32, name=f"x_sb{a}{j}", tag=f"x_sb{a}{j}", align_bytes=64) for j in range(PACK)] for a in range(PASSES)]
@@ -78,8 +78,8 @@ def tile_picked_sub_lin_relu_sub_e_kernel(tc, xT, w, b, gate, offs, pos1, pos2, 
                     nc.tensor.transpose(spread[:, e, h * P : (h + 1) * P], cols[:, h, d : d + 1].to_broadcast([P, P]), ident[:])
             nc.scalar.copy(gate_sb[:, 2 * pair_of_turns : 2 * pair_of_turns + 2, :], spread[:])
 
-        bias_tags = {0: ("late_scales",), 1: ("slot12", "slot3"), 3: ("turn01",)}
-        biases = {2: [cols[:, 0, D + 2 : D + 3]]}
+        bias_tags = {0: ("late_scales",), 1: ("slot12", "slot03"), 2: ("slot13", "turn01")}
+        biases = {3: [cols[:, 0, D + 3 : D + 4]]}
         for c, tags in bias_tags.items():
             biases[c] = []
             for tag in tags:
@@ -92,13 +92,8 @@ def tile_picked_sub_lin_relu_sub_e_kernel(tc, xT, w, b, gate, offs, pos1, pos2, 
         w_scales = {}
 
         def interleave_w(a, c):
-            if c < BLOCKS - 1:
-                grouped = keep.tile([P, P, PACK], BF16, name=f"w_grp{a}{c}", tag=f"slot{a}{c}", align_bytes=64)
-                w_grp[a, c] = grouped[:]
-            elif a == 0:
-                both = keep.tile([P, PASSES * P, PACK], BF16, name="w_grp_last", tag="slot3", align_bytes=64)
-                for e in range(PASSES):
-                    w_grp[e, c] = both[:, e * P : (e + 1) * P, :]
+            grouped = keep.tile([P, P, PACK], BF16, name=f"w_grp{a}{c}", tag=f"slot{a}{c}", align_bytes=64)
+            w_grp[a, c] = grouped[:]
             nc.scalar.copy(
                 w_grp[a, c].rearrange("p (g i) j -> p g j i", i=2),
                 w_raw[a, c].rearrange("p j (g i) -> p g j i", i=2),
@@ -147,7 +142,7 @@ def tile_picked_sub_lin_relu_sub_e_kernel(tc, xT, w, b, gate, offs, pos1, pos2, 
             gather_x(1, PACK - 1, s0, s1)
 
         pieces = [(a, c) for c in range(BLOCKS) for a in range(PASSES)]
-        early = 3
+        early = 2
         codes_all = keep.tile([P, len(pieces) * P], U32, name="codes_all", tag="x_sb13", align_bytes=64)
         scales_early = keep.tile([P, early * P], U8, name="scales_early", align_bytes=64)
         for i, piece in enumerate(pieces):
@@ -170,11 +165,9 @@ def tile_picked_sub_lin_relu_sub_e_kernel(tc, xT, w, b, gate, offs, pos1, pos2, 
         quantize_w(1, 0)
         for acc, (s0, s1) in zip(first, halves):
             multiply(acc, 0, 1, s0, s1)
-        accs = {1: psum2.tile([P, S], F32, name="acc")}
-        weights(0, 1)
+        accs = {}
         for acc, (s0, s1) in zip(first, halves):
             nc.vector.tensor_scalar(y_sb[0][:, s0:s1], acc[:], biases[0][0], 0.0, ADD, MAX)
-        multiply(accs[1], 1, 0, 0, S)
 
         scales_late = keep.tile([P, (len(pieces) - early) * P], U8, name="scales_late", tag="late_scales", align_bytes=64)
         for i, piece in enumerate(pieces[early:]):
@@ -191,9 +184,10 @@ def tile_picked_sub_lin_relu_sub_e_kernel(tc, xT, w, b, gate, offs, pos1, pos2, 
                     part = slice(i * width, (i + 1) * width)
                     nc.scalar.activation(y_sb[c][:, part], accs[c][:, part], RELU, bias=one)
 
+        layer(0, 1)
         prods = {}
-        held = {0: "slot11", 1: "slot12", 2: "slot3", 3: "rest3"}
-        after = {(0, 0): (1, 1), (0, 2): (0, 2), (1, 0): (1, 2), (1, 1): (0, 3), (1, 2): (1, 3)}
+        held = {0: "slot11", 1: "slot12", 2: "slot13", 3: "rest3"}
+        after = {(0, 0): (1, 1), (0, 2): (0, 2), (1, 0): (1, 2), (1, 2): (0, 3), (2, 0): (1, 3)}
 
         def neighbour(c, d):
             if d == 0:
@@ -251,10 +245,9 @@ def tile_picked_sub_lin_relu_sub_e_kernel(tc, xT, w, b, gate, offs, pos1, pos2, 
         for c in range(BLOCKS):
             for d in range(D):
                 neighbour(c, d)
-            if c == 1:
-                finish(0)
-            if c in (1, 2):
-                finish(c)
+            if c == 2:
+                for done in range(c + 1):
+                    finish(done)
         c = BLOCKS - 1
         total = keep.tile([P, V], F32, name="total_last")
         back = add_up(c, 2)
@@ -262,6 +255,6 @@ def tile_picked_sub_lin_relu_sub_e_kernel(tc, xT, w, b, gate, offs, pos1, pos2, 
         parts = [slice(h * P, (h + 1) * P) for h in range(VH)]
         for part in parts:
             nc.vector.tensor_tensor(pair[:, part], prods[c, 2][:, part], prods[c, 3][:, part], ADD)
-        for part, queue in zip(parts, (nc.scalar, nc.sync)):
+        for part in parts:
             nc.vector.tensor_tensor(total[:, part], pair[:, part], back[:, part], ADD)
-            queue.dma_start(ov[c][:, part], total[:, part])
+            nc.sync.dma_start(ov[c][:, part], total[:, part])

@@ -31,7 +31,6 @@ def tile_picked_sub_lin_relu_sub_e_kernel(tc, xT, w, b, gate, offs, pos1, pos2, 
     with ExitStack() as ctx:
         lists = ctx.enter_context(tc.tile_pool(name="lists", bufs=1))
         keep = ctx.enter_context(tc.tile_pool(name="keep", bufs=1))
-        work = ctx.enter_context(tc.tile_pool(name="work", bufs=2))
         psum = ctx.enter_context(tc.psum_pool(name="psum", bufs=1))
         psum2 = ctx.enter_context(tc.psum_pool(name="psum2", bufs=2))
 
@@ -42,7 +41,7 @@ def tile_picked_sub_lin_relu_sub_e_kernel(tc, xT, w, b, gate, offs, pos1, pos2, 
         offs_sb = lists.tile([P, S // 16], U16, name="offs_sb")
         pos_sb = [lists.tile([P, V // 16], U16, name=f"pos_sb{d}") for d in range(D)]
         w_loads = [(c, c + 1) for c in range(BLOCKS)]
-        w_tiles = {(a, c0): keep.tile([P, PACK, (c1 - c0) * P], F32, name=f"w_raw{a}{c0}") for c0, c1 in w_loads for a in range(PASSES)}
+        w_tiles = {(a, c0): keep.tile([P, PACK, (c1 - c0) * P], F32, name=f"w_raw{a}{c0}", tag=f"w_raw{a}{c0}", align_bytes=64) for c0, c1 in w_loads for a in range(PASSES)}
         w_raw = {(a, c): w_tiles[a, c0][:, :, (c - c0) * P : (c - c0 + 1) * P] for c0, c1 in w_loads for c in range(c0, c1) for a in range(PASSES)}
         x_sb = [[keep.tile([P, T], F32, name=f"x_sb{a}{j}", tag=f"x_sb{a}{j}", align_bytes=64) for j in range(PACK)] for a in range(PASSES)]
 
@@ -71,14 +70,14 @@ def tile_picked_sub_lin_relu_sub_e_kernel(tc, xT, w, b, gate, offs, pos1, pos2, 
         nc.scalar.copy(cols[:], cols_ps[:, :, 0 : D + BLOCKS])
         gate_sb = keep.tile([P, D, V], F32, name="gate_sb")
         for pair_of_turns in range(D // 2):
-            spread = psum2.tile([P, 2, V], F32, name="acc")
+            spread = psum.tile([P, 2, V], F32, name="spread", tag=f"acc{pair_of_turns + 1}")
             for e in range(2):
                 d = 2 * pair_of_turns + e
                 for h in range(VH):
                     nc.tensor.transpose(spread[:, e, h * P : (h + 1) * P], cols[:, h, d : d + 1].to_broadcast([P, P]), ident[:])
             nc.scalar.copy(gate_sb[:, 2 * pair_of_turns : 2 * pair_of_turns + 2, :], spread[:])
 
-        bias_tags = {0: ("late_scales",), 1: ("slot12", "slot03"), 2: ("slot13", "turn01")}
+        bias_tags = {0: ("late_scales", "slot11"), 1: ("slot12", "slot3"), 2: ("turned0",)}
         biases = {3: [cols[:, 0, D + 3 : D + 4]]}
         for c, tags in bias_tags.items():
             biases[c] = []
@@ -92,8 +91,13 @@ def tile_picked_sub_lin_relu_sub_e_kernel(tc, xT, w, b, gate, offs, pos1, pos2, 
         w_scales = {}
 
         def interleave_w(a, c):
-            grouped = keep.tile([P, P, PACK], BF16, name=f"w_grp{a}{c}", tag=f"slot{a}{c}", align_bytes=64)
-            w_grp[a, c] = grouped[:]
+            if c < BLOCKS - 1:
+                grouped = keep.tile([P, P, PACK], BF16, name=f"w_grp{a}{c}", tag=f"slot{a}{c}", align_bytes=64)
+                w_grp[a, c] = grouped[:]
+            elif a == 0:
+                both = keep.tile([P, PASSES * P, PACK], BF16, name="w_grp_last", tag="slot3", align_bytes=64)
+                for e in range(PASSES):
+                    w_grp[e, c] = both[:, e * P : (e + 1) * P, :]
             nc.scalar.copy(
                 w_grp[a, c].rearrange("p (g i) j -> p g j i", i=2),
                 w_raw[a, c].rearrange("p j (g i) -> p g j i", i=2),
@@ -107,7 +111,7 @@ def tile_picked_sub_lin_relu_sub_e_kernel(tc, xT, w, b, gate, offs, pos1, pos2, 
             )
 
         x_grp = [keep.tile([P, S, PACK], BF16, name=f"x_grp{a}", align_bytes=64) for a in range(PASSES)]
-        x_codes = [keep.tile([P, S], U32, name=f"x_codes{a}", align_bytes=64) for a in range(PASSES)]
+        x_codes = [keep.tile([P, S], U32, name="x_codes0", align_bytes=64)]
         x_scales = [keep.tile([P, S], U8, name=f"x_scales{a}", align_bytes=64) for a in range(PASSES)]
         y_sb = [keep.tile([P, S], F32, name=f"y_sb{c}") for c in range(BLOCKS)]
 
@@ -143,7 +147,7 @@ def tile_picked_sub_lin_relu_sub_e_kernel(tc, xT, w, b, gate, offs, pos1, pos2, 
 
         pieces = [(a, c) for c in range(BLOCKS) for a in range(PASSES)]
         early = 2
-        codes_all = keep.tile([P, len(pieces) * P], U32, name="codes_all", tag="x_sb13", align_bytes=64)
+        codes_all = keep.tile([P, len(pieces) * P], U32, name="codes_all", align_bytes=64)
         scales_early = keep.tile([P, early * P], U8, name="scales_early", align_bytes=64)
         for i, piece in enumerate(pieces):
             w_codes[piece] = codes_all[:, i * P : (i + 1) * P]
@@ -160,14 +164,15 @@ def tile_picked_sub_lin_relu_sub_e_kernel(tc, xT, w, b, gate, offs, pos1, pos2, 
         quantize_w(0, 0)
         for acc, (s0, s1) in zip(first, halves):
             multiply(acc, 0, 0, s0, s1)
+        x_codes.append(keep.tile([P, S], U32, name="x_codes1", tag="w_raw00", align_bytes=64))
         for s0, s1 in halves:
             quantize_x(1, s0, s1)
         quantize_w(1, 0)
         for acc, (s0, s1) in zip(first, halves):
             multiply(acc, 0, 1, s0, s1)
         accs = {}
-        for acc, (s0, s1) in zip(first, halves):
-            nc.vector.tensor_scalar(y_sb[0][:, s0:s1], acc[:], biases[0][0], 0.0, ADD, MAX)
+        nc.vector.tensor_scalar(y_sb[0][:, 0:HALF], first[0][:], biases[0][0], 0.0, ADD, MAX)
+        nc.scalar.activation(y_sb[0][:, HALF:S], first[1][:], RELU, bias=biases[0][1])
 
         scales_late = keep.tile([P, (len(pieces) - early) * P], U8, name="scales_late", tag="late_scales", align_bytes=64)
         for i, piece in enumerate(pieces[early:]):
@@ -175,7 +180,7 @@ def tile_picked_sub_lin_relu_sub_e_kernel(tc, xT, w, b, gate, offs, pos1, pos2, 
 
         def layer(a, c):
             if a == 0:
-                accs[c] = psum2.tile([P, S], F32, name="acc")
+                accs[c] = psum.tile([P, S], F32, name=f"acc{c}", tag=f"acc{c}")
             weights(a, c)
             multiply(accs[c], c, a, 0, S)
             if a == PASSES - 1:
@@ -186,17 +191,15 @@ def tile_picked_sub_lin_relu_sub_e_kernel(tc, xT, w, b, gate, offs, pos1, pos2, 
 
         layer(0, 1)
         prods = {}
-        held = {0: "slot11", 1: "slot12", 2: "slot13", 3: "rest3"}
-        after = {(0, 0): (1, 1), (0, 2): (0, 2), (1, 0): (1, 2), (1, 2): (0, 3), (2, 0): (1, 3)}
+        held = {(0, 1): ("w_raw11", 3), (1, 1): ("w_raw12", 1), (1, 2): ("w_raw03", 2), (2, 1): ("w_raw13", 3)}
+        after = {(0, 0): (1, 1), (0, 2): (0, 2), (1, 0): (1, 2), (1, 1): (0, 3), (1, 3): (1, 3)}
 
         def neighbour(c, d):
-            if d == 0:
-                lead = keep.tile([P, V], F32, name=f"lead{c}")
-                prods[c, d] = lead[:]
-            elif d == 1:
-                rest = keep.tile([P, (D - 1) * V], F32, name=f"rest{c}", tag=held[c], align_bytes=64)
-                for e in range(1, D):
-                    prods[c, e] = rest[:, (e - 1) * V : e * V]
+            if (c, d) not in prods:
+                tag, count = held.get((c, d), (f"prod{c}{d}", 1))
+                group = keep.tile([P, count * V], F32, name=f"prod{c}{d}", tag=tag, align_bytes=64)
+                for e in range(count):
+                    prods[c, d + e] = group[:, e * V : (e + 1) * V]
             cuts = VH if (c, d) == (BLOCKS - 1, D - 1) else 1
             width = V // cuts
             for v0 in range(0, V, width):
@@ -209,52 +212,61 @@ def tile_picked_sub_lin_relu_sub_e_kernel(tc, xT, w, b, gate, offs, pos1, pos2, 
             if (c, d) in after:
                 layer(*after[c, d])
 
-        turned_of = {}
+        def add_turned(region, c, h, d, turns):
+            nc.tensor.matmul(region, prods[c, d][:, h * P : (h + 1) * P], ident[:], start=(d == turns[0]), stop=(d == turns[-1]), is_transpose=True)
 
-        def add_up(c, count):
-            banks = [psum.tile([P, P], F32, name=f"sum_t{h}", tag=f"first{h}" if c % 2 else f"sum_t{h}") for h in range(VH)]
-            for d in range(count):
-                for h in range(VH):
-                    nc.tensor.matmul(
-                        banks[h][:],
-                        prods[c, d][:, h * P : (h + 1) * P],
-                        ident[:],
-                        start=(d == 0),
-                        stop=(d == count - 1),
-                        is_transpose=True,
-                    )
-            if c == 0:
-                two = keep.tile([P, 2 * V], F32, name="turned01", tag="turn01", align_bytes=64)
-                turned_of[0] = two[:, 0:V]
-                turned_of[1] = two[:, V : 2 * V]
-            elif c > 1:
-                turned_of[c] = work.tile([P, V], F32, name="turned")[:]
-            turned = turned_of[c]
-            for h in range(VH):
-                nc.scalar.copy(turned[:, h * P : (h + 1) * P], banks[h][:])
+        def turn_back(turned):
             back = psum2.tile([P, V], F32, name="back")
             for h in range(VH):
                 nc.tensor.transpose(back[:, h * P : (h + 1) * P], turned[:, h * P : (h + 1) * P], ident[:])
             return back
 
+        def add_up_one_bank(c, tag):
+            bank = psum.tile([P, V], F32, name=f"sum{c}", tag=tag)
+            for h in range(VH):
+                for d in range(D):
+                    add_turned(bank[:, h * P : (h + 1) * P], c, h, d, range(D))
+            turned = keep.tile([P, V], F32, name=f"turned{c}", tag=f"turned{c}", align_bytes=64)
+            nc.scalar.copy(turned[:], bank[:])
+            return turned
+
+        def add_up_two_banks(c, turns):
+            tags = ("acc1", "sum2") if c == 2 else ("first0", "first1")
+            banks = [psum.tile([P, P], F32, name=f"sum{c}{h}", tag=tags[h]) for h in range(VH)]
+            for d in turns:
+                for h in range(VH):
+                    add_turned(banks[h][:], c, h, d, turns)
+            turned = keep.tile([P, V], F32, name=f"turned{c}", tag=f"turned{c}", align_bytes=64)
+            for h in range(VH):
+                nc.scalar.copy(turned[:, h * P : (h + 1) * P], banks[h][:])
+            return turned
+
         def finish(c):
             total = keep.tile([P, V], F32, name=f"total{c}")
-            nc.scalar.copy(total[:], add_up(c, D)[:])
+            nc.scalar.copy(total[:], turn_back(turned_of[c])[:])
             nc.sync.dma_start(ov[c], total[:])
+
+        turned_of = {}
 
         for c in range(BLOCKS):
             for d in range(D):
                 neighbour(c, d)
             if c == 2:
                 for done in range(c + 1):
-                    finish(done)
+                    turned_of[done] = add_up_one_bank(done, "acc2") if done == 1 else add_up_two_banks(done, (1, 0, 2, 3) if done == 0 else range(D))
+                    if done < c:
+                        finish(done)
         c = BLOCKS - 1
         total = keep.tile([P, V], F32, name="total_last")
-        back = add_up(c, 2)
+        turned = add_up_two_banks(c, range(2))
+        backs = [psum.tile([P, P], F32, name=f"back_last{h}", tag=("acc2", "acc3")[h]) for h in range(VH)]
+        for h in range(VH):
+            nc.tensor.transpose(backs[h][:], turned[:, h * P : (h + 1) * P], ident[:])
+        finish(c - 1)
         pair = keep.tile([P, V], F32, name="pair")
         parts = [slice(h * P, (h + 1) * P) for h in range(VH)]
         for part in parts:
             nc.vector.tensor_tensor(pair[:, part], prods[c, 2][:, part], prods[c, 3][:, part], ADD)
-        for part in parts:
-            nc.vector.tensor_tensor(total[:, part], pair[:, part], back[:, part], ADD)
+        for part, back in zip(parts, backs):
+            nc.vector.tensor_tensor(total[:, part], pair[:, part], back[:], ADD)
             nc.sync.dma_start(ov[c][:, part], total[:, part])

@@ -19,10 +19,13 @@ P = 128
 PACK = 4
 PASSES = K // (P * PACK)
 BLOCKS = N // P
+LAST = BLOCKS - 1
 HALF = S // 2
-VH = V // P
+V_HALVES = V // P
+PER_COLUMN = 16
+ALIGN = 64
 FLOPS = 2 * N * K * S
-BYTES = 4 * (K * T + K * N + N + D * V + N * V) + 2 * P * (S + D * V) // 16
+BYTES = 4 * (K * T + K * N + N + D * V + N * V) + 2 * P * (S + D * V) // PER_COLUMN
 
 
 def tile_picked_sub_lin_relu_sub_e_kernel(tc, xT, w, b, gate, offs, pos1, pos2, pos3, pos4, out):
@@ -32,75 +35,88 @@ def tile_picked_sub_lin_relu_sub_e_kernel(tc, xT, w, b, gate, offs, pos1, pos2, 
         lists = ctx.enter_context(tc.tile_pool(name="lists", bufs=1))
         keep = ctx.enter_context(tc.tile_pool(name="keep", bufs=1))
         psum = ctx.enter_context(tc.psum_pool(name="psum", bufs=1))
-        psum2 = ctx.enter_context(tc.psum_pool(name="psum2", bufs=2))
+        psum_back = ctx.enter_context(tc.psum_pool(name="psum_back", bufs=2))
 
-        xv = xT.rearrange("(a p j) t -> a j p t", a=PASSES, j=PACK)
-        wv = w.rearrange("(a p j) n -> a p j n", a=PASSES, j=PACK)
+        xv = xT.rearrange("(a p j) t -> a p j t", a=PASSES, j=PACK)
+        wv = w.rearrange("(a p j) (c m) -> a c p j m", a=PASSES, j=PACK, c=BLOCKS)
         ov = out.rearrange("(c p) v -> c p v", c=BLOCKS)
+        pieces = [(a, c) for c in range(BLOCKS) for a in range(PASSES)]
+        v_halves = [slice(h * P, (h + 1) * P) for h in range(V_HALVES)]
 
-        offs_sb = lists.tile([P, S // 16], U16, name="offs_sb")
-        pos_sb = [lists.tile([P, V // 16], U16, name=f"pos_sb{d}") for d in range(D)]
-        w_loads = [(c, c + 1) for c in range(BLOCKS)]
-        w_tiles = {(a, c0): keep.tile([P, PACK, (c1 - c0) * P], F32, name=f"w_raw{a}{c0}", tag=f"w_raw{a}{c0}", align_bytes=64) for c0, c1 in w_loads for a in range(PASSES)}
-        w_raw = {(a, c): w_tiles[a, c0][:, :, (c - c0) * P : (c - c0 + 1) * P] for c0, c1 in w_loads for c in range(c0, c1) for a in range(PASSES)}
-        x_sb = [[keep.tile([P, T], F32, name=f"x_sb{a}{j}", tag=f"x_sb{a}{j}", align_bytes=64) for j in range(PACK)] for a in range(PASSES)]
+        small_rows = keep.tile([P, V], F32, name="small_rows")
+        nc.vector.memset(small_rows[:], 0.0)
+        nc.scalar.dma_start(small_rows[0:D, :], gate[:, 0, :])
+        nc.scalar.dma_start(small_rows[D : D + BLOCKS, 0:P], b.rearrange("(c p) o -> c (p o)", c=BLOCKS))
 
-        rows = keep.tile([P, V], F32, name="rows")
-        nc.vector.memset(rows[:], 0.0)
-        nc.scalar.dma_start(rows[0:D, :], gate[:, 0, :])
-        nc.scalar.dma_start(rows[D : D + BLOCKS, 0:P], b.rearrange("(c p) o -> c (p o)", c=BLOCKS))
-        planes = [(a, j) for a in range(PASSES) for j in range(PACK)]
-        for i, (a, j) in enumerate(planes):
-            nc.sync.dma_start(x_sb[a][j][:], xv[a, j])
-            if i == 0:
+        offs_sb = lists.tile([P, S // PER_COLUMN], U16, name="offs_sb")
+        pos_sb = [lists.tile([P, V // PER_COLUMN], U16, name=f"pos_sb{d}") for d in range(D)]
+        x_plane = {}
+        for a, j0, j1 in [(0, 0, 2)] + [(i // PACK, i % PACK, i % PACK + 1) for i in range(2, PASSES * PACK)]:
+            planes = keep.tile([P, (j1 - j0) * T], F32, name=f"x_sb{a}{j0}")
+            for j in range(j0, j1):
+                x_plane[a, j] = planes[:, (j - j0) * T : (j - j0 + 1) * T]
+            nc.sync.dma_start(planes[:], xv[a][:, j0:j1, :].rearrange("p j t -> p (j t)"))
+            if (a, j0) == (0, 0):
                 nc.sync.dma_start(offs_sb[:], offs)
-        lists_behind = {(1, 0): (0,), (0, 1): (1,), (1, 1): (2, 3)}
-        for c0, c1 in w_loads:
-            for a in range(PASSES):
-                nc.sync.dma_start(w_tiles[a, c0][:], wv[a][:, :, c0 * P : c1 * P])
-                for d in lists_behind.get((a, c0), ()):
-                    nc.sync.dma_start(pos_sb[d][:], positions[d])
+        w_raw = {}
+        lists_behind = {(0, 1): range(0, 1), (1, 1): range(1, D)}
+        for a, c in pieces:
+            raw = keep.tile([P, PACK, P], F32, name=f"w_raw{a}{c}", tag=f"w_raw{a}{c}", align_bytes=ALIGN)
+            w_raw[a, c] = raw
+            nc.sync.dma_start(raw[:], wv[a, c])
+            for d in lists_behind.get((a, c), ()):
+                nc.sync.dma_start(pos_sb[d][:], positions[d])
 
         ident = keep.tile([P, P], F32, name="ident")
         make_identity(nc, ident[:])
-        cols_ps = psum2.tile([P, VH, P], F32, name="back")
-        for h in range(VH):
-            nc.tensor.transpose(cols_ps[:, h, :], rows[:, h * P : (h + 1) * P], ident[:])
-        cols = keep.tile([P, VH, D + BLOCKS], F32, name="cols")
-        nc.scalar.copy(cols[:], cols_ps[:, :, 0 : D + BLOCKS])
+        small_cols = psum_back.tile([P, V_HALVES, P], F32, name="back")
+        for h, part in enumerate(v_halves):
+            nc.tensor.transpose(small_cols[:, h, :], small_rows[:, part], ident[:])
+        gate_cols = keep.tile([P, V_HALVES, D], F32, name="gate_cols")
+        nc.scalar.copy(gate_cols[:], small_cols[:, :, 0:D])
         gate_sb = keep.tile([P, D, V], F32, name="gate_sb")
-        for pair_of_turns in range(D // 2):
-            spread = psum.tile([P, 2, V], F32, name="spread", tag=f"acc{pair_of_turns + 1}")
-            for e in range(2):
-                d = 2 * pair_of_turns + e
-                for h in range(VH):
-                    nc.tensor.transpose(spread[:, e, h * P : (h + 1) * P], cols[:, h, d : d + 1].to_broadcast([P, P]), ident[:])
-            nc.scalar.copy(gate_sb[:, 2 * pair_of_turns : 2 * pair_of_turns + 2, :], spread[:])
+        turns_a_bank = 2
+        for d0 in range(0, D, turns_a_bank):
+            spread = psum.tile([P, turns_a_bank, V], F32, name="spread", tag=f"acc{d0 // turns_a_bank + 1}")
+            for e in range(turns_a_bank):
+                for h, part in enumerate(v_halves):
+                    nc.tensor.transpose(spread[:, e, part], gate_cols[:, h, d0 + e : d0 + e + 1].to_broadcast([P, P]), ident[:])
+            nc.scalar.copy(gate_sb[:, d0 : d0 + turns_a_bank, :], spread[:])
 
-        bias_tags = {0: ("late_scales", "slot11"), 1: ("slot12", "slot3"), 2: ("turned0",)}
-        biases = {3: [cols[:, 0, D + 3 : D + 4]]}
-        for c, tags in bias_tags.items():
-            biases[c] = []
-            for tag in tags:
-                one = keep.tile([P, 1], F32, name=f"bias_{tag}", tag=tag, align_bytes=64)
-                nc.scalar.copy(one[:], cols_ps[:, 0, D + c : D + c + 1])
-                biases[c].append(one[:])
+        bias_tags = (("late_scales", "w_grp11"), ("w_grp12", "w_grp_last"), ("turned0",), ("bias_last",))
+        biases = []
+        for c, tags in enumerate(bias_tags):
+            biases.append([keep.tile([P, 1], F32, name=f"bias_{tag}", tag=tag, align_bytes=ALIGN) for tag in tags])
+            for column in biases[c]:
+                nc.scalar.copy(column[:], small_cols[:, 0, D + c : D + c + 1])
 
-        w_grp = {}
-        w_codes = {}
-        w_scales = {}
+        x_grp = [keep.tile([P, S, PACK], BF16, name=f"x_grp{a}", align_bytes=ALIGN) for a in range(PASSES)]
+        x_scales = [keep.tile([P, S], U8, name=f"x_scales{a}", align_bytes=ALIGN) for a in range(PASSES)]
+        x_codes = [keep.tile([P, S], U32, name="x_codes0", align_bytes=ALIGN)]
+        y_sb = [keep.tile([P, S], F32, name=f"y_sb{c}") for c in range(BLOCKS)]
+        w_grp, w_codes, w_scales = {}, {}, {}
+
+        def gather_x(a, j, s0, s1):
+            nc.vector.tensor_copy(x_grp[a][:, s0:s1, j], x_plane[a, j].indirect(offs_sb[:, s0 // PER_COLUMN : s1 // PER_COLUMN]))
+
+        def quantize_x(a, s0, s1):
+            nc.vector.quantize_mx(
+                out=x_codes[a][:, s0:s1].bitcast(FP8X4),
+                scales=x_scales[a][:, s0:s1],
+                in_=x_grp[a][:, s0:s1, :].rearrange("p s j -> p (s j)"),
+            )
 
         def interleave_w(a, c):
-            if c < BLOCKS - 1:
-                grouped = keep.tile([P, P, PACK], BF16, name=f"w_grp{a}{c}", tag=f"slot{a}{c}", align_bytes=64)
+            if c < LAST:
+                grouped = keep.tile([P, P, PACK], BF16, name=f"w_grp{a}{c}", tag=f"w_grp{a}{c}", align_bytes=ALIGN)
                 w_grp[a, c] = grouped[:]
             elif a == 0:
-                both = keep.tile([P, PASSES * P, PACK], BF16, name="w_grp_last", tag="slot3", align_bytes=64)
+                both = keep.tile([P, PASSES * P, PACK], BF16, name="w_grp_last", tag="w_grp_last", align_bytes=ALIGN)
                 for e in range(PASSES):
                     w_grp[e, c] = both[:, e * P : (e + 1) * P, :]
             nc.scalar.copy(
                 w_grp[a, c].rearrange("p (g i) j -> p g j i", i=2),
-                w_raw[a, c].rearrange("p j (g i) -> p g j i", i=2),
+                w_raw[a, c][:].rearrange("p j (g i) -> p g j i", i=2),
             )
 
         def quantize_w(a, c):
@@ -110,22 +126,7 @@ def tile_picked_sub_lin_relu_sub_e_kernel(tc, xT, w, b, gate, offs, pos1, pos2, 
                 in_=w_grp[a, c].rearrange("p m j -> p (m j)"),
             )
 
-        x_grp = [keep.tile([P, S, PACK], BF16, name=f"x_grp{a}", align_bytes=64) for a in range(PASSES)]
-        x_codes = [keep.tile([P, S], U32, name="x_codes0", align_bytes=64)]
-        x_scales = [keep.tile([P, S], U8, name=f"x_scales{a}", align_bytes=64) for a in range(PASSES)]
-        y_sb = [keep.tile([P, S], F32, name=f"y_sb{c}") for c in range(BLOCKS)]
-
-        def gather_x(a, j, s0, s1):
-            nc.vector.tensor_copy(x_grp[a][:, s0:s1, j], x_sb[a][j][:].indirect(offs_sb[:, s0 // 16 : s1 // 16]))
-
-        def quantize_x(a, s0, s1):
-            nc.vector.quantize_mx(
-                out=x_codes[a][:, s0:s1].bitcast(FP8X4),
-                scales=x_scales[a][:, s0:s1],
-                in_=x_grp[a][:, s0:s1, :].rearrange("p s j -> p (s j)"),
-            )
-
-        def multiply(acc, c, a, s0, s1):
+        def multiply(acc, a, c, s0, s1):
             nc.tensor.matmul_mx(
                 out=acc[:],
                 lhsT=w_codes[a, c].bitcast(FP8X4),
@@ -136,137 +137,125 @@ def tile_picked_sub_lin_relu_sub_e_kernel(tc, xT, w, b, gate, offs, pos1, pos2, 
                 stop=(a == PASSES - 1),
             )
 
-        halves = [(0, HALF), (HALF, S)]
+        s_halves = [(0, HALF), (HALF, S)]
         for j in range(PACK):
             gather_x(0, j, 0, S)
         quantize_x(0, 0, S)
         for j in range(PACK - 1):
             gather_x(1, j, 0, S)
-        for s0, s1 in halves:
+        for s0, s1 in s_halves:
             gather_x(1, PACK - 1, s0, s1)
 
-        pieces = [(a, c) for c in range(BLOCKS) for a in range(PASSES)]
-        early = 2
-        codes_all = keep.tile([P, len(pieces) * P], U32, name="codes_all", align_bytes=64)
-        scales_early = keep.tile([P, early * P], U8, name="scales_early", align_bytes=64)
+        codes_all = keep.tile([P, len(pieces) * P], U32, name="codes_all", align_bytes=ALIGN)
+        early_scales = keep.tile([P, PASSES * P], U8, name="early_scales", align_bytes=ALIGN)
         for i, piece in enumerate(pieces):
             w_codes[piece] = codes_all[:, i * P : (i + 1) * P]
-        for i, piece in enumerate(pieces[:early]):
-            w_scales[piece] = scales_early[:, i * P : (i + 1) * P]
+        for i, piece in enumerate(pieces[:PASSES]):
+            w_scales[piece] = early_scales[:, i * P : (i + 1) * P]
 
-        def weights(a, c):
-            interleave_w(a, c)
-            quantize_w(a, c)
-
-        first = [psum.tile([P, HALF], F32, name=f"first{i}") for i in range(2)]
+        runs = [(0, HALF), (HALF, HALF + P), (HALF + P, S)]
+        first = [psum.tile([P, s1 - s0], F32, name=f"first{i}", tag=("first0", "first1", "acc3")[i]) for i, (s0, s1) in enumerate(runs)]
         interleave_w(0, 0)
         interleave_w(1, 0)
         quantize_w(0, 0)
-        for acc, (s0, s1) in zip(first, halves):
+        for acc, (s0, s1) in zip(first, runs):
             multiply(acc, 0, 0, s0, s1)
-        x_codes.append(keep.tile([P, S], U32, name="x_codes1", tag="w_raw00", align_bytes=64))
-        for s0, s1 in halves:
+        x_codes.append(keep.tile([P, S], U32, name="x_codes1", tag="w_raw00", align_bytes=ALIGN))
+        for s0, s1 in s_halves:
             quantize_x(1, s0, s1)
         quantize_w(1, 0)
-        for acc, (s0, s1) in zip(first, halves):
-            multiply(acc, 0, 1, s0, s1)
+        for acc, (s0, s1) in zip(first, runs):
+            multiply(acc, 1, 0, s0, s1)
+        nc.vector.tensor_scalar(y_sb[0][:, 0:HALF], first[0][:], biases[0][0][:], 0.0, ADD, MAX)
+        for acc, (s0, s1) in zip(first[1:], runs[1:]):
+            nc.scalar.activation(y_sb[0][:, s0:s1], acc[:], RELU, bias=biases[0][1][:])
+
+        late_scales = keep.tile([P, (len(pieces) - PASSES) * P], U8, name="late_scales", tag="late_scales", align_bytes=ALIGN)
+        for i, piece in enumerate(pieces[PASSES:]):
+            w_scales[piece] = late_scales[:, i * P : (i + 1) * P]
         accs = {}
-        nc.vector.tensor_scalar(y_sb[0][:, 0:HALF], first[0][:], biases[0][0], 0.0, ADD, MAX)
-        nc.scalar.activation(y_sb[0][:, HALF:S], first[1][:], RELU, bias=biases[0][1])
 
-        scales_late = keep.tile([P, (len(pieces) - early) * P], U8, name="scales_late", tag="late_scales", align_bytes=64)
-        for i, piece in enumerate(pieces[early:]):
-            w_scales[piece] = scales_late[:, i * P : (i + 1) * P]
-
-        def layer(a, c):
+        def layer_piece(a, c):
             if a == 0:
                 accs[c] = psum.tile([P, S], F32, name=f"acc{c}", tag=f"acc{c}")
-            weights(a, c)
-            multiply(accs[c], c, a, 0, S)
+            interleave_w(a, c)
+            quantize_w(a, c)
+            multiply(accs[c], a, c, 0, S)
             if a == PASSES - 1:
                 width = S // len(biases[c])
-                for i, one in enumerate(biases[c]):
+                for i, column in enumerate(biases[c]):
                     part = slice(i * width, (i + 1) * width)
-                    nc.scalar.activation(y_sb[c][:, part], accs[c][:, part], RELU, bias=one)
+                    nc.scalar.activation(y_sb[c][:, part], accs[c][:, part], RELU, bias=column[:])
 
-        layer(0, 1)
-        prods = {}
+        piece_after = {(0, 0): (1, 1), (0, 2): (0, 2), (1, 0): (1, 2), (1, 1): (0, 3), (1, 3): (1, 3)}
         held = {(0, 1): ("w_raw11", 3), (1, 1): ("w_raw12", 1), (1, 2): ("w_raw03", 2), (2, 1): ("w_raw13", 3)}
-        after = {(0, 0): (1, 1), (0, 2): (0, 2), (1, 0): (1, 2), (1, 1): (0, 3), (1, 3): (1, 3)}
+        prods = {}
 
         def neighbour(c, d):
             if (c, d) not in prods:
                 tag, count = held.get((c, d), (f"prod{c}{d}", 1))
-                group = keep.tile([P, count * V], F32, name=f"prod{c}{d}", tag=tag, align_bytes=64)
+                group = keep.tile([P, count * V], F32, name=f"prod{c}{d}", tag=tag, align_bytes=ALIGN)
                 for e in range(count):
                     prods[c, d + e] = group[:, e * V : (e + 1) * V]
-            cuts = VH if (c, d) == (BLOCKS - 1, D - 1) else 1
-            width = V // cuts
-            for v0 in range(0, V, width):
+            for part in v_halves if (c, d) == (LAST, D - 1) else [slice(0, V)]:
                 nc.vector.tensor_tensor(
-                    prods[c, d][:, v0 : v0 + width],
-                    y_sb[c][:].indirect(pos_sb[d][:, v0 // 16 : (v0 + width) // 16]),
-                    gate_sb[:, d, v0 : v0 + width],
+                    prods[c, d][:, part],
+                    y_sb[c][:].indirect(pos_sb[d][:, part.start // PER_COLUMN : part.stop // PER_COLUMN]),
+                    gate_sb[:, d, part],
                     MULT,
                 )
-            if (c, d) in after:
-                layer(*after[c, d])
+            if (c, d) in piece_after:
+                layer_piece(*piece_after[c, d])
 
-        def add_turned(region, c, h, d, turns):
-            nc.tensor.matmul(region, prods[c, d][:, h * P : (h + 1) * P], ident[:], start=(d == turns[0]), stop=(d == turns[-1]), is_transpose=True)
+        def add_turned(region, c, part, d, turns):
+            nc.tensor.matmul(region, prods[c, d][:, part], ident[:], start=(d == turns[0]), stop=(d == turns[-1]), is_transpose=True)
 
-        def turn_back(turned):
-            back = psum2.tile([P, V], F32, name="back")
-            for h in range(VH):
-                nc.tensor.transpose(back[:, h * P : (h + 1) * P], turned[:, h * P : (h + 1) * P], ident[:])
-            return back
-
-        def add_up_one_bank(c, tag):
+        def add_up_in_one_bank(c, tag):
             bank = psum.tile([P, V], F32, name=f"sum{c}", tag=tag)
-            for h in range(VH):
+            for part in v_halves:
                 for d in range(D):
-                    add_turned(bank[:, h * P : (h + 1) * P], c, h, d, range(D))
-            turned = keep.tile([P, V], F32, name=f"turned{c}", tag=f"turned{c}", align_bytes=64)
+                    add_turned(bank[:, part], c, part, d, range(D))
+            turned = keep.tile([P, V], F32, name=f"turned{c}", tag=f"turned{c}", align_bytes=ALIGN)
             nc.scalar.copy(turned[:], bank[:])
             return turned
 
-        def add_up_two_banks(c, turns):
-            tags = ("acc1", "sum2") if c == 2 else ("first0", "first1")
-            banks = [psum.tile([P, P], F32, name=f"sum{c}{h}", tag=tags[h]) for h in range(VH)]
+        def add_up_in_two_banks(c, tags, turns):
+            banks = [psum.tile([P, P], F32, name=f"sum{c}{h}", tag=tags[h]) for h in range(V_HALVES)]
             for d in turns:
-                for h in range(VH):
-                    add_turned(banks[h][:], c, h, d, turns)
-            turned = keep.tile([P, V], F32, name=f"turned{c}", tag=f"turned{c}", align_bytes=64)
-            for h in range(VH):
-                nc.scalar.copy(turned[:, h * P : (h + 1) * P], banks[h][:])
+                for bank, part in zip(banks, v_halves):
+                    add_turned(bank[:], c, part, d, turns)
+            turned = keep.tile([P, V], F32, name=f"turned{c}", tag=f"turned{c}", align_bytes=ALIGN)
+            for bank, part in zip(banks, v_halves):
+                nc.scalar.copy(turned[:, part], bank[:])
             return turned
 
-        def finish(c):
+        def turn_back_and_store(c, turned):
             total = keep.tile([P, V], F32, name=f"total{c}")
-            nc.scalar.copy(total[:], turn_back(turned_of[c])[:])
+            back = psum_back.tile([P, V], F32, name="back")
+            for part in v_halves:
+                nc.tensor.transpose(back[:, part], turned[:, part], ident[:])
+            nc.scalar.copy(total[:], back[:])
             nc.sync.dma_start(ov[c], total[:])
 
-        turned_of = {}
-
-        for c in range(BLOCKS):
+        layer_piece(0, 1)
+        for c in range(LAST):
             for d in range(D):
                 neighbour(c, d)
-            if c == 2:
-                for done in range(c + 1):
-                    turned_of[done] = add_up_one_bank(done, "acc2") if done == 1 else add_up_two_banks(done, (1, 0, 2, 3) if done == 0 else range(D))
-                    if done < c:
-                        finish(done)
-        c = BLOCKS - 1
-        total = keep.tile([P, V], F32, name="total_last")
-        turned = add_up_two_banks(c, range(2))
-        backs = [psum.tile([P, P], F32, name=f"back_last{h}", tag=("acc2", "acc3")[h]) for h in range(VH)]
-        for h in range(VH):
-            nc.tensor.transpose(backs[h][:], turned[:, h * P : (h + 1) * P], ident[:])
-        finish(c - 1)
+        turn_back_and_store(0, add_up_in_two_banks(0, ("first0", "first1"), (1, 0, 2, 3)))
+        turn_back_and_store(1, add_up_in_one_bank(1, "acc2"))
+        turned_before_last = add_up_in_two_banks(2, ("acc1", "sum2"), range(D))
+
+        for d in range(D):
+            neighbour(LAST, d)
+        total_last = keep.tile([P, V], F32, name="total_last")
+        turned_last = add_up_in_two_banks(LAST, ("first0", "first1"), range(2))
+        backs = [psum.tile([P, P], F32, name=f"back_last{h}", tag=("acc2", "acc3")[h]) for h in range(V_HALVES)]
+        for back, part in zip(backs, v_halves):
+            nc.tensor.transpose(back[:], turned_last[:, part], ident[:])
+        turn_back_and_store(LAST - 1, turned_before_last)
         pair = keep.tile([P, V], F32, name="pair")
-        parts = [slice(h * P, (h + 1) * P) for h in range(VH)]
-        for part in parts:
-            nc.vector.tensor_tensor(pair[:, part], prods[c, 2][:, part], prods[c, 3][:, part], ADD)
-        for part, back in zip(parts, backs):
-            nc.vector.tensor_tensor(total[:, part], pair[:, part], back[:], ADD)
-            nc.sync.dma_start(ov[c][:, part], total[:, part])
+        for part in v_halves:
+            nc.vector.tensor_tensor(pair[:, part], prods[LAST, 2][:, part], prods[LAST, 3][:, part], ADD)
+        for back, part in zip(backs, v_halves):
+            nc.vector.tensor_tensor(total_last[:, part], pair[:, part], back[:], ADD)
+            nc.sync.dma_start(ov[LAST][:, part], total_last[:, part])

@@ -51,13 +51,13 @@ def tile_picked_sub_lin_relu_sub_e_kernel(tc, xT, w, b, gate, offs, pos1, pos2, 
         offs_sb = lists.tile([P, S // PER_COLUMN], U16, name="offs_sb")
         pos_sb = [lists.tile([P, V // PER_COLUMN], U16, name=f"pos_sb{d}") for d in range(D)]
         x_plane = {}
-        for a, j0, j1 in [(0, 0, 2)] + [(i // PACK, i % PACK, i % PACK + 1) for i in range(2, PASSES * PACK)]:
-            planes = keep.tile([P, (j1 - j0) * T], F32, name=f"x_sb{a}{j0}")
-            for j in range(j0, j1):
-                x_plane[a, j] = planes[:, (j - j0) * T : (j - j0 + 1) * T]
-            nc.sync.dma_start(planes[:], xv[a][:, j0:j1, :].rearrange("p j t -> p (j t)"))
-            if (a, j0) == (0, 0):
-                nc.sync.dma_start(offs_sb[:], offs)
+        for a in range(PASSES):
+            for j in range(PACK):
+                plane = keep.tile([P, T], F32, name=f"x_sb{a}{j}")
+                x_plane[a, j] = plane[:]
+                nc.sync.dma_start(plane[:], xv[a][:, j, :])
+                if (a, j) == (0, 0):
+                    nc.sync.dma_start(offs_sb[:], offs)
         w_raw = {}
         lists_behind = {(0, 1): range(0, 1), (1, 1): range(1, D)}
         for a, c in pieces:
@@ -83,7 +83,7 @@ def tile_picked_sub_lin_relu_sub_e_kernel(tc, xT, w, b, gate, offs, pos1, pos2, 
                     nc.tensor.transpose(spread[:, e, part], gate_cols[:, h, d0 + e : d0 + e + 1].to_broadcast([P, P]), ident[:])
             nc.scalar.copy(gate_sb[:, d0 : d0 + turns_a_bank, :], spread[:])
 
-        bias_tags = (("late_scales", "w_grp11"), ("w_grp12", "w_grp_last"), ("turned0",), ("bias_last",))
+        bias_tags = (("late_scales", "w_grp11", "bias_first"), ("w_grp12", "w_grp_last"), ("turned0",), ("bias_last",))
         biases = []
         for c, tags in enumerate(bias_tags):
             biases.append([keep.tile([P, 1], F32, name=f"bias_{tag}", tag=tag, align_bytes=ALIGN) for tag in tags])
@@ -106,7 +106,7 @@ def tile_picked_sub_lin_relu_sub_e_kernel(tc, xT, w, b, gate, offs, pos1, pos2, 
                 in_=x_grp[a][:, s0:s1, :].rearrange("p s j -> p (s j)"),
             )
 
-        def interleave_w(a, c):
+        def interleave_w(a, c, cuts=1):
             if c < LAST:
                 grouped = keep.tile([P, P, PACK], BF16, name=f"w_grp{a}{c}", tag=f"w_grp{a}{c}", align_bytes=ALIGN)
                 w_grp[a, c] = grouped[:]
@@ -114,17 +114,21 @@ def tile_picked_sub_lin_relu_sub_e_kernel(tc, xT, w, b, gate, offs, pos1, pos2, 
                 both = keep.tile([P, PASSES * P, PACK], BF16, name="w_grp_last", tag="w_grp_last", align_bytes=ALIGN)
                 for e in range(PASSES):
                     w_grp[e, c] = both[:, e * P : (e + 1) * P, :]
-            nc.scalar.copy(
-                w_grp[a, c].rearrange("p (g i) j -> p g j i", i=2),
-                w_raw[a, c][:].rearrange("p j (g i) -> p g j i", i=2),
-            )
+            for m0 in range(0, P, P // cuts):
+                m1 = m0 + P // cuts
+                nc.scalar.copy(
+                    w_grp[a, c][:, m0:m1, :].rearrange("p (g i) j -> p g j i", i=2),
+                    w_raw[a, c][:, :, m0:m1].rearrange("p j (g i) -> p g j i", i=2),
+                )
 
-        def quantize_w(a, c):
-            nc.vector.quantize_mx(
-                out=w_codes[a, c].bitcast(FP8X4),
-                scales=w_scales[a, c],
-                in_=w_grp[a, c].rearrange("p m j -> p (m j)"),
-            )
+        def quantize_w(a, c, cuts=1):
+            for m0 in range(0, P, P // cuts):
+                m1 = m0 + P // cuts
+                nc.vector.quantize_mx(
+                    out=w_codes[a, c][:, m0:m1].bitcast(FP8X4),
+                    scales=w_scales[a, c][:, m0:m1],
+                    in_=w_grp[a, c][:, m0:m1, :].rearrange("p m j -> p (m j)"),
+                )
 
         def multiply(acc, a, c, s0, s1):
             nc.tensor.matmul_mx(
@@ -156,19 +160,21 @@ def tile_picked_sub_lin_relu_sub_e_kernel(tc, xT, w, b, gate, offs, pos1, pos2, 
         runs = [(0, HALF), (HALF, HALF + P), (HALF + P, S)]
         first = [psum.tile([P, s1 - s0], F32, name=f"first{i}", tag=("first0", "first1", "acc3")[i]) for i, (s0, s1) in enumerate(runs)]
         interleave_w(0, 0)
-        interleave_w(1, 0)
+        interleave_w(1, 0, cuts=2)
         quantize_w(0, 0)
         for acc, (s0, s1) in zip(first, runs):
             multiply(acc, 0, 0, s0, s1)
         x_codes.append(keep.tile([P, S], U32, name="x_codes1", tag="w_raw00", align_bytes=ALIGN))
         for s0, s1 in s_halves:
             quantize_x(1, s0, s1)
-        quantize_w(1, 0)
+        quantize_w(1, 0, cuts=2)
         for acc, (s0, s1) in zip(first, runs):
             multiply(acc, 1, 0, s0, s1)
-        nc.vector.tensor_scalar(y_sb[0][:, 0:HALF], first[0][:], biases[0][0][:], 0.0, ADD, MAX)
-        for acc, (s0, s1) in zip(first[1:], runs[1:]):
-            nc.scalar.activation(y_sb[0][:, s0:s1], acc[:], RELU, bias=biases[0][1][:])
+        for i, (acc, (s0, s1), column) in enumerate(zip(first, runs, biases[0])):
+            if i == 1:
+                nc.scalar.activation(y_sb[0][:, s0:s1], acc[:], RELU, bias=column[:])
+            else:
+                nc.vector.tensor_scalar(y_sb[0][:, s0:s1], acc[:], column[:], 0.0, ADD, MAX)
 
         late_scales = keep.tile([P, (len(pieces) - PASSES) * P], U8, name="late_scales", tag="late_scales", align_bytes=ALIGN)
         for i, piece in enumerate(pieces[PASSES:]):
@@ -187,8 +193,8 @@ def tile_picked_sub_lin_relu_sub_e_kernel(tc, xT, w, b, gate, offs, pos1, pos2, 
                     part = slice(i * width, (i + 1) * width)
                     nc.scalar.activation(y_sb[c][:, part], accs[c][:, part], RELU, bias=column[:])
 
-        piece_after = {(0, 0): (1, 1), (0, 2): (0, 2), (1, 0): (1, 2), (1, 1): (0, 3), (1, 3): (1, 3)}
-        held = {(0, 1): ("w_raw11", 3), (1, 1): ("w_raw12", 1), (1, 2): ("w_raw03", 2), (2, 1): ("w_raw13", 3)}
+        piece_after = {(0, 0): (1, 1), (0, 2): (0, 2), (1, 0): (1, 2), (1, 1): (0, 3), (1, 2): (1, 3)}
+        held = {(0, 1): ("w_raw11", 3), (1, 1): ("w_raw12", 1), (1, 2): ("w_raw03", 1), (1, 3): ("w_raw13", 1), (2, 3): ("bias_last", 1)}
         prods = {}
 
         def neighbour(c, d):
@@ -197,13 +203,7 @@ def tile_picked_sub_lin_relu_sub_e_kernel(tc, xT, w, b, gate, offs, pos1, pos2, 
                 group = keep.tile([P, count * V], F32, name=f"prod{c}{d}", tag=tag, align_bytes=ALIGN)
                 for e in range(count):
                     prods[c, d + e] = group[:, e * V : (e + 1) * V]
-            for part in v_halves if (c, d) == (LAST, D - 1) else [slice(0, V)]:
-                nc.vector.tensor_tensor(
-                    prods[c, d][:, part],
-                    y_sb[c][:].indirect(pos_sb[d][:, part.start // PER_COLUMN : part.stop // PER_COLUMN]),
-                    gate_sb[:, d, part],
-                    MULT,
-                )
+            nc.vector.tensor_tensor(prods[c, d], y_sb[c][:].indirect(pos_sb[d][:]), gate_sb[:, d, :], MULT)
             if (c, d) in piece_after:
                 layer_piece(*piece_after[c, d])
 
@@ -238,24 +238,29 @@ def tile_picked_sub_lin_relu_sub_e_kernel(tc, xT, w, b, gate, offs, pos1, pos2, 
             nc.sync.dma_start(ov[c], total[:])
 
         layer_piece(0, 1)
-        for c in range(LAST):
+        for c in range(LAST - 1):
             for d in range(D):
                 neighbour(c, d)
+        for c in (LAST - 1, LAST):
+            for d in range(D - 1):
+                neighbour(c, d)
+        for c in (LAST - 1, LAST):
+            neighbour(c, D - 1)
         turn_back_and_store(0, add_up_in_two_banks(0, ("first0", "first1"), (1, 0, 2, 3)))
         turn_back_and_store(1, add_up_in_one_bank(1, "acc2"))
-        turned_before_last = add_up_in_two_banks(2, ("acc1", "sum2"), range(D))
 
-        for d in range(D):
-            neighbour(LAST, d)
-        total_last = keep.tile([P, V], F32, name="total_last")
-        turned_last = add_up_in_two_banks(LAST, ("first0", "first1"), range(2))
-        backs = [psum.tile([P, P], F32, name=f"back_last{h}", tag=("acc2", "acc3")[h]) for h in range(V_HALVES)]
-        for back, part in zip(backs, v_halves):
-            nc.tensor.transpose(back[:], turned_last[:, part], ident[:])
-        turn_back_and_store(LAST - 1, turned_before_last)
-        pair = keep.tile([P, V], F32, name="pair")
+        turned_before_last = add_up_in_two_banks(LAST - 1, ("acc1", "sum2"), range(D - 1))
+        back_before_last = psum_back.tile([P, V], F32, name="back")
         for part in v_halves:
-            nc.vector.tensor_tensor(pair[:, part], prods[LAST, 2][:, part], prods[LAST, 3][:, part], ADD)
-        for back, part in zip(backs, v_halves):
-            nc.vector.tensor_tensor(total_last[:, part], pair[:, part], back[:], ADD)
+            nc.tensor.transpose(back_before_last[:, part], turned_before_last[:, part], ident[:])
+        turned_last = add_up_in_two_banks(LAST, ("first0", "first1"), range(D - 1))
+        backs = [psum.tile([P, P], F32, name=f"back_last{h}", tag=("acc2", "acc3")[h]) for h in range(V_HALVES)]
+        for back_half, part in zip(backs, v_halves):
+            nc.tensor.transpose(back_half[:], turned_last[:, part], ident[:])
+        total_before_last = keep.tile([P, V], F32, name="total_before_last")
+        nc.vector.tensor_tensor(total_before_last[:], prods[LAST - 1, D - 1], back_before_last[:], ADD)
+        nc.sync.dma_start(ov[LAST - 1], total_before_last[:])
+        total_last = keep.tile([P, V], F32, name="total_last")
+        for back_half, part in zip(backs, v_halves):
+            nc.vector.tensor_tensor(total_last[:, part], prods[LAST, D - 1][:, part], back_half[:], ADD)
             nc.sync.dma_start(ov[LAST][:, part], total_last[:, part])

@@ -45,19 +45,19 @@ def tile_picked_sub_lin_relu_sub_e_kernel(tc, xT, w, b, gate, offs, pos1, pos2, 
 
         small_rows = keep.tile([P, V], F32, name="small_rows")
         nc.vector.memset(small_rows[:], 0.0)
-        nc.scalar.dma_start(small_rows[0:D, :], gate[:, 0, :])
-        nc.scalar.dma_start(small_rows[D : D + BLOCKS, 0:P], b.rearrange("(c p) o -> c (p o)", c=BLOCKS))
 
         offs_sb = lists.tile([P, S // PER_COLUMN], U16, name="offs_sb")
         pos_sb = [lists.tile([P, V // PER_COLUMN], U16, name=f"pos_sb{d}") for d in range(D)]
         x_plane = {}
-        for a in range(PASSES):
-            for j in range(PACK):
-                plane = keep.tile([P, T], F32, name=f"x_sb{a}{j}")
-                x_plane[a, j] = plane[:]
-                nc.sync.dma_start(plane[:], xv[a][:, j, :])
-                if (a, j) == (0, 0):
-                    nc.sync.dma_start(offs_sb[:], offs)
+        for a, j0, count in [(0, 0, 2), (0, 2, 2)] + [(1, j, 1) for j in range(PACK)]:
+            planes = keep.tile([P, count, T], F32, name=f"x_sb{a}{j0}")
+            for e in range(count):
+                x_plane[a, j0 + e] = planes[:, e, :]
+            nc.sync.dma_start(planes[:], xv[a][:, j0 : j0 + count, :])
+            if (a, j0) == (0, 0):
+                nc.sync.dma_start(offs_sb[:], offs)
+                nc.sync.dma_start(small_rows[0:D, :], gate[:, 0, :])
+                nc.sync.dma_start(small_rows[D : D + BLOCKS, 0:P], b.rearrange("(c p) o -> c (p o)", c=BLOCKS))
         w_raw = {}
         lists_behind = {(0, 1): range(0, 1), (1, 1): range(1, D)}
         for a, c in pieces:
@@ -83,7 +83,7 @@ def tile_picked_sub_lin_relu_sub_e_kernel(tc, xT, w, b, gate, offs, pos1, pos2, 
                     nc.tensor.transpose(spread[:, e, part], gate_cols[:, h, d0 + e : d0 + e + 1].to_broadcast([P, P]), ident[:])
             nc.scalar.copy(gate_sb[:, d0 : d0 + turns_a_bank, :], spread[:])
 
-        bias_tags = (("late_scales", "w_grp11", "bias_first"), ("w_grp12", "w_grp_last"), ("turned0",), ("bias_last",))
+        bias_tags = (("bias_first", "late_scales", "w_grp11"), ("w_grp12", "w_grp_last"), ("turned0",), ("bias_last",))
         biases = []
         for c, tags in enumerate(bias_tags):
             biases.append([keep.tile([P, 1], F32, name=f"bias_{tag}", tag=tag, align_bytes=ALIGN) for tag in tags])
@@ -92,7 +92,12 @@ def tile_picked_sub_lin_relu_sub_e_kernel(tc, xT, w, b, gate, offs, pos1, pos2, 
 
         x_grp = [keep.tile([P, S, PACK], BF16, name=f"x_grp{a}", align_bytes=ALIGN) for a in range(PASSES)]
         x_scales = [keep.tile([P, S], U8, name=f"x_scales{a}", align_bytes=ALIGN) for a in range(PASSES)]
-        x_codes = [keep.tile([P, S], U32, name="x_codes0", align_bytes=ALIGN)]
+        x_codes = [[(0, keep.tile([P, S], U32, name="x_codes0", align_bytes=ALIGN))], []]
+
+        def x_words(a, s0, s1):
+            first, words = [entry for entry in x_codes[a] if entry[0] <= s0][-1]
+            return words[:, s0 - first : s1 - first].bitcast(FP8X4)
+
         y_sb = [keep.tile([P, S], F32, name=f"y_sb{c}") for c in range(BLOCKS)]
         w_grp, w_codes, w_scales = {}, {}, {}
 
@@ -101,7 +106,7 @@ def tile_picked_sub_lin_relu_sub_e_kernel(tc, xT, w, b, gate, offs, pos1, pos2, 
 
         def quantize_x(a, s0, s1):
             nc.vector.quantize_mx(
-                out=x_codes[a][:, s0:s1].bitcast(FP8X4),
+                out=x_words(a, s0, s1),
                 scales=x_scales[a][:, s0:s1],
                 in_=x_grp[a][:, s0:s1, :].rearrange("p s j -> p (s j)"),
             )
@@ -130,20 +135,25 @@ def tile_picked_sub_lin_relu_sub_e_kernel(tc, xT, w, b, gate, offs, pos1, pos2, 
                     in_=w_grp[a, c][:, m0:m1, :].rearrange("p m j -> p (m j)"),
                 )
 
-        def multiply(acc, a, c, s0, s1):
+        def multiply(acc, a, c, s0, s1, closes=True):
             nc.tensor.matmul_mx(
-                out=acc[:],
+                out=acc,
                 lhsT=w_codes[a, c].bitcast(FP8X4),
                 lhsT_scale=w_scales[a, c],
-                rhs=x_codes[a][:, s0:s1].bitcast(FP8X4),
+                rhs=x_words(a, s0, s1),
                 rhs_scale=x_scales[a][:, s0:s1],
                 start=(a == 0),
-                stop=(a == PASSES - 1),
+                stop=(a == PASSES - 1 and closes),
             )
 
         s_halves = [(0, HALF), (HALF, S)]
+        picked = keep.tile([P, PACK, S], F32, name="picked")
         for j in range(PACK):
-            gather_x(0, j, 0, S)
+            nc.vector.tensor_copy(picked[:, j, :], x_plane[0, j].indirect(offs_sb[:]))
+        nc.scalar.copy(
+            x_grp[0][:].rearrange("p (g i) j -> p g j i", i=2),
+            picked[:].rearrange("p j (g i) -> p g j i", i=2),
+        )
         quantize_x(0, 0, S)
         for j in range(PACK - 1):
             gather_x(1, j, 0, S)
@@ -160,18 +170,20 @@ def tile_picked_sub_lin_relu_sub_e_kernel(tc, xT, w, b, gate, offs, pos1, pos2, 
         runs = [(0, HALF), (HALF, HALF + P), (HALF + P, S)]
         first = [psum.tile([P, s1 - s0], F32, name=f"first{i}", tag=("first0", "first1", "acc3")[i]) for i, (s0, s1) in enumerate(runs)]
         interleave_w(0, 0)
-        interleave_w(1, 0, cuts=2)
+        interleave_w(1, 0)
         quantize_w(0, 0)
         for acc, (s0, s1) in zip(first, runs):
-            multiply(acc, 0, 0, s0, s1)
-        x_codes.append(keep.tile([P, S], U32, name="x_codes1", tag="w_raw00", align_bytes=ALIGN))
-        for s0, s1 in s_halves:
+            multiply(acc[:], 0, 0, s0, s1)
+        for h, (s0, s1) in enumerate(s_halves):
+            x_codes[1].append((s0, keep.tile([P, HALF], U32, name=f"x_codes1{h}", tag=f"w_raw{h}0", align_bytes=ALIGN)))
+        quantize_x(1, *runs[0])
+        quantize_w(1, 0)
+        for s0, s1 in runs[1:]:
             quantize_x(1, s0, s1)
-        quantize_w(1, 0, cuts=2)
         for acc, (s0, s1) in zip(first, runs):
-            multiply(acc, 1, 0, s0, s1)
+            multiply(acc[:], 1, 0, s0, s1)
         for i, (acc, (s0, s1), column) in enumerate(zip(first, runs, biases[0])):
-            if i == 1:
+            if i > 0:
                 nc.scalar.activation(y_sb[0][:, s0:s1], acc[:], RELU, bias=column[:])
             else:
                 nc.vector.tensor_scalar(y_sb[0][:, s0:s1], acc[:], column[:], 0.0, ADD, MAX)
@@ -186,7 +198,11 @@ def tile_picked_sub_lin_relu_sub_e_kernel(tc, xT, w, b, gate, offs, pos1, pos2, 
                 accs[c] = psum.tile([P, S], F32, name=f"acc{c}", tag=f"acc{c}")
             interleave_w(a, c)
             quantize_w(a, c)
-            multiply(accs[c], a, c, 0, S)
+            if a == 0:
+                multiply(accs[c][:], a, c, 0, S)
+            else:
+                for s0, s1 in s_halves:
+                    multiply(accs[c][:, s0:s1], a, c, s0, s1, closes=(s1 == S))
             if a == PASSES - 1:
                 width = S // len(biases[c])
                 for i, column in enumerate(biases[c]):

@@ -147,14 +147,17 @@ def tile_picked_sub_lin_relu_sub_e_kernel(tc, xT, w, b, gate, offs, pos1, pos2, 
             )
 
         s_halves = [(0, HALF), (HALF, S)]
-        picked = keep.tile([P, PACK, S], F32, name="picked")
-        for j in range(PACK):
-            nc.vector.tensor_copy(picked[:, j, :], x_plane[0, j].indirect(offs_sb[:]))
-        nc.scalar.copy(
-            x_grp[0][:].rearrange("p (g i) j -> p g j i", i=2),
-            picked[:].rearrange("p j (g i) -> p g j i", i=2),
-        )
-        quantize_x(0, 0, S)
+        picked = [keep.tile([P, PACK, HALF], F32, name=f"picked{h}") for h in range(len(s_halves))]
+        for j0 in range(0, PACK, 2):
+            for half, (s0, s1) in zip(picked, s_halves):
+                for j in (j0, j0 + 1):
+                    nc.vector.tensor_copy(half[:, j, :], x_plane[0, j].indirect(offs_sb[:, s0 // PER_COLUMN : s1 // PER_COLUMN]))
+        for half, (s0, s1) in zip(picked, s_halves):
+            nc.scalar.copy(
+                x_grp[0][:, s0:s1, :].rearrange("p (g i) j -> p g j i", i=2),
+                half[:].rearrange("p j (g i) -> p g j i", i=2),
+            )
+            quantize_x(0, s0, s1)
         for j in range(PACK - 1):
             gather_x(1, j, 0, S)
         for s0, s1 in s_halves:
@@ -192,22 +195,23 @@ def tile_picked_sub_lin_relu_sub_e_kernel(tc, xT, w, b, gate, offs, pos1, pos2, 
         for i, piece in enumerate(pieces[PASSES:]):
             w_scales[piece] = late_scales[:, i * P : (i + 1) * P]
         accs = {}
+        acc_banks = {1: ("acc1", "sum2"), 2: ("acc2",), 3: ("acc3",)}
 
         def layer_piece(a, c):
+            banks = acc_banks[c]
+            width = S // len(banks)
             if a == 0:
-                accs[c] = psum.tile([P, S], F32, name=f"acc{c}", tag=f"acc{c}")
+                accs[c] = [psum.tile([P, width], F32, name=f"acc{c}{i}", tag=tag) for i, tag in enumerate(banks)]
             interleave_w(a, c)
             quantize_w(a, c)
             if a == 0:
-                multiply(accs[c][:], a, c, 0, S)
+                for i, acc in enumerate(accs[c]):
+                    multiply(acc[:], a, c, i * width, (i + 1) * width)
             else:
                 for s0, s1 in s_halves:
-                    multiply(accs[c][:, s0:s1], a, c, s0, s1, closes=(s1 == S))
-            if a == PASSES - 1:
-                width = S // len(biases[c])
-                for i, column in enumerate(biases[c]):
-                    part = slice(i * width, (i + 1) * width)
-                    nc.scalar.activation(y_sb[c][:, part], accs[c][:, part], RELU, bias=column[:])
+                    multiply(accs[c][s0 // width][:, s0 % width : s0 % width + HALF], a, c, s0, s1, closes=(s1 % width == 0))
+                for acc, column, s0 in zip(accs[c], biases[c], range(0, S, width)):
+                    nc.scalar.activation(y_sb[c][:, s0 : s0 + width], acc[:], RELU, bias=column[:])
 
         piece_after = {(0, 0): (1, 1), (0, 2): (0, 2), (1, 0): (1, 2), (1, 1): (0, 3), (1, 2): (1, 3)}
         held = {(0, 1): ("w_raw11", 3), (1, 1): ("w_raw12", 1), (1, 2): ("w_raw03", 1), (1, 3): ("w_raw13", 1), (2, 3): ("bias_last", 1)}

@@ -158,8 +158,11 @@ def tile_picked_sub_lin_relu_sub_e_kernel(tc, xT, w, b, gate, offs, pos1, pos2, 
                 half[:].rearrange("p j (g i) -> p g j i", i=2),
             )
             quantize_x(0, s0, s1)
-        for j in range(PACK - 1):
-            gather_x(1, j, 0, S)
+        picked_pair = keep.tile([P, 2, S], F32, name="picked_pair")
+        for j in range(2):
+            nc.vector.tensor_copy(picked_pair[:, j, :], x_plane[1, j].indirect(offs_sb[:]))
+        nc.scalar.copy(x_grp[1][:, :, 0:2], picked_pair[:].rearrange("p j s -> p s j"))
+        gather_x(1, 2, 0, S)
         for s0, s1 in s_halves:
             gather_x(1, PACK - 1, s0, s1)
 

@@ -59,7 +59,7 @@ def tile_picked_sub_lin_relu_sub_e_kernel(tc, xT, w, b, gate, offs, pos1, pos2, 
                 nc.sync.dma_start(small_rows[0:D, :], gate[:, 0, :])
                 nc.sync.dma_start(small_rows[D : D + BLOCKS, 0:P], b.rearrange("(c p) o -> c (p o)", c=BLOCKS))
         w_raw = {}
-        lists_behind = {(0, 1): range(0, 1), (1, 1): range(1, D)}
+        lists_behind = {(0, 1): range(0, 1), (1, 1): range(1, 2), (0, 2): range(2, D)}
         for a, c in pieces:
             raw = keep.tile([P, PACK, P], F32, name=f"w_raw{a}{c}", tag=f"w_raw{a}{c}", align_bytes=ALIGN)
             w_raw[a, c] = raw
@@ -98,7 +98,8 @@ def tile_picked_sub_lin_relu_sub_e_kernel(tc, xT, w, b, gate, offs, pos1, pos2, 
             first, words = [entry for entry in x_codes[a] if entry[0] <= s0][-1]
             return words[:, s0 - first : s1 - first].bitcast(FP8X4)
 
-        y_sb = [keep.tile([P, S], F32, name=f"y_sb{c}") for c in range(BLOCKS)]
+        y_tags = ("y_sb0", "w_raw02", "y_sb2", "y_sb3")
+        y_sb = [keep.tile([P, S], F32, name=f"y_sb{c}", tag=y_tags[c], align_bytes=ALIGN) for c in range(BLOCKS)]
         w_grp, w_codes, w_scales = {}, {}, {}
 
         def gather_x(a, j, s0, s1):
@@ -205,7 +206,10 @@ def tile_picked_sub_lin_relu_sub_e_kernel(tc, xT, w, b, gate, offs, pos1, pos2, 
             width = S // len(banks)
             if a == 0:
                 accs[c] = [psum.tile([P, width], F32, name=f"acc{c}{i}", tag=tag) for i, tag in enumerate(banks)]
-            interleave_w(a, c)
+            if (a, c) != (0, 2):
+                interleave_w(a, c)
+            if (a, c) == (1, 1):
+                interleave_w(0, 2)
             quantize_w(a, c)
             if a == 0:
                 for i, acc in enumerate(accs[c]):

@@ -50,7 +50,7 @@ def tile_picked_sub_lin_relu_sub_e_kernel(tc, xT, w, b, gate, offs, pos1, pos2, 
         pos_sb = [lists.tile([P, V // PER_COLUMN], U16, name=f"pos_sb{d}") for d in range(D)]
         x_plane = {}
         for a, j0, count in [(0, 0, 2), (0, 2, 2)] + [(1, j, 1) for j in range(PACK)]:
-            planes = keep.tile([P, count, T], F32, name=f"x_sb{a}{j0}")
+            planes = keep.tile([P, count, T], F32, name=f"x_sb{a}{j0}", tag=f"x_sb{a}{j0}", align_bytes=ALIGN)
             for e in range(count):
                 x_plane[a, j0 + e] = planes[:, e, :]
             nc.sync.dma_start(planes[:], xv[a][:, j0 : j0 + count, :])
@@ -69,7 +69,7 @@ def tile_picked_sub_lin_relu_sub_e_kernel(tc, xT, w, b, gate, offs, pos1, pos2, 
 
         ident = keep.tile([P, P], F32, name="ident")
         make_identity(nc, ident[:])
-        small_cols = psum_back.tile([P, V_HALVES, P], F32, name="back")
+        small_cols = psum.tile([P, V_HALVES, P], F32, name="small_cols", tag="sum2")
         for h, part in enumerate(v_halves):
             nc.tensor.transpose(small_cols[:, h, :], small_rows[:, part], ident[:])
         gate_cols = keep.tile([P, V_HALVES, D], F32, name="gate_cols")
@@ -83,11 +83,11 @@ def tile_picked_sub_lin_relu_sub_e_kernel(tc, xT, w, b, gate, offs, pos1, pos2, 
                     nc.tensor.transpose(spread[:, e, part], gate_cols[:, h, d0 + e : d0 + e + 1].to_broadcast([P, P]), ident[:])
             nc.scalar.copy(gate_sb[:, d0 : d0 + turns_a_bank, :], spread[:])
 
-        bias_tags = (("bias_first", "late_scales", "w_grp11"), ("w_grp12", "w_grp_last"), ("turned0",), ("bias_last",))
+        bias_tags = (("x_sb12", "late_scales", "w_grp11"), ("w_grp12", "w_grp_last"), ("turned0",), ("bias_last",))
         biases = []
         for c, tags in enumerate(bias_tags):
             biases.append([keep.tile([P, 1], F32, name=f"bias_{tag}", tag=tag, align_bytes=ALIGN) for tag in tags])
-            for column in biases[c]:
+            for column in biases[c][1 if c == 0 else 0 :]:
                 nc.scalar.copy(column[:], small_cols[:, 0, D + c : D + c + 1])
 
         x_grp = [keep.tile([P, S, PACK], BF16, name=f"x_grp{a}", align_bytes=ALIGN) for a in range(PASSES)]
@@ -164,6 +164,18 @@ def tile_picked_sub_lin_relu_sub_e_kernel(tc, xT, w, b, gate, offs, pos1, pos2, 
             nc.vector.tensor_copy(picked_pair[:, j, :], x_plane[1, j].indirect(offs_sb[:]))
         nc.scalar.copy(x_grp[1][:, :, 0:2], picked_pair[:].rearrange("p j s -> p s j"))
         gather_x(1, 2, 0, S)
+        nc.scalar.copy(biases[0][0][:], small_cols[:, 0, D : D + 1])
+        warm = psum.tile([P, S], F32, name="warm", tag="sum2")
+        for e in range(2):
+            nc.tensor.matmul_mx(
+                out=warm[:],
+                lhsT=x_words(0, 0, P),
+                lhsT_scale=x_scales[0][:, 0:P],
+                rhs=x_words(0, 0, S),
+                rhs_scale=x_scales[0][:],
+                start=True,
+                stop=True,
+            )
         for s0, s1 in s_halves:
             gather_x(1, PACK - 1, s0, s1)
 

@@ -232,8 +232,8 @@ def tile_picked_sub_lin_relu_sub_e_kernel(tc, xT, w, b, gate, offs, pos1, pos2, 
                 for acc, column, s0 in zip(accs[c], biases[c], range(0, S, width)):
                     nc.scalar.activation(y_sb[c][:, s0 : s0 + width], acc[:], RELU, bias=column[:])
 
-        piece_after = {(0, 0): (1, 1), (0, 2): (0, 2), (1, 0): (1, 2), (1, 1): (0, 3), (1, 2): (1, 3)}
-        held = {(0, 1): ("w_raw11", 3), (1, 1): ("w_raw12", 1), (1, 2): ("w_raw03", 1), (1, 3): ("w_raw13", 1), (2, 3): ("bias_last", 1)}
+        piece_after = {(0, 0): [(1, 1)], (0, 2): [(0, 2)], (1, 0): [(1, 2), (0, 3)], (1, 1): [(1, 3)]}
+        held = {(0, 1): ("w_raw11", 3), (1, 1): ("w_raw03", 1), (1, 2): ("w_raw13", 2), (2, 3): ("bias_last", 1)}
         prods = {}
 
         def neighbour(c, d):
@@ -243,8 +243,8 @@ def tile_picked_sub_lin_relu_sub_e_kernel(tc, xT, w, b, gate, offs, pos1, pos2, 
                 for e in range(count):
                     prods[c, d + e] = group[:, e * V : (e + 1) * V]
             nc.vector.tensor_tensor(prods[c, d], y_sb[c][:].indirect(pos_sb[d][:]), gate_sb[:, d, :], MULT)
-            if (c, d) in piece_after:
-                layer_piece(*piece_after[c, d])
+            for piece in piece_after.get((c, d), ()):
+                layer_piece(*piece)
 
         def add_turned(region, c, part, d, turns):
             nc.tensor.matmul(region, prods[c, d][:, part], ident[:], start=(d == turns[0]), stop=(d == turns[-1]), is_transpose=True)

@@ -13,17 +13,17 @@ MULT = mybir.AluOpType.mult
 ADD = mybir.AluOpType.add
 MAX = mybir.AluOpType.max
 RELU = mybir.ActivationFunctionType.Relu
+COPY = mybir.ActivationFunctionType.Copy
 
 K, T, D, S, V, N = 1024, 2048, 4, 512, 256, 512
 P = 128
 PACK = 4
 PASSES = K // (P * PACK)
 BLOCKS = N // P
-LAST = BLOCKS - 1
-HALF = S // 2
 V_HALVES = V // P
 PER_COLUMN = 16
 ALIGN = 64
+SCALAR_NODES = 128
 FLOPS = 2 * N * K * S
 BYTES = 4 * (K * T + K * N + N + D * V + N * V) + 2 * P * (S + D * V) // PER_COLUMN
 
@@ -35,271 +35,223 @@ def tile_picked_sub_lin_relu_sub_e_kernel(tc, xT, w, b, gate, offs, pos1, pos2, 
         lists = ctx.enter_context(tc.tile_pool(name="lists", bufs=1))
         keep = ctx.enter_context(tc.tile_pool(name="keep", bufs=1))
         psum = ctx.enter_context(tc.psum_pool(name="psum", bufs=1))
-        psum_back = ctx.enter_context(tc.psum_pool(name="psum_back", bufs=2))
+
+        def bank(number, shape, name):
+            return psum.tile(shape, F32, name=name, tag=f"bank{number}")
 
         xv = xT.rearrange("(a p j) t -> a p j t", a=PASSES, j=PACK)
-        wv = w.rearrange("(a p j) (c m) -> a c p j m", a=PASSES, j=PACK, c=BLOCKS)
+        wv = w.rearrange("(a p j) m -> a p j m", a=PASSES, j=PACK)
         ov = out.rearrange("(c p) v -> c p v", c=BLOCKS)
-        pieces = [(a, c) for c in range(BLOCKS) for a in range(PASSES)]
         v_halves = [slice(h * P, (h + 1) * P) for h in range(V_HALVES)]
 
         small_rows = keep.tile([P, V], F32, name="small_rows")
         nc.vector.memset(small_rows[:], 0.0)
-
         offs_sb = lists.tile([P, S // PER_COLUMN], U16, name="offs_sb")
         pos_sb = [lists.tile([P, V // PER_COLUMN], U16, name=f"pos_sb{d}") for d in range(D)]
+
+        w_first = keep.tile([P, PACK, N], F32, name="w_first", align_bytes=ALIGN)
+        nc.sync.dma_start(w_first[:], wv[0])
+        nc.sync.dma_start(offs_sb[:], offs)
+        nc.sync.dma_start(small_rows[0:D, :], gate[:, 0, :])
+        nc.sync.dma_start(small_rows[D : D + BLOCKS, 0:P], b.rearrange("(c p) o -> c (p o)", c=BLOCKS))
+        placed = ctx.enter_context(tc.tile_pool(name="placed", bufs=1))
+        raw_bytes = 4 * PACK * P
+        w_raw = [keep.tile([P, PACK, P], F32, name=f"w_raw{c}", tag=f"w_raw{c}", align_bytes=ALIGN) for c in range(BLOCKS - 1)]
+        w_raw.append(placed.tile([P, PACK, P], F32, name="w_raw_last", offset=raw_bytes // 2, align_bytes=ALIGN))
+        nc.sync.dma_start(w_raw[0][:], wv[1][:, :, 0:P])
+        x_loads = [(0, 0, 3), (1, 0, 2), (0, 3, 1), (1, 2, 1), (1, 3, 1)]
         x_plane = {}
-        for a, j0, count in [(0, 0, 2), (0, 2, 2)] + [(1, j, 1) for j in range(PACK)]:
+        for a, j0, count in x_loads:
             planes = keep.tile([P, count, T], F32, name=f"x_sb{a}{j0}", tag=f"x_sb{a}{j0}", align_bytes=ALIGN)
             for e in range(count):
                 x_plane[a, j0 + e] = planes[:, e, :]
             nc.sync.dma_start(planes[:], xv[a][:, j0 : j0 + count, :])
-            if (a, j0) == (0, 0):
-                nc.sync.dma_start(offs_sb[:], offs)
-                nc.sync.dma_start(small_rows[0:D, :], gate[:, 0, :])
-                nc.sync.dma_start(small_rows[D : D + BLOCKS, 0:P], b.rearrange("(c p) o -> c (p o)", c=BLOCKS))
-        w_raw = {}
-        lists_behind = {(0, 1): range(0, 1), (1, 1): range(1, 2), (0, 2): range(2, D)}
-        for a, c in pieces:
-            raw = keep.tile([P, PACK, P], F32, name=f"w_raw{a}{c}", tag=f"w_raw{a}{c}", align_bytes=ALIGN)
-            w_raw[a, c] = raw
-            nc.sync.dma_start(raw[:], wv[a, c])
-            for d in lists_behind.get((a, c), ()):
+        lists_behind = {1: range(0, 1), 2: range(1, 2), 3: range(2, D)}
+        for c in range(1, BLOCKS):
+            nc.sync.dma_start(w_raw[c][:], wv[1][:, :, c * P : (c + 1) * P])
+            for d in lists_behind.get(c, ()):
                 nc.sync.dma_start(pos_sb[d][:], positions[d])
 
         ident = keep.tile([P, P], F32, name="ident")
         make_identity(nc, ident[:])
-        small_cols = psum.tile([P, V_HALVES, P], F32, name="small_cols", tag="sum2")
+        small_cols = bank(0, [P, V_HALVES, P], "small_cols")
         for h, part in enumerate(v_halves):
             nc.tensor.transpose(small_cols[:, h, :], small_rows[:, part], ident[:])
-        gate_cols = keep.tile([P, V_HALVES, D], F32, name="gate_cols")
-        nc.scalar.copy(gate_cols[:], small_cols[:, :, 0:D])
+        cols = keep.tile([P, V_HALVES, D + BLOCKS], F32, name="cols")
+        nc.scalar.copy(cols[:], small_cols[:, :, 0 : D + BLOCKS])
         gate_sb = keep.tile([P, D, V], F32, name="gate_sb")
         turns_a_bank = 2
         for d0 in range(0, D, turns_a_bank):
-            spread = psum.tile([P, turns_a_bank, V], F32, name="spread", tag=f"acc{d0 // turns_a_bank + 1}")
+            spread = bank(1 + d0 // turns_a_bank, [P, turns_a_bank, V], "spread")
             for e in range(turns_a_bank):
                 for h, part in enumerate(v_halves):
-                    nc.tensor.transpose(spread[:, e, part], gate_cols[:, h, d0 + e : d0 + e + 1].to_broadcast([P, P]), ident[:])
+                    nc.tensor.transpose(spread[:, e, part], cols[:, h, d0 + e : d0 + e + 1].to_broadcast([P, P]), ident[:])
             nc.scalar.copy(gate_sb[:, d0 : d0 + turns_a_bank, :], spread[:])
 
-        bias_tags = (("x_sb12", "late_scales", "w_grp11"), ("w_grp12", "w_grp_last"), ("turned0",), ("bias_last",))
-        biases = []
-        for c, tags in enumerate(bias_tags):
-            biases.append([keep.tile([P, 1], F32, name=f"bias_{tag}", tag=tag, align_bytes=ALIGN) for tag in tags])
-            for column in biases[c][1 if c == 0 else 0 :]:
-                nc.scalar.copy(column[:], small_cols[:, 0, D + c : D + c + 1])
+        bias_last = keep.tile([P, 1], F32, name="bias_last", tag="bias_last", align_bytes=ALIGN)
+        nc.scalar.copy(bias_last[:], small_cols[:, 0, D + BLOCKS - 1 : D + BLOCKS])
 
-        x_grp = [keep.tile([P, S, PACK], BF16, name=f"x_grp{a}", align_bytes=ALIGN) for a in range(PASSES)]
+        def bias(c):
+            return bias_last[:] if c == BLOCKS - 1 else cols[:, 0, D + c : D + c + 1]
+
+        def interleave(copy, grouped, planes):
+            copy(grouped.rearrange("p (g i) j -> p g j i", i=2), planes.rearrange("p j (g i) -> p g j i", i=2))
+
+        def quantize(codes, scales, grouped):
+            nc.vector.quantize_mx(out=codes.bitcast(FP8X4), scales=scales, in_=grouped.rearrange("p s j -> p (s j)"))
+
+        w_codes = [keep.tile([P, N], U32, name=f"w_codes{a}", tag=("x_sb12", "w_codes1")[a], align_bytes=ALIGN) for a in range(PASSES)]
+        w_scales = [keep.tile([P, N], U8, name=f"w_scales{a}", align_bytes=ALIGN) for a in range(PASSES)]
+        w_first_grp = keep.tile([P, N, PACK], BF16, name="w_first_grp", align_bytes=ALIGN)
+        interleave(nc.scalar.copy, w_first_grp[:], w_first[:])
+
+        w_grp = [keep.tile([P, P, PACK], BF16, name=f"w_grp{c}", align_bytes=ALIGN) for c in range(BLOCKS)]
+
+        def quantize_w(c):
+            quantize(w_codes[1][:, c * P : (c + 1) * P], w_scales[1][:, c * P : (c + 1) * P], w_grp[c][:])
+
+        interleave(nc.scalar.copy, w_grp[0][:], w_raw[0][:])
+        quantize_w(0)
+
+        x_codes = [keep.tile([P, S], U32, name=f"x_codes{a}", align_bytes=ALIGN) for a in range(PASSES)]
         x_scales = [keep.tile([P, S], U8, name=f"x_scales{a}", align_bytes=ALIGN) for a in range(PASSES)]
-        x_codes = [[(0, keep.tile([P, S], U32, name="x_codes0", align_bytes=ALIGN))], []]
+        picked = [keep.tile([P, PACK, SCALAR_NODES], F32, name=f"picked{a}") for a in range(PASSES)]
+        grp_s = [keep.tile([P, SCALAR_NODES, PACK], BF16, name=f"grp_s{a}", align_bytes=ALIGN) for a in range(PASSES)]
+        grp_v = [keep.tile([P, S - SCALAR_NODES, PACK], BF16, name=f"grp_v{a}", align_bytes=ALIGN) for a in range(PASSES)]
+        runs = [(0, SCALAR_NODES), (SCALAR_NODES, S - P), (S - P, S)]
 
-        def x_words(a, s0, s1):
-            first, words = [entry for entry in x_codes[a] if entry[0] <= s0][-1]
-            return words[:, s0 - first : s1 - first].bitcast(FP8X4)
+        def pick(a, j):
+            cut = SCALAR_NODES // PER_COLUMN
+            nc.vector.tensor_copy(grp_v[a][:, :, j], x_plane[a, j].indirect(offs_sb[:, cut:]))
+            nc.scalar.activation(picked[a][:, j, :], x_plane[a, j].indirect(offs_sb[:, 0:cut]), COPY)
+            if j == PACK - 1:
+                interleave(nc.scalar.copy, grp_s[a][:], picked[a][:])
 
-        y_tags = ("y_sb0", "w_raw02", "y_sb2", "y_sb3")
-        y_sb = [keep.tile([P, S], F32, name=f"y_sb{c}", tag=y_tags[c], align_bytes=ALIGN) for c in range(BLOCKS)]
-        w_grp, w_codes, w_scales = {}, {}, {}
+        def quantize_x(a, run):
+            s0, s1 = runs[run]
+            grouped = grp_s[a][:] if run == 0 else grp_v[a][:, s0 - SCALAR_NODES : s1 - SCALAR_NODES, :]
+            quantize(x_codes[a][:, s0:s1], x_scales[a][:, s0:s1], grouped)
 
-        def gather_x(a, j, s0, s1):
-            nc.vector.tensor_copy(x_grp[a][:, s0:s1, j], x_plane[a, j].indirect(offs_sb[:, s0 // PER_COLUMN : s1 // PER_COLUMN]))
-
-        def quantize_x(a, s0, s1):
-            nc.vector.quantize_mx(
-                out=x_words(a, s0, s1),
-                scales=x_scales[a][:, s0:s1],
-                in_=x_grp[a][:, s0:s1, :].rearrange("p s j -> p (s j)"),
-            )
-
-        def interleave_w(a, c, cuts=1):
-            if c < LAST:
-                grouped = keep.tile([P, P, PACK], BF16, name=f"w_grp{a}{c}", tag=f"w_grp{a}{c}", align_bytes=ALIGN)
-                w_grp[a, c] = grouped[:]
-            elif a == 0:
-                both = keep.tile([P, PASSES * P, PACK], BF16, name="w_grp_last", tag="w_grp_last", align_bytes=ALIGN)
-                for e in range(PASSES):
-                    w_grp[e, c] = both[:, e * P : (e + 1) * P, :]
-            for m0 in range(0, P, P // cuts):
-                m1 = m0 + P // cuts
-                nc.scalar.copy(
-                    w_grp[a, c][:, m0:m1, :].rearrange("p (g i) j -> p g j i", i=2),
-                    w_raw[a, c][:, :, m0:m1].rearrange("p j (g i) -> p g j i", i=2),
-                )
-
-        def quantize_w(a, c, cuts=1):
-            for m0 in range(0, P, P // cuts):
-                m1 = m0 + P // cuts
-                nc.vector.quantize_mx(
-                    out=w_codes[a, c][:, m0:m1].bitcast(FP8X4),
-                    scales=w_scales[a, c][:, m0:m1],
-                    in_=w_grp[a, c][:, m0:m1, :].rearrange("p m j -> p (m j)"),
-                )
-
-        def multiply(acc, a, c, s0, s1, closes=True):
+        def multiply(acc, a, c, s0, s1):
             nc.tensor.matmul_mx(
                 out=acc,
-                lhsT=w_codes[a, c].bitcast(FP8X4),
-                lhsT_scale=w_scales[a, c],
-                rhs=x_words(a, s0, s1),
+                lhsT=w_codes[a][:, c * P : (c + 1) * P].bitcast(FP8X4),
+                lhsT_scale=w_scales[a][:, c * P : (c + 1) * P],
+                rhs=x_codes[a][:, s0:s1].bitcast(FP8X4),
                 rhs_scale=x_scales[a][:, s0:s1],
                 start=(a == 0),
-                stop=(a == PASSES - 1 and closes),
+                stop=(a == PASSES - 1),
             )
 
-        s_halves = [(0, HALF), (HALF, S)]
-        picked = [keep.tile([P, PACK, HALF], F32, name=f"picked{h}") for h in range(len(s_halves))]
-        for j0 in range(0, PACK, 2):
-            for half, (s0, s1) in zip(picked, s_halves):
-                for j in (j0, j0 + 1):
-                    nc.vector.tensor_copy(half[:, j, :], x_plane[0, j].indirect(offs_sb[:, s0 // PER_COLUMN : s1 // PER_COLUMN]))
-        for half, (s0, s1) in zip(picked, s_halves):
-            nc.scalar.copy(
-                x_grp[0][:, s0:s1, :].rearrange("p (g i) j -> p g j i", i=2),
-                half[:].rearrange("p j (g i) -> p g j i", i=2),
-            )
-            quantize_x(0, s0, s1)
-        picked_pair = keep.tile([P, 2, S], F32, name="picked_pair")
-        for j in range(2):
-            nc.vector.tensor_copy(picked_pair[:, j, :], x_plane[1, j].indirect(offs_sb[:]))
-        nc.scalar.copy(x_grp[1][:, :, 0:2], picked_pair[:].rearrange("p j s -> p s j"))
-        gather_x(1, 2, 0, S)
-        nc.scalar.copy(biases[0][0][:], small_cols[:, 0, D : D + 1])
-        warm = psum.tile([P, S], F32, name="warm", tag="sum2")
-        for e in range(2):
-            nc.tensor.matmul_mx(
-                out=warm[:],
-                lhsT=x_words(0, 0, P),
-                lhsT_scale=x_scales[0][:, 0:P],
-                rhs=x_words(0, 0, S),
-                rhs_scale=x_scales[0][:],
-                start=True,
-                stop=True,
-            )
-        for s0, s1 in s_halves:
-            gather_x(1, PACK - 1, s0, s1)
+        first = [bank(3 + i, [P, s1 - s0], f"first{i}") for i, (s0, s1) in enumerate(runs)]
+        accs = {c: bank((6, 7, 0)[c - 1], [P, S], f"acc{c}") for c in range(1, BLOCKS)}
+        for a, j0, count in x_loads:
+            for j in range(j0, j0 + count):
+                pick(a, j)
+            if (a, j0 + count) == (0, PACK):
+                for run in range(len(runs)):
+                    quantize_x(0, run)
+            if (a, j0) == (1, 2):
+                for m0 in range(0, N, N // 2):
+                    m1 = m0 + N // 2
+                    quantize(w_codes[0][:, m0:m1], w_scales[0][:, m0:m1], w_first_grp[:, m0:m1, :])
+                for acc, (s0, s1) in zip(first, runs):
+                    multiply(acc[:], 0, 0, s0, s1)
+                for c in range(1, BLOCKS):
+                    multiply(accs[c][:], 0, c, 0, S)
 
-        codes_all = keep.tile([P, len(pieces) * P], U32, name="codes_all", align_bytes=ALIGN)
-        early_scales = keep.tile([P, PASSES * P], U8, name="early_scales", align_bytes=ALIGN)
-        for i, piece in enumerate(pieces):
-            w_codes[piece] = codes_all[:, i * P : (i + 1) * P]
-        for i, piece in enumerate(pieces[:PASSES]):
-            w_scales[piece] = early_scales[:, i * P : (i + 1) * P]
+        for c in range(1, BLOCKS):
+            interleave(nc.scalar.copy, w_grp[c][:], w_raw[c][:])
+        y_sb = [keep.tile([P, S], F32, name=f"y_sb{c}", align_bytes=ALIGN) for c in (0, 2, 3)]
+        y_sb.insert(1, placed.tile([P, S], F32, name="y_sb1", offset=0, align_bytes=ALIGN))
+        closing = (1, 0, 2)
+        for run in closing:
+            quantize_x(1, run)
+        for run in closing:
+            multiply(first[run][:], 1, 0, *runs[run])
+        for run in closing:
+            s0, s1 = runs[run]
+            nc.vector.tensor_scalar(y_sb[0][:, s0:s1], first[run][:], bias(0), 0.0, ADD, MAX)
+        for c in (1, 2):
+            quantize_w(c)
+            multiply(accs[c][:], 1, c, 0, S)
+        first_prod = keep.tile([P, V], F32, name="first_prod", tag="w_raw2", align_bytes=ALIGN)
+        nc.vector.tensor_tensor(first_prod[:], y_sb[0][:].indirect(pos_sb[0][:]), gate_sb[:, 0, :], MULT)
+        quantize_w(3)
+        multiply(accs[3][:], 1, 3, 0, S)
+        for c in range(1, BLOCKS):
+            nc.scalar.activation(y_sb[c][:], accs[c][:], RELU, bias=bias(c))
 
-        runs = [(0, HALF), (HALF, HALF + P), (HALF + P, S)]
-        first = [psum.tile([P, s1 - s0], F32, name=f"first{i}", tag=("first0", "first1", "acc3")[i]) for i, (s0, s1) in enumerate(runs)]
-        interleave_w(0, 0)
-        interleave_w(1, 0)
-        quantize_w(0, 0)
-        for acc, (s0, s1) in zip(first, runs):
-            multiply(acc[:], 0, 0, s0, s1)
-        for h, (s0, s1) in enumerate(s_halves):
-            x_codes[1].append((s0, keep.tile([P, HALF], U32, name=f"x_codes1{h}", tag=f"w_raw{h}0", align_bytes=ALIGN)))
-        quantize_x(1, *runs[0])
-        quantize_w(1, 0)
-        for s0, s1 in runs[1:]:
-            quantize_x(1, s0, s1)
-        for acc, (s0, s1) in zip(first, runs):
-            multiply(acc[:], 1, 0, s0, s1)
-        for i, (acc, (s0, s1), column) in enumerate(zip(first, runs, biases[0])):
-            if i > 0:
-                nc.scalar.activation(y_sb[0][:, s0:s1], acc[:], RELU, bias=column[:])
-            else:
-                nc.vector.tensor_scalar(y_sb[0][:, s0:s1], acc[:], column[:], 0.0, ADD, MAX)
-
-        late_scales = keep.tile([P, (len(pieces) - PASSES) * P], U8, name="late_scales", tag="late_scales", align_bytes=ALIGN)
-        for i, piece in enumerate(pieces[PASSES:]):
-            w_scales[piece] = late_scales[:, i * P : (i + 1) * P]
-        accs = {}
-        acc_banks = {1: ("acc1", "sum2"), 2: ("acc2",), 3: ("acc3",)}
-
-        def layer_piece(a, c):
-            banks = acc_banks[c]
-            width = S // len(banks)
-            if a == 0:
-                accs[c] = [psum.tile([P, width], F32, name=f"acc{c}{i}", tag=tag) for i, tag in enumerate(banks)]
-            if (a, c) != (0, 2):
-                interleave_w(a, c)
-            if (a, c) == (1, 1):
-                interleave_w(0, 2)
-            quantize_w(a, c)
-            if a == 0:
-                for i, acc in enumerate(accs[c]):
-                    multiply(acc[:], a, c, i * width, (i + 1) * width)
-            else:
-                for s0, s1 in s_halves:
-                    multiply(accs[c][s0 // width][:, s0 % width : s0 % width + HALF], a, c, s0, s1, closes=(s1 % width == 0))
-                for acc, column, s0 in zip(accs[c], biases[c], range(0, S, width)):
-                    nc.scalar.activation(y_sb[c][:, s0 : s0 + width], acc[:], RELU, bias=column[:])
-
-        piece_after = {(0, 0): [(1, 1)], (0, 2): [(0, 2)], (1, 0): [(1, 2), (0, 3)], (1, 1): [(1, 3)]}
-        held = {(0, 1): ("w_raw11", 3), (1, 1): ("w_raw03", 1), (1, 2): ("w_raw13", 2), (2, 3): ("bias_last", 1)}
-        prods = {}
-
-        def neighbour(c, d):
-            if (c, d) not in prods:
-                tag, count = held.get((c, d), (f"prod{c}{d}", 1))
-                group = keep.tile([P, count * V], F32, name=f"prod{c}{d}", tag=tag, align_bytes=ALIGN)
-                for e in range(count):
-                    prods[c, d + e] = group[:, e * V : (e + 1) * V]
+        late = (2, 3)
+        held = [(0, d) for d in range(1, D)] + [(1, d) for d in range(2)] + [(c, d) for d in range(2) for c in late] + [(1, 2)]
+        held_prods = placed.tile([P, len(held), V], F32, name="held_prods", offset=raw_bytes, align_bytes=ALIGN)
+        prods = {member: held_prods[:, e, :] for e, member in enumerate(held)}
+        prods[0, 0] = first_prod[:]
+        for c, d in held:
             nc.vector.tensor_tensor(prods[c, d], y_sb[c][:].indirect(pos_sb[d][:]), gate_sb[:, d, :], MULT)
-            for piece in piece_after.get((c, d), ()):
-                layer_piece(*piece)
 
-        def add_turned(region, c, part, d, turns):
-            nc.tensor.matmul(region, prods[c, d][:, part], ident[:], start=(d == turns[0]), stop=(d == turns[-1]), is_transpose=True)
+        def turn_adding(target, sources):
+            for i, (h, source) in enumerate(sources):
+                nc.tensor.matmul(target[:, v_halves[h]], source, ident[:], start=(i == 0), stop=(i == len(sources) - 1), is_transpose=True)
 
-        def add_up_in_one_bank(c, tag):
-            bank = psum.tile([P, V], F32, name=f"sum{c}", tag=tag)
-            for part in v_halves:
-                for d in range(D):
-                    add_turned(bank[:, part], c, part, d, range(D))
-            turned = keep.tile([P, V], F32, name=f"turned{c}", tag=f"turned{c}", align_bytes=ALIGN)
-            nc.scalar.copy(turned[:], bank[:])
+        def add_up(c, number, turns):
+            total = bank(number, [P, V], f"sum{c}")
+            turn_adding(total, [(h, prods[c, d][:, part]) for d in turns for h, part in enumerate(v_halves)])
+            return total
+
+        def copy_out(source, name):
+            target = keep.tile([P, V], F32, name=name, align_bytes=ALIGN)
+            nc.scalar.copy(target[:], source[:])
+            return target
+
+        plain = {3: (1, 2, 3), 2: (2, 3)}
+        members = [(c, d) for d in plain for c in plain[d]]
+        fetched = keep.tile([P, len(members), V], F32, name="fetched", tag="bias_last", align_bytes=ALIGN)
+
+        def fetch(d, numbers):
+            turned = [bank(numbers[h], [P, len(plain[d]), P], f"plain{d}{h}") for h in range(V_HALVES)]
+            for i, c in enumerate(plain[d]):
+                values = fetched[:, members.index((c, d)), :]
+                nc.scalar.activation(values, y_sb[c][:].indirect(pos_sb[d][:]), COPY)
+                for h, part in enumerate(v_halves):
+                    nc.tensor.transpose(turned[h][:, i, :], values[:, part], ident[:])
             return turned
 
-        def add_up_in_two_banks(c, tags, turns):
-            banks = [psum.tile([P, P], F32, name=f"sum{c}{h}", tag=tags[h]) for h in range(V_HALVES)]
-            for d in turns:
-                for bank, part in zip(banks, v_halves):
-                    add_turned(bank[:], c, part, d, turns)
-            turned = keep.tile([P, V], F32, name=f"turned{c}", tag=f"turned{c}", align_bytes=ALIGN)
-            for bank, part in zip(banks, v_halves):
-                nc.scalar.copy(turned[:, part], bank[:])
-            return turned
+        scaled = {}
 
-        def turn_back_and_store(c, turned):
-            total = keep.tile([P, V], F32, name=f"total{c}")
-            back = psum_back.tile([P, V], F32, name="back")
-            for part in v_halves:
-                nc.tensor.transpose(back[:, part], turned[:, part], ident[:])
-            nc.scalar.copy(total[:], back[:])
-            nc.sync.dma_start(ov[c], total[:])
+        def weigh_turned(d, turned):
+            for h in range(V_HALVES):
+                target = keep.tile([P, len(plain[d]), P], F32, name=f"scaled{d}{h}", align_bytes=ALIGN)
+                nc.scalar.activation(target[:], turned[h][:], COPY, scale=cols[:, h, d : d + 1])
+                for i, c in enumerate(plain[d]):
+                    scaled[c, d, h] = target[:, i, :]
 
-        layer_piece(0, 1)
-        for c in range(LAST - 1):
-            for d in range(D):
-                neighbour(c, d)
-        for c in (LAST - 1, LAST):
-            for d in range(D - 1):
-                neighbour(c, d)
-        for c in (LAST - 1, LAST):
-            neighbour(c, D - 1)
-        turn_back_and_store(0, add_up_in_two_banks(0, ("first0", "first1"), (1, 0, 2, 3)))
-        turn_back_and_store(1, add_up_in_one_bank(1, "acc2"))
+        sum0 = add_up(0, 1, (1, 0, 2, 3))
+        plain3 = fetch(3, (2, 3))
+        turned0 = copy_out(sum0, "turned0")
+        back0 = bank(1, [P, V], "back0")
+        turn_adding(back0, [(h, turned0[:, part]) for h, part in enumerate(v_halves)])
+        plain2 = fetch(2, (4, 5))
+        sum1 = add_up(1, 6, range(2))
+        weigh_turned(3, plain3)
+        turned1 = copy_out(sum1, "turned1")
+        back1 = bank(6, [P, V], "back1")
+        turn_adding(back1, [(h, scaled[1, 3, h]) for h in range(V_HALVES)] + [(h, turned1[:, part]) for h, part in enumerate(v_halves)])
+        weigh_turned(2, plain2)
+        backs = {}
+        for c, number in zip(late, (7, 0)):
+            backs[c] = bank(number, [P, V], f"back{c}")
+            turn_adding(backs[c], [(h, scaled[c, d, h]) for d in plain for h in range(V_HALVES)])
+        nc.sync.dma_start(ov[0], copy_out(back0, "total0")[:])
 
-        turned_before_last = add_up_in_two_banks(LAST - 1, ("acc1", "sum2"), range(D - 1))
-        back_before_last = psum_back.tile([P, V], F32, name="back")
-        for part in v_halves:
-            nc.tensor.transpose(back_before_last[:, part], turned_before_last[:, part], ident[:])
-        turned_last = add_up_in_two_banks(LAST, ("first0", "first1"), range(D - 1))
-        backs = [psum.tile([P, P], F32, name=f"back_last{h}", tag=("acc2", "acc3")[h]) for h in range(V_HALVES)]
-        for back_half, part in zip(backs, v_halves):
-            nc.tensor.transpose(back_half[:], turned_last[:, part], ident[:])
-        total_before_last = keep.tile([P, V], F32, name="total_before_last")
-        nc.vector.tensor_tensor(total_before_last[:], prods[LAST - 1, D - 1], back_before_last[:], ADD)
-        nc.sync.dma_start(ov[LAST - 1], total_before_last[:])
-        total_last = keep.tile([P, V], F32, name="total_last")
-        for back_half, part in zip(backs, v_halves):
-            nc.vector.tensor_tensor(total_last[:, part], prods[LAST, D - 1][:, part], back_half[:], ADD)
-            nc.sync.dma_start(ov[LAST][:, part], total_last[:, part])
+        pair = {}
+        for c in late:
+            pair[c] = keep.tile([P, V], F32, name=f"pair{c}", align_bytes=ALIGN)[:]
+            nc.vector.tensor_tensor(pair[c], prods[c, 0], prods[c, 1], ADD)
+        pair[1] = prods[1, 2]
+        backs[1] = back1
+        for c in (1,) + late:
+            total = keep.tile([P, V], F32, name=f"total{c}", align_bytes=ALIGN)
+            for part in v_halves if c == late[-1] else [slice(0, V)]:
+                nc.vector.tensor_tensor(total[:, part], pair[c][:, part], backs[c][:, part], ADD)
+                nc.sync.dma_start(ov[c][:, part], total[:, part])

@@ -23,7 +23,7 @@ BLOCKS = N // P
 V_HALVES = V // P
 PER_COLUMN = 16
 ALIGN = 64
-SCALAR_NODES = 128
+AHEAD = 2
 FLOPS = 2 * N * K * S
 BYTES = 4 * (K * T + K * N + N + D * V + N * V) + 2 * P * (S + D * V) // PER_COLUMN
 
@@ -49,27 +49,35 @@ def tile_picked_sub_lin_relu_sub_e_kernel(tc, xT, w, b, gate, offs, pos1, pos2, 
         offs_sb = lists.tile([P, S // PER_COLUMN], U16, name="offs_sb")
         pos_sb = [lists.tile([P, V // PER_COLUMN], U16, name=f"pos_sb{d}") for d in range(D)]
 
-        w_first = keep.tile([P, PACK, N], F32, name="w_first", align_bytes=ALIGN)
-        nc.sync.dma_start(w_first[:], wv[0])
+        w_first = keep.tile([P, PACK, AHEAD * P], F32, name="w_first", align_bytes=ALIGN)
+        nc.sync.dma_start(w_first[:], wv[0][:, :, 0 : AHEAD * P])
         nc.sync.dma_start(offs_sb[:], offs)
         nc.sync.dma_start(small_rows[0:D, :], gate[:, 0, :])
         nc.sync.dma_start(small_rows[D : D + BLOCKS, 0:P], b.rearrange("(c p) o -> c (p o)", c=BLOCKS))
         placed = ctx.enter_context(tc.tile_pool(name="placed", bufs=1))
         raw_bytes = 4 * PACK * P
-        w_raw = [keep.tile([P, PACK, P], F32, name=f"w_raw{c}", tag=f"w_raw{c}", align_bytes=ALIGN) for c in range(BLOCKS - 1)]
-        w_raw.append(placed.tile([P, PACK, P], F32, name="w_raw_last", offset=raw_bytes // 2, align_bytes=ALIGN))
-        nc.sync.dma_start(w_raw[0][:], wv[1][:, :, 0:P])
-        x_loads = [(0, 0, 3), (1, 0, 2), (0, 3, 1), (1, 2, 1), (1, 3, 1)]
+        behind = [(1, 0), (1, 1), (0, 2), (1, 2), (0, 3), (1, 3)]
+        stretch = 2 * raw_bytes
+
+        def lower(piece):
+            return behind.index(piece) * stretch
+
+        def upper(piece):
+            return lower(piece) + raw_bytes
+
+        w_raw = {}
+        for a, c in behind:
+            w_raw[a, c] = placed.tile([P, PACK, P], F32, name=f"w_raw{a}{c}", offset=lower((a, c)) + raw_bytes // 2, align_bytes=ALIGN)
+        x_loads = [(0, 0, 2), (0, 2, 2)] + [(1, j, 1) for j in range(PACK)]
         x_plane = {}
         for a, j0, count in x_loads:
             planes = keep.tile([P, count, T], F32, name=f"x_sb{a}{j0}", tag=f"x_sb{a}{j0}", align_bytes=ALIGN)
             for e in range(count):
                 x_plane[a, j0 + e] = planes[:, e, :]
             nc.sync.dma_start(planes[:], xv[a][:, j0 : j0 + count, :])
-        lists_behind = {1: range(0, 1), 2: range(1, 2), 3: range(2, D)}
-        for c in range(1, BLOCKS):
-            nc.sync.dma_start(w_raw[c][:], wv[1][:, :, c * P : (c + 1) * P])
-            for d in lists_behind.get(c, ()):
+        for i, (a, c) in enumerate(behind):
+            nc.sync.dma_start(w_raw[a, c][:], wv[a][:, :, c * P : (c + 1) * P])
+            for d in {2: range(1), len(behind) - 1: range(1, D)}.get(i, ()):
                 nc.sync.dma_start(pos_sb[d][:], positions[d])
 
         ident = keep.tile([P, P], F32, name="ident")
@@ -88,11 +96,11 @@ def tile_picked_sub_lin_relu_sub_e_kernel(tc, xT, w, b, gate, offs, pos1, pos2, 
                     nc.tensor.transpose(spread[:, e, part], cols[:, h, d0 + e : d0 + e + 1].to_broadcast([P, P]), ident[:])
             nc.scalar.copy(gate_sb[:, d0 : d0 + turns_a_bank, :], spread[:])
 
-        bias_last = keep.tile([P, 1], F32, name="bias_last", tag="bias_last", align_bytes=ALIGN)
-        nc.scalar.copy(bias_last[:], small_cols[:, 0, D + BLOCKS - 1 : D + BLOCKS])
+        gate_last = keep.tile([P, 1], F32, name="gate_last", tag="gate_last", align_bytes=ALIGN)
+        nc.scalar.copy(gate_last[:], small_cols[:, V_HALVES - 1, D - 1 : D])
 
         def bias(c):
-            return bias_last[:] if c == BLOCKS - 1 else cols[:, 0, D + c : D + c + 1]
+            return cols[:, 0, D + c : D + c + 1]
 
         def interleave(copy, grouped, planes):
             copy(grouped.rearrange("p (g i) j -> p g j i", i=2), planes.rearrange("p j (g i) -> p g j i", i=2))
@@ -100,158 +108,191 @@ def tile_picked_sub_lin_relu_sub_e_kernel(tc, xT, w, b, gate, offs, pos1, pos2, 
         def quantize(codes, scales, grouped):
             nc.vector.quantize_mx(out=codes.bitcast(FP8X4), scales=scales, in_=grouped.rearrange("p s j -> p (s j)"))
 
-        w_codes = [keep.tile([P, N], U32, name=f"w_codes{a}", tag=("x_sb12", "w_codes1")[a], align_bytes=ALIGN) for a in range(PASSES)]
-        w_scales = [keep.tile([P, N], U8, name=f"w_scales{a}", align_bytes=ALIGN) for a in range(PASSES)]
-        w_first_grp = keep.tile([P, N, PACK], BF16, name="w_first_grp", align_bytes=ALIGN)
+        def operand(name, width, tag):
+            codes = keep.tile([P, width], U32, name=f"{name}_codes", tag=tag, align_bytes=ALIGN)
+            scales = keep.tile([P, width], U8, name=f"{name}_scales", align_bytes=ALIGN)
+            return codes, scales
+
+        w_first_grp = keep.tile([P, AHEAD * P, PACK], BF16, name="w_first_grp", align_bytes=ALIGN)
         interleave(nc.scalar.copy, w_first_grp[:], w_first[:])
+        w_head = operand("w_head", AHEAD * P, "x_sb12")
+        w_parts = {(0, c): (w_head, c * P) for c in range(AHEAD)}
+        w_rest = operand("w_rest", len(w_raw) * P, "w_rest")
+        w_grp = {}
+        for i, (a, c) in enumerate(w_raw):
+            w_parts[a, c] = (w_rest, i * P)
+            w_grp[a, c] = keep.tile([P, P, PACK], BF16, name=f"w_grp{a}{c}", align_bytes=ALIGN)
 
-        w_grp = [keep.tile([P, P, PACK], BF16, name=f"w_grp{c}", align_bytes=ALIGN) for c in range(BLOCKS)]
+        def interleave_w(piece):
+            interleave(nc.scalar.copy, w_grp[piece][:], w_raw[piece][:])
 
-        def quantize_w(c):
-            quantize(w_codes[1][:, c * P : (c + 1) * P], w_scales[1][:, c * P : (c + 1) * P], w_grp[c][:])
-
-        interleave(nc.scalar.copy, w_grp[0][:], w_raw[0][:])
-        quantize_w(0)
+        def quantize_w(piece):
+            (codes, scales), m0 = w_parts[piece]
+            quantize(codes[:, m0 : m0 + P], scales[:, m0 : m0 + P], w_grp[piece][:])
 
         x_codes = [keep.tile([P, S], U32, name=f"x_codes{a}", align_bytes=ALIGN) for a in range(PASSES)]
         x_scales = [keep.tile([P, S], U8, name=f"x_scales{a}", align_bytes=ALIGN) for a in range(PASSES)]
-        picked = [keep.tile([P, PACK, SCALAR_NODES], F32, name=f"picked{a}") for a in range(PASSES)]
-        grp_s = [keep.tile([P, SCALAR_NODES, PACK], BF16, name=f"grp_s{a}", align_bytes=ALIGN) for a in range(PASSES)]
-        grp_v = [keep.tile([P, S - SCALAR_NODES, PACK], BF16, name=f"grp_v{a}", align_bytes=ALIGN) for a in range(PASSES)]
-        runs = [(0, SCALAR_NODES), (SCALAR_NODES, S - P), (S - P, S)]
 
-        def pick(a, j):
-            cut = SCALAR_NODES // PER_COLUMN
-            nc.vector.tensor_copy(grp_v[a][:, :, j], x_plane[a, j].indirect(offs_sb[:, cut:]))
-            nc.scalar.activation(picked[a][:, j, :], x_plane[a, j].indirect(offs_sb[:, 0:cut]), COPY)
-            if j == PACK - 1:
-                interleave(nc.scalar.copy, grp_s[a][:], picked[a][:])
-
-        def quantize_x(a, run):
-            s0, s1 = runs[run]
-            grouped = grp_s[a][:] if run == 0 else grp_v[a][:, s0 - SCALAR_NODES : s1 - SCALAR_NODES, :]
-            quantize(x_codes[a][:, s0:s1], x_scales[a][:, s0:s1], grouped)
+        def entries(s0, s1):
+            return offs_sb[:, s0 // PER_COLUMN : s1 // PER_COLUMN]
 
         def multiply(acc, a, c, s0, s1):
+            (codes, scales), m0 = w_parts[a, c]
             nc.tensor.matmul_mx(
                 out=acc,
-                lhsT=w_codes[a][:, c * P : (c + 1) * P].bitcast(FP8X4),
-                lhsT_scale=w_scales[a][:, c * P : (c + 1) * P],
+                lhsT=codes[:, m0 : m0 + P].bitcast(FP8X4),
+                lhsT_scale=scales[:, m0 : m0 + P],
                 rhs=x_codes[a][:, s0:s1].bitcast(FP8X4),
                 rhs_scale=x_scales[a][:, s0:s1],
                 start=(a == 0),
                 stop=(a == PASSES - 1),
             )
 
+        half = S // 2
+        s_halves = [(0, half), (half, S)]
+        picked = [keep.tile([P, PACK, half], F32, name=f"picked{h}") for h in range(2)]
+        for j0 in range(0, PACK, 2):
+            for part, (s0, s1) in zip(picked, s_halves):
+                for j in (j0, j0 + 1):
+                    nc.vector.tensor_copy(part[:, j, :], x_plane[0, j].indirect(entries(s0, s1)))
+        grp_first = keep.tile([P, S, PACK], BF16, name="grp_first", align_bytes=ALIGN)
+        for part, (s0, s1) in zip(picked, s_halves):
+            interleave(nc.scalar.copy, grp_first[:, s0:s1, :], part[:])
+            quantize(x_codes[0][:, s0:s1], x_scales[0][:, s0:s1], grp_first[:, s0:s1, :])
+
+        runs = [(0, half), (half, half + P), (half + P, S)]
         first = [bank(3 + i, [P, s1 - s0], f"first{i}") for i, (s0, s1) in enumerate(runs)]
         accs = {c: bank((6, 7, 0)[c - 1], [P, S], f"acc{c}") for c in range(1, BLOCKS)}
-        for a, j0, count in x_loads:
-            for j in range(j0, j0 + count):
-                pick(a, j)
-            if (a, j0 + count) == (0, PACK):
-                for run in range(len(runs)):
-                    quantize_x(0, run)
-            if (a, j0) == (1, 2):
-                for m0 in range(0, N, N // 2):
-                    m1 = m0 + N // 2
-                    quantize(w_codes[0][:, m0:m1], w_scales[0][:, m0:m1], w_first_grp[:, m0:m1, :])
-                for acc, (s0, s1) in zip(first, runs):
-                    multiply(acc[:], 0, 0, s0, s1)
-                for c in range(1, BLOCKS):
-                    multiply(accs[c][:], 0, c, 0, S)
+        picked_pair = keep.tile([P, 2, S], F32, name="picked_pair")
+        grp_second = keep.tile([P, S, PACK], BF16, name="grp_second", align_bytes=ALIGN)
+        for j in range(2):
+            nc.vector.tensor_copy(picked_pair[:, j, :], x_plane[1, j].indirect(offs_sb[:]))
+        nc.scalar.copy(grp_second[:, :, 0:2], picked_pair[:].rearrange("p j s -> p s j"))
+        nc.vector.tensor_copy(grp_second[:, :, 2], x_plane[1, 2].indirect(offs_sb[:]))
+        quantize(w_head[0][:], w_head[1][:], w_first_grp[:])
+        for acc, (s0, s1) in zip(first, runs):
+            multiply(acc[:], 0, 0, s0, s1)
+        for c in range(1, AHEAD):
+            multiply(accs[c][:], 0, c, 0, S)
+        for s0, s1 in s_halves:
+            nc.vector.tensor_copy(grp_second[:, s0:s1, PACK - 1], x_plane[1, PACK - 1].indirect(entries(s0, s1)))
 
-        for c in range(1, BLOCKS):
-            interleave(nc.scalar.copy, w_grp[c][:], w_raw[c][:])
-        y_sb = [keep.tile([P, S], F32, name=f"y_sb{c}", align_bytes=ALIGN) for c in (0, 2, 3)]
-        y_sb.insert(1, placed.tile([P, S], F32, name="y_sb1", offset=0, align_bytes=ALIGN))
-        closing = (1, 0, 2)
-        for run in closing:
-            quantize_x(1, run)
-        for run in closing:
-            multiply(first[run][:], 1, 0, *runs[run])
-        for run in closing:
+        def quantize_x(run):
             s0, s1 = runs[run]
-            nc.vector.tensor_scalar(y_sb[0][:, s0:s1], first[run][:], bias(0), 0.0, ADD, MAX)
-        for c in (1, 2):
-            quantize_w(c)
-            multiply(accs[c][:], 1, c, 0, S)
-        first_prod = keep.tile([P, V], F32, name="first_prod", tag="w_raw2", align_bytes=ALIGN)
-        nc.vector.tensor_tensor(first_prod[:], y_sb[0][:].indirect(pos_sb[0][:]), gate_sb[:, 0, :], MULT)
-        quantize_w(3)
-        multiply(accs[3][:], 1, 3, 0, S)
-        for c in range(1, BLOCKS):
+            quantize(x_codes[1][:, s0:s1], x_scales[1][:, s0:s1], grp_second[:, s0:s1, :])
+
+        y_sb = [
+            keep.tile([P, S], F32, name="y_sb0", align_bytes=ALIGN),
+            placed.tile([P, S], F32, name="y_sb1", offset=lower((1, 2)), align_bytes=ALIGN),
+            placed.tile([P, S], F32, name="y_sb2", offset=lower((1, 3)), align_bytes=ALIGN),
+            keep.tile([P, S], F32, name="y_sb3", align_bytes=ALIGN),
+        ]
+
+        def relu(c):
             nc.scalar.activation(y_sb[c][:], accs[c][:], RELU, bias=bias(c))
 
+        def layer_piece(piece):
+            a, c = piece
+            interleave_w(piece)
+            quantize_w(piece)
+            multiply(accs[c][:], a, c, 0, S)
+
+        interleave_w((1, 0))
+        quantize_x(0)
+        quantize_w((1, 0))
+        quantize_x(1)
+        quantize_x(2)
+        for acc, (s0, s1) in zip(first, runs):
+            multiply(acc[:], 1, 0, s0, s1)
+        layer_piece((1, 1))
+        for acc, (s0, s1) in zip(first, runs):
+            nc.vector.tensor_scalar(y_sb[0][:, s0:s1], acc[:], bias(0), 0.0, ADD, MAX)
+
         late = (2, 3)
-        held = [(0, d) for d in range(1, D)] + [(1, d) for d in range(2)] + [(c, d) for d in range(2) for c in late] + [(1, 2)]
-        held_prods = placed.tile([P, len(held), V], F32, name="held_prods", offset=raw_bytes, align_bytes=ALIGN)
-        prods = {member: held_prods[:, e, :] for e, member in enumerate(held)}
-        prods[0, 0] = first_prod[:]
-        for c, d in held:
+        plain_turns = (2, 3)
+        prods = {}
+
+        def place_products(members, piece):
+            group = placed.tile([P, len(members), V], F32, name=f"prods{piece[0]}{piece[1]}", offset=upper(piece), align_bytes=ALIGN)
+            for e, member in enumerate(members):
+                prods[member] = group[:, e, :]
+
+        def weighed(c, d):
             nc.vector.tensor_tensor(prods[c, d], y_sb[c][:].indirect(pos_sb[d][:]), gate_sb[:, d, :], MULT)
 
         def turn_adding(target, sources):
-            for i, (h, source) in enumerate(sources):
-                nc.tensor.matmul(target[:, v_halves[h]], source, ident[:], start=(i == 0), stop=(i == len(sources) - 1), is_transpose=True)
+            for i, (e, source) in enumerate(sources):
+                nc.tensor.matmul(target[:, e * P : (e + 1) * P], source, ident[:], start=(i == 0), stop=(i == len(sources) - 1), is_transpose=True)
 
-        def add_up(c, number, turns):
-            total = bank(number, [P, V], f"sum{c}")
-            turn_adding(total, [(h, prods[c, d][:, part]) for d in turns for h, part in enumerate(v_halves)])
-            return total
+        def add_turn(total, c, d, turns):
+            for h, part in enumerate(v_halves):
+                opens, closes = (d, h) == (turns[0], 0), (d, h) == (turns[-1], V_HALVES - 1)
+                nc.tensor.matmul(total[:, part], prods[c, d][:, part], ident[:], start=opens, stop=closes, is_transpose=True)
 
-        def copy_out(source, name):
-            target = keep.tile([P, V], F32, name=name, align_bytes=ALIGN)
+        def copy_out(source, name, tag):
+            target = keep.tile([P, V], F32, name=name, tag=tag, align_bytes=ALIGN)
             nc.scalar.copy(target[:], source[:])
             return target
 
-        plain = {3: (1, 2, 3), 2: (2, 3)}
-        members = [(c, d) for d in plain for c in plain[d]]
-        fetched = keep.tile([P, len(members), V], F32, name="fetched", tag="bias_last", align_bytes=ALIGN)
+        def turn_back(c, turned, number):
+            back = bank(number, [P, V], f"back{c}")
+            turn_adding(back, [(h, turned[:, part]) for h, part in enumerate(v_halves)])
+            return back
 
-        def fetch(d, numbers):
-            turned = [bank(numbers[h], [P, len(plain[d]), P], f"plain{d}{h}") for h in range(V_HALVES)]
-            for i, c in enumerate(plain[d]):
-                values = fetched[:, members.index((c, d)), :]
-                nc.scalar.activation(values, y_sb[c][:].indirect(pos_sb[d][:]), COPY)
-                for h, part in enumerate(v_halves):
-                    nc.tensor.transpose(turned[h][:, i, :], values[:, part], ident[:])
-            return turned
+        plain = {d: bank(d, [P, V_HALVES, len(late), P], f"plain{d}") for d in plain_turns}
 
-        scaled = {}
+        def fetch(c, d):
+            values = keep.tile([P, V], F32, name=f"fetched{c}{d}", align_bytes=ALIGN)
+            nc.scalar.activation(values[:], y_sb[c][:].indirect(pos_sb[d][:]), COPY)
+            for h, part in enumerate(v_halves):
+                nc.tensor.transpose(plain[d][:, h, late.index(c), :], values[:, part], ident[:])
 
-        def weigh_turned(d, turned):
-            for h in range(V_HALVES):
-                target = keep.tile([P, len(plain[d]), P], F32, name=f"scaled{d}{h}", align_bytes=ALIGN)
-                nc.scalar.activation(target[:], turned[h][:], COPY, scale=cols[:, h, d : d + 1])
-                for i, c in enumerate(plain[d]):
-                    scaled[c, d, h] = target[:, i, :]
+        rest = [(0, 2), (0, 3)] + [(1, d) for d in range(D)] + [(c, d) for d in range(2) for c in late]
+        for d, piece in enumerate(behind[2:]):
+            layer_piece(piece)
+            if piece[0] == 1:
+                relu(piece[1] - 1)
+            if piece != (0, 3):
+                place_products([(0, d)] if d < 2 else rest, piece)
+                weighed(0, min(d, 2))
+        weighed(0, 3)
+        sum0 = bank(1, [P, V], "sum0")
+        turns0 = (2, 0, 1, 3)
+        for d in turns0:
+            add_turn(sum0, 0, d, turns0)
+        fetch(2, 2)
+        relu(3)
+        for c, d in rest[2:]:
+            weighed(c, d)
+        sum1 = bank(6, [P, V], "sum1")
+        add_turn(sum1, 1, 0, range(D))
+        fetch(2, 3)
+        add_turn(sum1, 1, 1, range(D))
+        fetch(3, 2)
+        back0 = turn_back(0, copy_out(sum0, "turned0", "turned0"), 4)
+        add_turn(sum1, 1, 2, range(D))
+        fetch(3, 3)
+        add_turn(sum1, 1, 3, range(D))
+        backs = []
+        for h in range(V_HALVES):
+            if h == 1:
+                back1 = turn_back(1, copy_out(sum1, "turned1", "turned1"), 5)
+            scaled = keep.tile([P, len(plain_turns), len(late) * P], F32, name=f"scaled{h}", align_bytes=ALIGN)
+            for e, d in enumerate(plain_turns):
+                column = gate_last[:] if (d, h) == (D - 1, V_HALVES - 1) else cols[:, h, d : d + 1]
+                nc.scalar.activation(scaled[:, e, :], plain[d][:, h, :, :].rearrange("p c m -> p (c m)"), COPY, scale=column)
+            backs.append(bank((7, 0)[h], [P, len(late) * P], f"back_late{h}"))
+            turn_adding(backs[h], [(i, scaled[:, e, i * P : (i + 1) * P]) for e in range(len(plain_turns)) for i in range(len(late))])
+        totals = keep.tile([P, 2, V], F32, name="totals", tag="gate_last", align_bytes=ALIGN)
+        for c, back in enumerate((back0, back1)):
+            nc.scalar.copy(totals[:, c, :], back[:])
+            nc.sync.dma_start(ov[c], totals[:, c, :])
 
-        sum0 = add_up(0, 1, (1, 0, 2, 3))
-        plain3 = fetch(3, (2, 3))
-        turned0 = copy_out(sum0, "turned0")
-        back0 = bank(1, [P, V], "back0")
-        turn_adding(back0, [(h, turned0[:, part]) for h, part in enumerate(v_halves)])
-        plain2 = fetch(2, (4, 5))
-        sum1 = add_up(1, 6, range(2))
-        weigh_turned(3, plain3)
-        turned1 = copy_out(sum1, "turned1")
-        back1 = bank(6, [P, V], "back1")
-        turn_adding(back1, [(h, scaled[1, 3, h]) for h in range(V_HALVES)] + [(h, turned1[:, part]) for h, part in enumerate(v_halves)])
-        weigh_turned(2, plain2)
-        backs = {}
-        for c, number in zip(late, (7, 0)):
-            backs[c] = bank(number, [P, V], f"back{c}")
-            turn_adding(backs[c], [(h, scaled[c, d, h]) for d in plain for h in range(V_HALVES)])
-        nc.sync.dma_start(ov[0], copy_out(back0, "total0")[:])
-
-        pair = {}
-        for c in late:
-            pair[c] = keep.tile([P, V], F32, name=f"pair{c}", align_bytes=ALIGN)[:]
-            nc.vector.tensor_tensor(pair[c], prods[c, 0], prods[c, 1], ADD)
-        pair[1] = prods[1, 2]
-        backs[1] = back1
-        for c in (1,) + late:
-            total = keep.tile([P, V], F32, name=f"total{c}", align_bytes=ALIGN)
-            for part in v_halves if c == late[-1] else [slice(0, V)]:
-                nc.vector.tensor_tensor(total[:, part], pair[c][:, part], backs[c][:, part], ADD)
-                nc.sync.dma_start(ov[c][:, part], total[:, part])
+        pair = keep.tile([P, len(late), V], F32, name="pair", align_bytes=ALIGN)
+        for i, c in enumerate(late):
+            nc.vector.tensor_tensor(pair[:, i, :], prods[c, 0], prods[c, 1], ADD)
+        late_out = out.rearrange("(c p) v -> p c v", c=BLOCKS)[:, late[0] : late[-1] + 1, :]
+        for h, part in enumerate(v_halves):
+            total = keep.tile([P, len(late), P], F32, name=f"total_late{h}", align_bytes=ALIGN)
+            nc.vector.tensor_tensor(total[:], pair[:, :, part], backs[h][:].rearrange("p (c m) -> p c m", c=len(late)), ADD)
+            nc.sync.dma_start(late_out[:, :, part], total[:])

@@ -56,18 +56,22 @@ def tile_picked_sub_lin_relu_sub_e_kernel(tc, xT, w, b, gate, offs, pos1, pos2, 
         nc.sync.dma_start(small_rows[D : D + BLOCKS, 0:P], b.rearrange("(c p) o -> c (p o)", c=BLOCKS))
         placed = ctx.enter_context(tc.tile_pool(name="placed", bufs=1))
         raw_bytes = 4 * PACK * P
-        behind = [(1, 0), (1, 1), (0, 2), (1, 2), (0, 3), (1, 3)]
-        stretch = 2 * raw_bytes
+        behind = [(1, 0, 1), (1, 1, 1), (0, 2, 2), (1, 2, 2)]
+        stretch = 4 * raw_bytes
 
-        def lower(piece):
-            return behind.index(piece) * stretch
+        def lower(load):
+            return behind.index(load) * stretch
 
-        def upper(piece):
-            return lower(piece) + raw_bytes
+        def upper(load):
+            return lower(load) + raw_bytes
 
+        w_loaded = {}
         w_raw = {}
-        for a, c in behind:
-            w_raw[a, c] = placed.tile([P, PACK, P], F32, name=f"w_raw{a}{c}", offset=lower((a, c)) + raw_bytes // 2, align_bytes=ALIGN)
+        for load in behind:
+            a, c0, count = load
+            w_loaded[load] = placed.tile([P, PACK, count * P], F32, name=f"w_raw{a}{c0}", offset=lower(load) + raw_bytes // 2, align_bytes=ALIGN)
+            for e in range(count):
+                w_raw[a, c0 + e] = w_loaded[load][:, :, e * P : (e + 1) * P]
         x_loads = [(0, 0, 2), (0, 2, 2)] + [(1, j, 1) for j in range(PACK)]
         x_plane = {}
         for a, j0, count in x_loads:
@@ -75,8 +79,8 @@ def tile_picked_sub_lin_relu_sub_e_kernel(tc, xT, w, b, gate, offs, pos1, pos2, 
             for e in range(count):
                 x_plane[a, j0 + e] = planes[:, e, :]
             nc.sync.dma_start(planes[:], xv[a][:, j0 : j0 + count, :])
-        for i, (a, c) in enumerate(behind):
-            nc.sync.dma_start(w_raw[a, c][:], wv[a][:, :, c * P : (c + 1) * P])
+        for i, (a, c0, count) in enumerate(behind):
+            nc.sync.dma_start(w_loaded[a, c0, count][:], wv[a][:, :, c0 * P : (c0 + count) * P])
             for d in {2: range(1), len(behind) - 1: range(1, D)}.get(i, ()):
                 nc.sync.dma_start(pos_sb[d][:], positions[d])
 
@@ -124,7 +128,7 @@ def tile_picked_sub_lin_relu_sub_e_kernel(tc, xT, w, b, gate, offs, pos1, pos2, 
             w_grp[a, c] = keep.tile([P, P, PACK], BF16, name=f"w_grp{a}{c}", align_bytes=ALIGN)
 
         def interleave_w(piece):
-            interleave(nc.scalar.copy, w_grp[piece][:], w_raw[piece][:])
+            interleave(nc.scalar.copy, w_grp[piece][:], w_raw[piece])
 
         def quantize_w(piece):
             (codes, scales), m0 = w_parts[piece]
@@ -183,8 +187,8 @@ def tile_picked_sub_lin_relu_sub_e_kernel(tc, xT, w, b, gate, offs, pos1, pos2, 
 
         y_sb = [
             keep.tile([P, S], F32, name="y_sb0", align_bytes=ALIGN),
-            placed.tile([P, S], F32, name="y_sb1", offset=lower((1, 2)), align_bytes=ALIGN),
-            placed.tile([P, S], F32, name="y_sb2", offset=lower((1, 3)), align_bytes=ALIGN),
+            placed.tile([P, S], F32, name="y_sb1", offset=lower(behind[-1]), align_bytes=ALIGN),
+            keep.tile([P, S], F32, name="y_sb2", align_bytes=ALIGN),
             keep.tile([P, S], F32, name="y_sb3", align_bytes=ALIGN),
         ]
 
@@ -213,7 +217,7 @@ def tile_picked_sub_lin_relu_sub_e_kernel(tc, xT, w, b, gate, offs, pos1, pos2, 
         prods = {}
 
         def place_products(members, piece):
-            group = placed.tile([P, len(members), V], F32, name=f"prods{piece[0]}{piece[1]}", offset=upper(piece), align_bytes=ALIGN)
+            group = placed.tile([P, len(members), V], F32, name=f"prods{len(members)}", offset=upper(piece), align_bytes=ALIGN)
             for e, member in enumerate(members):
                 prods[member] = group[:, e, :]
 
@@ -247,23 +251,23 @@ def tile_picked_sub_lin_relu_sub_e_kernel(tc, xT, w, b, gate, offs, pos1, pos2, 
             for h, part in enumerate(v_halves):
                 nc.tensor.transpose(plain[d][:, h, late.index(c), :], values[:, part], ident[:])
 
-        rest = [(0, 2), (0, 3)] + [(1, d) for d in range(D)] + [(c, d) for d in range(2) for c in late]
-        for d, piece in enumerate(behind[2:]):
-            layer_piece(piece)
-            if piece[0] == 1:
-                relu(piece[1] - 1)
-            if piece != (0, 3):
-                place_products([(0, d)] if d < 2 else rest, piece)
-                weighed(0, min(d, 2))
-        weighed(0, 3)
+        rest = [(0, d) for d in range(1, D)] + [(1, d) for d in range(D)] + [(c, d) for d in range(2) for c in late]
+        for c in late:
+            layer_piece((0, c))
+        place_products([(0, 0)], behind[-2])
+        weighed(0, 0)
+        for c in late:
+            layer_piece((1, c))
+        for c in range(1, BLOCKS):
+            relu(c)
+        place_products(rest, behind[-1])
+        for c, d in rest:
+            weighed(c, d)
         sum0 = bank(1, [P, V], "sum0")
-        turns0 = (2, 0, 1, 3)
+        turns0 = (1, 0, 2, 3)
         for d in turns0:
             add_turn(sum0, 0, d, turns0)
         fetch(2, 2)
-        relu(3)
-        for c, d in rest[2:]:
-            weighed(c, d)
         sum1 = bank(6, [P, V], "sum1")
         add_turn(sum1, 1, 0, range(D))
         fetch(2, 3)

@@ -56,7 +56,7 @@ def tile_picked_sub_lin_relu_sub_e_kernel(tc, xT, w, b, gate, offs, pos1, pos2, 
         nc.sync.dma_start(small_rows[D : D + BLOCKS, 0:P], b.rearrange("(c p) o -> c (p o)", c=BLOCKS))
         placed = ctx.enter_context(tc.tile_pool(name="placed", bufs=1))
         raw_bytes = 4 * PACK * P
-        behind = [(1, 0, 1), (1, 1, 1), (0, 2, 2), (1, 2, 2)]
+        behind = [(1, 0, 1), (1, 1, 1), (0, 2, 2), (1, 2, 1), (1, 3, 1)]
         stretch = 4 * raw_bytes
 
         def lower(load):
@@ -75,10 +75,10 @@ def tile_picked_sub_lin_relu_sub_e_kernel(tc, xT, w, b, gate, offs, pos1, pos2, 
         x_loads = [(0, 0, 2), (0, 2, 2)] + [(1, j, 1) for j in range(PACK)]
         x_plane = {}
         for a, j0, count in x_loads:
-            planes = keep.tile([P, count, T], F32, name=f"x_sb{a}{j0}", tag=f"x_sb{a}{j0}", align_bytes=ALIGN)
+            planes = keep.tile([P, count * T], F32, name=f"x_sb{a}{j0}", tag=f"x_sb{a}{j0}", align_bytes=ALIGN)
             for e in range(count):
-                x_plane[a, j0 + e] = planes[:, e, :]
-            nc.sync.dma_start(planes[:], xv[a][:, j0 : j0 + count, :])
+                x_plane[a, j0 + e] = planes[:, e * T : (e + 1) * T]
+            nc.sync.dma_start(planes[:], xv[a][:, j0 : j0 + count, :].rearrange("p j t -> p (j t)"))
         for i, (a, c0, count) in enumerate(behind):
             nc.sync.dma_start(w_loaded[a, c0, count][:], wv[a][:, :, c0 * P : (c0 + count) * P])
             for d in {2: range(1), len(behind) - 1: range(1, D)}.get(i, ()):
@@ -134,7 +134,7 @@ def tile_picked_sub_lin_relu_sub_e_kernel(tc, xT, w, b, gate, offs, pos1, pos2, 
             (codes, scales), m0 = w_parts[piece]
             quantize(codes[:, m0 : m0 + P], scales[:, m0 : m0 + P], w_grp[piece][:])
 
-        x_codes = [keep.tile([P, S], U32, name=f"x_codes{a}", align_bytes=ALIGN) for a in range(PASSES)]
+        x_codes = [keep.tile([P, S], U32, name=f"x_codes{a}", tag=("x_codes0", "x_sb13")[a], align_bytes=ALIGN) for a in range(PASSES)]
         x_scales = [keep.tile([P, S], U8, name=f"x_scales{a}", align_bytes=ALIGN) for a in range(PASSES)]
 
         def entries(s0, s1):
@@ -164,7 +164,7 @@ def tile_picked_sub_lin_relu_sub_e_kernel(tc, xT, w, b, gate, offs, pos1, pos2, 
             interleave(nc.scalar.copy, grp_first[:, s0:s1, :], part[:])
             quantize(x_codes[0][:, s0:s1], x_scales[0][:, s0:s1], grp_first[:, s0:s1, :])
 
-        runs = [(0, half), (half, half + P), (half + P, S)]
+        runs = s_halves
         first = [bank(3 + i, [P, s1 - s0], f"first{i}") for i, (s0, s1) in enumerate(runs)]
         accs = {c: bank((6, 7, 0)[c - 1], [P, S], f"acc{c}") for c in range(1, BLOCKS)}
         picked_pair = keep.tile([P, 2, S], F32, name="picked_pair")
@@ -178,8 +178,10 @@ def tile_picked_sub_lin_relu_sub_e_kernel(tc, xT, w, b, gate, offs, pos1, pos2, 
             multiply(acc[:], 0, 0, s0, s1)
         for c in range(1, AHEAD):
             multiply(accs[c][:], 0, c, 0, S)
-        for s0, s1 in s_halves:
-            nc.vector.tensor_copy(grp_second[:, s0:s1, PACK - 1], x_plane[1, PACK - 1].indirect(entries(s0, s1)))
+        last_half = keep.tile([P, half], BF16, name="last_half", align_bytes=ALIGN)
+        nc.scalar.activation(last_half[:], x_plane[1, PACK - 1].indirect(entries(half, S)), COPY)
+        nc.vector.tensor_copy(grp_second[:, 0:half, PACK - 1], x_plane[1, PACK - 1].indirect(entries(0, half)))
+        nc.vector.tensor_copy(grp_second[:, half:S, PACK - 1], last_half[:])
 
         def quantize_x(run):
             s0, s1 = runs[run]
@@ -205,7 +207,6 @@ def tile_picked_sub_lin_relu_sub_e_kernel(tc, xT, w, b, gate, offs, pos1, pos2, 
         quantize_x(0)
         quantize_w((1, 0))
         quantize_x(1)
-        quantize_x(2)
         for acc, (s0, s1) in zip(first, runs):
             multiply(acc[:], 1, 0, s0, s1)
         layer_piece((1, 1))
@@ -217,7 +218,7 @@ def tile_picked_sub_lin_relu_sub_e_kernel(tc, xT, w, b, gate, offs, pos1, pos2, 
         prods = {}
 
         def place_products(members, piece):
-            group = placed.tile([P, len(members), V], F32, name=f"prods{len(members)}", offset=upper(piece), align_bytes=ALIGN)
+            group = placed.tile([P, len(members), V], F32, name=f"prods{piece[0]}{piece[1]}", offset=upper(piece), align_bytes=ALIGN)
             for e, member in enumerate(members):
                 prods[member] = group[:, e, :]
 
@@ -251,12 +252,12 @@ def tile_picked_sub_lin_relu_sub_e_kernel(tc, xT, w, b, gate, offs, pos1, pos2, 
             for h, part in enumerate(v_halves):
                 nc.tensor.transpose(plain[d][:, h, late.index(c), :], values[:, part], ident[:])
 
-        rest = [(0, d) for d in range(1, D)] + [(1, d) for d in range(D)] + [(c, d) for d in range(2) for c in late]
+        rest = [(0, d) for d in range(2, D)] + [(1, d) for d in range(D)] + [(c, d) for d in range(2) for c in late]
         for c in late:
             layer_piece((0, c))
-        place_products([(0, 0)], behind[-2])
-        weighed(0, 0)
-        for c in late:
+        for d, c in enumerate(late):
+            place_products([(0, d)], behind[d - 3])
+            weighed(0, d)
             layer_piece((1, c))
         for c in range(1, BLOCKS):
             relu(c)
@@ -264,7 +265,7 @@ def tile_picked_sub_lin_relu_sub_e_kernel(tc, xT, w, b, gate, offs, pos1, pos2, 
         for c, d in rest:
             weighed(c, d)
         sum0 = bank(1, [P, V], "sum0")
-        turns0 = (1, 0, 2, 3)
+        turns0 = (2, 0, 1, 3)
         for d in turns0:
             add_turn(sum0, 0, d, turns0)
         fetch(2, 2)

@@ -56,7 +56,7 @@ def tile_picked_sub_lin_relu_sub_e_kernel(tc, xT, w, b, gate, offs, pos1, pos2, 
         nc.sync.dma_start(small_rows[D : D + BLOCKS, 0:P], b.rearrange("(c p) o -> c (p o)", c=BLOCKS))
         placed = ctx.enter_context(tc.tile_pool(name="placed", bufs=1))
         raw_bytes = 4 * PACK * P
-        behind = [(1, 0, 1), (1, 1, 1), (0, 2, 2), (1, 2, 1), (1, 3, 1)]
+        behind = [(1, 0, 1), (1, 1, 1), (0, 2, 1), (0, 3, 1), (1, 2, 1), (1, 3, 1)]
         stretch = 4 * raw_bytes
 
         def lower(load):
@@ -134,26 +134,37 @@ def tile_picked_sub_lin_relu_sub_e_kernel(tc, xT, w, b, gate, offs, pos1, pos2, 
             (codes, scales), m0 = w_parts[piece]
             quantize(codes[:, m0 : m0 + P], scales[:, m0 : m0 + P], w_grp[piece][:])
 
-        x_codes = [keep.tile([P, S], U32, name=f"x_codes{a}", tag=("x_codes0", "x_sb13")[a], align_bytes=ALIGN) for a in range(PASSES)]
-        x_scales = [keep.tile([P, S], U8, name=f"x_scales{a}", align_bytes=ALIGN) for a in range(PASSES)]
+        half = S // 2
+        s_halves = [(0, half), (half, S)]
+        first_codes = keep.tile([P, S], U32, name="first_codes", align_bytes=ALIGN)
+        first_scales = keep.tile([P, S], U8, name="first_scales", align_bytes=ALIGN)
+        second_codes = [
+            keep.tile([P, half], U32, name="second_codes0", tag="x_sb13", align_bytes=ALIGN),
+            placed.tile([P, half], U32, name="second_codes1", offset=lower(behind[0]) + raw_bytes // 2, align_bytes=ALIGN),
+        ]
+        x_codes = {(0, 0, S): first_codes[:]}
+        x_scales = {(0, 0, S): first_scales[:]}
+        for h, (s0, s1) in enumerate(s_halves):
+            x_codes[0, s0, s1] = first_codes[:, s0:s1]
+            x_scales[0, s0, s1] = first_scales[:, s0:s1]
+            x_codes[1, s0, s1] = second_codes[h][:]
+            x_scales[1, s0, s1] = keep.tile([P, half], U8, name=f"second_scales{h}", align_bytes=ALIGN)[:]
 
         def entries(s0, s1):
             return offs_sb[:, s0 // PER_COLUMN : s1 // PER_COLUMN]
 
-        def multiply(acc, a, c, s0, s1):
+        def multiply(acc, a, c, s0, s1, closes):
             (codes, scales), m0 = w_parts[a, c]
             nc.tensor.matmul_mx(
                 out=acc,
                 lhsT=codes[:, m0 : m0 + P].bitcast(FP8X4),
                 lhsT_scale=scales[:, m0 : m0 + P],
-                rhs=x_codes[a][:, s0:s1].bitcast(FP8X4),
-                rhs_scale=x_scales[a][:, s0:s1],
+                rhs=x_codes[a, s0, s1].bitcast(FP8X4),
+                rhs_scale=x_scales[a, s0, s1],
                 start=(a == 0),
-                stop=(a == PASSES - 1),
+                stop=closes,
             )
 
-        half = S // 2
-        s_halves = [(0, half), (half, S)]
         picked = [keep.tile([P, PACK, half], F32, name=f"picked{h}") for h in range(2)]
         for j0 in range(0, PACK, 2):
             for part, (s0, s1) in zip(picked, s_halves):
@@ -162,7 +173,7 @@ def tile_picked_sub_lin_relu_sub_e_kernel(tc, xT, w, b, gate, offs, pos1, pos2, 
         grp_first = keep.tile([P, S, PACK], BF16, name="grp_first", align_bytes=ALIGN)
         for part, (s0, s1) in zip(picked, s_halves):
             interleave(nc.scalar.copy, grp_first[:, s0:s1, :], part[:])
-            quantize(x_codes[0][:, s0:s1], x_scales[0][:, s0:s1], grp_first[:, s0:s1, :])
+            quantize(x_codes[0, s0, s1], x_scales[0, s0, s1], grp_first[:, s0:s1, :])
 
         runs = s_halves
         first = [bank(3 + i, [P, s1 - s0], f"first{i}") for i, (s0, s1) in enumerate(runs)]
@@ -175,9 +186,9 @@ def tile_picked_sub_lin_relu_sub_e_kernel(tc, xT, w, b, gate, offs, pos1, pos2, 
         nc.vector.tensor_copy(grp_second[:, :, 2], x_plane[1, 2].indirect(offs_sb[:]))
         quantize(w_head[0][:], w_head[1][:], w_first_grp[:])
         for acc, (s0, s1) in zip(first, runs):
-            multiply(acc[:], 0, 0, s0, s1)
+            multiply(acc[:], 0, 0, s0, s1, False)
         for c in range(1, AHEAD):
-            multiply(accs[c][:], 0, c, 0, S)
+            multiply(accs[c][:], 0, c, 0, S, False)
         last_half = keep.tile([P, half], BF16, name="last_half", align_bytes=ALIGN)
         nc.scalar.activation(last_half[:], x_plane[1, PACK - 1].indirect(entries(half, S)), COPY)
         nc.vector.tensor_copy(grp_second[:, 0:half, PACK - 1], x_plane[1, PACK - 1].indirect(entries(0, half)))
@@ -185,10 +196,10 @@ def tile_picked_sub_lin_relu_sub_e_kernel(tc, xT, w, b, gate, offs, pos1, pos2, 
 
         def quantize_x(run):
             s0, s1 = runs[run]
-            quantize(x_codes[1][:, s0:s1], x_scales[1][:, s0:s1], grp_second[:, s0:s1, :])
+            quantize(x_codes[1, s0, s1], x_scales[1, s0, s1], grp_second[:, s0:s1, :])
 
         y_sb = [
-            keep.tile([P, S], F32, name="y_sb0", align_bytes=ALIGN),
+            placed.tile([P, S], F32, name="y_sb0", offset=lower(behind[1]), align_bytes=ALIGN),
             placed.tile([P, S], F32, name="y_sb1", offset=lower(behind[-1]), align_bytes=ALIGN),
             keep.tile([P, S], F32, name="y_sb2", align_bytes=ALIGN),
             keep.tile([P, S], F32, name="y_sb3", align_bytes=ALIGN),
@@ -201,14 +212,15 @@ def tile_picked_sub_lin_relu_sub_e_kernel(tc, xT, w, b, gate, offs, pos1, pos2, 
             a, c = piece
             interleave_w(piece)
             quantize_w(piece)
-            multiply(accs[c][:], a, c, 0, S)
+            for s0, s1 in runs if a else [(0, S)]:
+                multiply(accs[c][:, s0:s1], a, c, s0, s1, a == 1 and s1 == S)
 
         interleave_w((1, 0))
         quantize_x(0)
         quantize_w((1, 0))
         quantize_x(1)
         for acc, (s0, s1) in zip(first, runs):
-            multiply(acc[:], 1, 0, s0, s1)
+            multiply(acc[:], 1, 0, s0, s1, True)
         layer_piece((1, 1))
         for acc, (s0, s1) in zip(first, runs):
             nc.vector.tensor_scalar(y_sb[0][:, s0:s1], acc[:], bias(0), 0.0, ADD, MAX)
@@ -253,11 +265,11 @@ def tile_picked_sub_lin_relu_sub_e_kernel(tc, xT, w, b, gate, offs, pos1, pos2, 
                 nc.tensor.transpose(plain[d][:, h, late.index(c), :], values[:, part], ident[:])
 
         rest = [(0, d) for d in range(2, D)] + [(1, d) for d in range(D)] + [(c, d) for d in range(2) for c in late]
-        for c in late:
-            layer_piece((0, c))
         for d, c in enumerate(late):
-            place_products([(0, d)], behind[d - 3])
+            layer_piece((0, c))
+            place_products([(0, d)], (0, c, 1))
             weighed(0, d)
+        for c in late:
             layer_piece((1, c))
         for c in range(1, BLOCKS):
             relu(c)

@@ -51,9 +51,6 @@ def tile_picked_sub_lin_relu_sub_e_kernel(tc, xT, w, b, gate, offs, pos1, pos2, 
 
         w_first = keep.tile([P, PACK, AHEAD * P], F32, name="w_first", align_bytes=ALIGN)
         nc.sync.dma_start(w_first[:], wv[0][:, :, 0 : AHEAD * P])
-        nc.sync.dma_start(offs_sb[:], offs)
-        nc.sync.dma_start(small_rows[0:D, :], gate[:, 0, :])
-        nc.sync.dma_start(small_rows[D : D + BLOCKS, 0:P], b.rearrange("(c p) o -> c (p o)", c=BLOCKS))
         placed = ctx.enter_context(tc.tile_pool(name="placed", bufs=1))
         raw_bytes = 4 * PACK * P
         behind = [(1, 0, 1), (1, 1, 1), (0, 2, 1), (0, 3, 1), (1, 2, 1), (1, 3, 1)]
@@ -72,13 +69,17 @@ def tile_picked_sub_lin_relu_sub_e_kernel(tc, xT, w, b, gate, offs, pos1, pos2, 
             w_loaded[load] = placed.tile([P, PACK, count * P], F32, name=f"w_raw{a}{c0}", offset=lower(load) + raw_bytes // 2, align_bytes=ALIGN)
             for e in range(count):
                 w_raw[a, c0 + e] = w_loaded[load][:, :, e * P : (e + 1) * P]
-        x_loads = [(0, 0, 2), (0, 2, 2)] + [(1, j, 1) for j in range(PACK)]
+        x_loads = [(0, 0, PACK), (1, 0, 2), (1, 2, 1), (1, 3, 1)]
         x_plane = {}
         for a, j0, count in x_loads:
             planes = keep.tile([P, count * T], F32, name=f"x_sb{a}{j0}", tag=f"x_sb{a}{j0}", align_bytes=ALIGN)
             for e in range(count):
                 x_plane[a, j0 + e] = planes[:, e * T : (e + 1) * T]
             nc.sync.dma_start(planes[:], xv[a][:, j0 : j0 + count, :].rearrange("p j t -> p (j t)"))
+            if (a, j0) == (0, 0):
+                nc.sync.dma_start(offs_sb[:], offs)
+                nc.sync.dma_start(small_rows[0:D, :], gate[:, 0, :])
+                nc.sync.dma_start(small_rows[D : D + BLOCKS, 0:P], b.rearrange("(c p) o -> c (p o)", c=BLOCKS))
         for i, (a, c0, count) in enumerate(behind):
             nc.sync.dma_start(w_loaded[a, c0, count][:], wv[a][:, :, c0 * P : (c0 + count) * P])
             for d in {2: range(1), len(behind) - 1: range(1, D)}.get(i, ()):
@@ -166,13 +167,14 @@ def tile_picked_sub_lin_relu_sub_e_kernel(tc, xT, w, b, gate, offs, pos1, pos2, 
             )
 
         picked = [keep.tile([P, PACK, half], F32, name=f"picked{h}") for h in range(2)]
-        for j0 in range(0, PACK, 2):
-            for part, (s0, s1) in zip(picked, s_halves):
-                for j in (j0, j0 + 1):
-                    nc.vector.tensor_copy(part[:, j, :], x_plane[0, j].indirect(entries(s0, s1)))
+        for part, (s0, s1) in zip(picked, s_halves):
+            for j in range(2):
+                nc.vector.tensor_copy(part[:, j, :], x_plane[0, j].indirect(entries(s0, s1)))
+                nc.scalar.activation(part[:, 2 + j, :], x_plane[0, 2 + j].indirect(entries(s0, s1)), COPY)
         grp_first = keep.tile([P, S, PACK], BF16, name="grp_first", align_bytes=ALIGN)
         for part, (s0, s1) in zip(picked, s_halves):
-            interleave(nc.scalar.copy, grp_first[:, s0:s1, :], part[:])
+            interleave(nc.vector.tensor_copy, grp_first[:, s0:s1, :], part[:])
+        for s0, s1 in s_halves:
             quantize(x_codes[0, s0, s1], x_scales[0, s0, s1], grp_first[:, s0:s1, :])
 
         runs = s_halves
@@ -180,8 +182,8 @@ def tile_picked_sub_lin_relu_sub_e_kernel(tc, xT, w, b, gate, offs, pos1, pos2, 
         accs = {c: bank((6, 7, 0)[c - 1], [P, S], f"acc{c}") for c in range(1, BLOCKS)}
         picked_pair = keep.tile([P, 2, S], F32, name="picked_pair")
         grp_second = keep.tile([P, S, PACK], BF16, name="grp_second", align_bytes=ALIGN)
-        for j in range(2):
-            nc.vector.tensor_copy(picked_pair[:, j, :], x_plane[1, j].indirect(offs_sb[:]))
+        nc.vector.tensor_copy(picked_pair[:, 0, :], x_plane[1, 0].indirect(offs_sb[:]))
+        nc.scalar.activation(picked_pair[:, 1, :], x_plane[1, 1].indirect(offs_sb[:]), COPY)
         nc.scalar.copy(grp_second[:, :, 0:2], picked_pair[:].rearrange("p j s -> p s j"))
         nc.vector.tensor_copy(grp_second[:, :, 2], x_plane[1, 2].indirect(offs_sb[:]))
         quantize(w_head[0][:], w_head[1][:], w_first_grp[:])

@@ -191,10 +191,11 @@ def tile_picked_sub_lin_relu_sub_e_kernel(tc, xT, w, b, gate, offs, pos1, pos2, 
             multiply(acc[:], 0, 0, s0, s1, False)
         for c in range(1, AHEAD):
             multiply(accs[c][:], 0, c, 0, S, False)
-        last_half = keep.tile([P, half], BF16, name="last_half", align_bytes=ALIGN)
-        nc.scalar.activation(last_half[:], x_plane[1, PACK - 1].indirect(entries(half, S)), COPY)
-        nc.vector.tensor_copy(grp_second[:, 0:half, PACK - 1], x_plane[1, PACK - 1].indirect(entries(0, half)))
-        nc.vector.tensor_copy(grp_second[:, half:S, PACK - 1], last_half[:])
+        own = 5 * S // 8
+        last_part = keep.tile([P, S - own], BF16, name="last_part", align_bytes=ALIGN)
+        nc.scalar.activation(last_part[:], x_plane[1, PACK - 1].indirect(entries(own, S)), COPY)
+        nc.vector.tensor_copy(grp_second[:, 0:own, PACK - 1], x_plane[1, PACK - 1].indirect(entries(0, own)))
+        nc.vector.tensor_copy(grp_second[:, own:S, PACK - 1], last_part[:])
 
         def quantize_x(run):
             s0, s1 = runs[run]
@@ -292,16 +293,26 @@ def tile_picked_sub_lin_relu_sub_e_kernel(tc, xT, w, b, gate, offs, pos1, pos2, 
         add_turn(sum1, 1, 2, range(D))
         fetch(3, 3)
         add_turn(sum1, 1, 3, range(D))
-        backs = []
-        for h in range(V_HALVES):
-            if h == 1:
-                back1 = turn_back(1, copy_out(sum1, "turned1", "turned1"), 5)
-            scaled = keep.tile([P, len(plain_turns), len(late) * P], F32, name=f"scaled{h}", align_bytes=ALIGN)
-            for e, d in enumerate(plain_turns):
-                column = gate_last[:] if (d, h) == (D - 1, V_HALVES - 1) else cols[:, h, d : d + 1]
-                nc.scalar.activation(scaled[:, e, :], plain[d][:, h, :, :].rearrange("p c m -> p (c m)"), COPY, scale=column)
-            backs.append(bank((7, 0)[h], [P, len(late) * P], f"back_late{h}"))
-            turn_adding(backs[h], [(i, scaled[:, e, i * P : (i + 1) * P]) for e in range(len(plain_turns)) for i in range(len(late))])
+        def weigh(d, h, members, column):
+            first_member, width = members[0], len(members) * P
+            scaled = keep.tile([P, width], F32, name=f"scaled{d}{h}{first_member}", align_bytes=ALIGN)
+            source = plain[d][:, h, first_member : first_member + len(members), :]
+            nc.scalar.activation(scaled[:], source.rearrange("p c m -> p (c m)"), COPY, scale=column)
+            return {i: scaled[:, e * P : (e + 1) * P] for e, i in enumerate(members)}
+
+        both = range(len(late))
+        back_first = bank(7, [P, len(late) * P], "back_first")
+        weighed_first = [weigh(d, 0, both, cols[:, 0, d : d + 1]) for d in plain_turns]
+        turn_adding(back_first, [(i, part[i]) for part in weighed_first for i in both])
+        back1 = turn_back(1, copy_out(sum1, "turned1", "turned1"), 5)
+        back_last = [bank((0, 1)[i], [P, P], f"back_last{i}") for i in both]
+        opening = weigh(plain_turns[0], 1, both, cols[:, 1, plain_turns[0] : plain_turns[0] + 1])
+        for i in both:
+            nc.tensor.matmul(back_last[i][:], opening[i], ident[:], start=True, stop=False, is_transpose=True)
+        for i in both:
+            column = gate_last[:] if i == both[-1] else cols[:, 1, D - 1 : D]
+            closing = weigh(D - 1, 1, [i], column)
+            nc.tensor.matmul(back_last[i][:], closing[i], ident[:], start=False, stop=True, is_transpose=True)
         totals = keep.tile([P, 2, V], F32, name="totals", tag="gate_last", align_bytes=ALIGN)
         for c, back in enumerate((back0, back1)):
             nc.scalar.copy(totals[:, c, :], back[:])
@@ -311,7 +322,10 @@ def tile_picked_sub_lin_relu_sub_e_kernel(tc, xT, w, b, gate, offs, pos1, pos2, 
         for i, c in enumerate(late):
             nc.vector.tensor_tensor(pair[:, i, :], prods[c, 0], prods[c, 1], ADD)
         late_out = out.rearrange("(c p) v -> p c v", c=BLOCKS)[:, late[0] : late[-1] + 1, :]
-        for h, part in enumerate(v_halves):
-            total = keep.tile([P, len(late), P], F32, name=f"total_late{h}", align_bytes=ALIGN)
-            nc.vector.tensor_tensor(total[:], pair[:, :, part], backs[h][:].rearrange("p (c m) -> p c m", c=len(late)), ADD)
-            nc.sync.dma_start(late_out[:, :, part], total[:])
+        total = keep.tile([P, len(late), P], F32, name="total_late", align_bytes=ALIGN)
+        nc.vector.tensor_tensor(total[:], pair[:, :, 0:P], back_first[:].rearrange("p (c m) -> p c m", c=len(late)), ADD)
+        nc.sync.dma_start(late_out[:, :, 0:P], total[:])
+        for i, c in enumerate(late):
+            last = keep.tile([P, P], F32, name=f"total_last{c}", align_bytes=ALIGN)
+            nc.vector.tensor_tensor(last[:], pair[:, i, P:V], back_last[i][:], ADD)
+            nc.sync.dma_start(ov[c][:, P:V], last[:])

@@ -262,16 +262,19 @@ def tile_picked_sub_lin_relu_sub_e_kernel(tc, xT, w, b, gate, offs, pos1, pos2, 
         plain = {d: bank(d, [P, V_HALVES, len(late), P], f"plain{d}") for d in plain_turns}
 
         def fetch(c, d):
-            values = keep.tile([P, V], F32, name=f"fetched{c}{d}", align_bytes=ALIGN)
+            values = keep.tile([P, V], F32, name=f"fetched{c}{d}", tag=f"fetched{c}{d}", align_bytes=ALIGN)
             nc.scalar.activation(values[:], y_sb[c][:].indirect(pos_sb[d][:]), COPY)
             for h, part in enumerate(v_halves):
                 nc.tensor.transpose(plain[d][:, h, late.index(c), :], values[:, part], ident[:])
 
         rest = [(0, d) for d in range(2, D)] + [(1, d) for d in range(D)] + [(c, d) for d in range(2) for c in late]
+        sum0 = bank(1, [P, V], "sum0")
+        turns0 = (0, 2, 1, 3)
         for d, c in enumerate(late):
             layer_piece((0, c))
             place_products([(0, d)], (0, c, 1))
             weighed(0, d)
+        add_turn(sum0, 0, 0, turns0)
         for c in late:
             layer_piece((1, c))
         for c in range(1, BLOCKS):
@@ -279,9 +282,7 @@ def tile_picked_sub_lin_relu_sub_e_kernel(tc, xT, w, b, gate, offs, pos1, pos2, 
         place_products(rest, behind[-1])
         for c, d in rest:
             weighed(c, d)
-        sum0 = bank(1, [P, V], "sum0")
-        turns0 = (2, 0, 1, 3)
-        for d in turns0:
+        for d in turns0[1:]:
             add_turn(sum0, 0, d, turns0)
         fetch(2, 2)
         sum1 = bank(6, [P, V], "sum1")
@@ -289,9 +290,9 @@ def tile_picked_sub_lin_relu_sub_e_kernel(tc, xT, w, b, gate, offs, pos1, pos2, 
         fetch(2, 3)
         add_turn(sum1, 1, 1, range(D))
         fetch(3, 2)
-        back0 = turn_back(0, copy_out(sum0, "turned0", "turned0"), 4)
         add_turn(sum1, 1, 2, range(D))
         fetch(3, 3)
+        back0 = turn_back(0, copy_out(sum0, "turned0", "fetched23"), 4)
         add_turn(sum1, 1, 3, range(D))
         def weigh(d, h, members, column):
             first_member, width = members[0], len(members) * P
@@ -314,9 +315,11 @@ def tile_picked_sub_lin_relu_sub_e_kernel(tc, xT, w, b, gate, offs, pos1, pos2, 
             closing = weigh(D - 1, 1, [i], column)
             nc.tensor.matmul(back_last[i][:], closing[i], ident[:], start=False, stop=True, is_transpose=True)
         totals = keep.tile([P, 2, V], F32, name="totals", tag="gate_last", align_bytes=ALIGN)
-        for c, back in enumerate((back0, back1)):
-            nc.scalar.copy(totals[:, c, :], back[:])
-            nc.sync.dma_start(ov[c], totals[:, c, :])
+        nc.scalar.copy(totals[:, 0, :], back0[:])
+        nc.sync.dma_start(ov[0], totals[:, 0, :])
+        for part in v_halves:
+            nc.scalar.copy(totals[:, 1, part], back1[:, part])
+            nc.sync.dma_start(ov[1][:, part], totals[:, 1, part])
 
         pair = keep.tile([P, len(late), V], F32, name="pair", align_bytes=ALIGN)
         for i, c in enumerate(late):

from contextlib import ExitStack

import concourse.mybir as mybir
from concourse.masks import make_identity

F32 = mybir.dt.float32
BF16 = mybir.dt.bfloat16
U32 = mybir.dt.uint32
U16 = mybir.dt.uint16
U8 = mybir.dt.uint8
FP8X4 = mybir.dt.float8_e4m3fn_x4
MULT = mybir.AluOpType.mult
ADD = mybir.AluOpType.add
MAX = mybir.AluOpType.max
RELU = mybir.ActivationFunctionType.Relu
COPY = mybir.ActivationFunctionType.Copy

K, T, D, S, V, N = 1024, 2048, 4, 512, 256, 512
P = 128
PACK = 4
PASSES = K // (P * PACK)
BLOCKS = N // P
V_HALVES = V // P
PER_COLUMN = 16
ALIGN = 64
AHEAD = 2
FLOPS = 2 * N * K * S
BYTES = 4 * (K * T + K * N + N + D * V + N * V) + 2 * P * (S + D * V) // PER_COLUMN


def tile_picked_sub_lin_relu_sub_e_kernel(tc, xT, w, b, gate, offs, pos1, pos2, pos3, pos4, out):
    nc = tc.nc
    positions = (pos1, pos2, pos3, pos4)
    with ExitStack() as ctx:
        lists = ctx.enter_context(tc.tile_pool(name="lists", bufs=1))
        keep = ctx.enter_context(tc.tile_pool(name="keep", bufs=1))
        psum = ctx.enter_context(tc.psum_pool(name="psum", bufs=1))

        def bank(number, shape, name):
            return psum.tile(shape, F32, name=name, tag=f"bank{number}")

        xv = xT.rearrange("(a p j) t -> a p j t", a=PASSES, j=PACK)
        wv = w.rearrange("(a p j) m -> a p j m", a=PASSES, j=PACK)
        ov = out.rearrange("(c p) v -> c p v", c=BLOCKS)
        v_halves = [slice(h * P, (h + 1) * P) for h in range(V_HALVES)]

        small_rows = keep.tile([P, V], F32, name="small_rows")
        nc.vector.memset(small_rows[:], 0.0)
        offs_sb = lists.tile([P, S // PER_COLUMN], U16, name="offs_sb")
        pos_sb = [lists.tile([P, V // PER_COLUMN], U16, name=f"pos_sb{d}") for d in range(D)]

        w_first = keep.tile([P, PACK, AHEAD * P], F32, name="w_first", align_bytes=ALIGN)
        nc.sync.dma_start(w_first[:], wv[0][:, :, 0 : AHEAD * P])
        placed = ctx.enter_context(tc.tile_pool(name="placed", bufs=1))
        raw_bytes = 4 * PACK * P
        behind = [(1, 0, 1), (1, 1, 1), (0, 2, 1), (0, 3, 1), (1, 2, 1), (1, 3, 1)]
        stretch = 4 * raw_bytes

        def lower(load):
            return behind.index(load) * stretch

        def upper(load):
            return lower(load) + raw_bytes

        w_loaded = {}
        w_raw = {}
        for load in behind:
            a, c0, count = load
            w_loaded[load] = placed.tile([P, PACK, count * P], F32, name=f"w_raw{a}{c0}", offset=lower(load) + raw_bytes // 2, align_bytes=ALIGN)
            for e in range(count):
                w_raw[a, c0 + e] = w_loaded[load][:, :, e * P : (e + 1) * P]
        x_loads = [(0, 0, PACK), (1, 0, 2), (1, 2, 1), (1, 3, 1)]
        x_plane = {}
        for a, j0, count in x_loads:
            planes = keep.tile([P, count * T], F32, name=f"x_sb{a}{j0}", tag=f"x_sb{a}{j0}", align_bytes=ALIGN)
            for e in range(count):
                x_plane[a, j0 + e] = planes[:, e * T : (e + 1) * T]
            nc.sync.dma_start(planes[:], xv[a][:, j0 : j0 + count, :].rearrange("p j t -> p (j t)"))
            if (a, j0) == (0, 0):
                nc.sync.dma_start(offs_sb[:], offs)
                nc.sync.dma_start(small_rows[0:D, :], gate[:, 0, :])
                nc.sync.dma_start(small_rows[D : D + BLOCKS, 0:P], b.rearrange("(c p) o -> c (p o)", c=BLOCKS))
        for i, (a, c0, count) in enumerate(behind):
            nc.sync.dma_start(w_loaded[a, c0, count][:], wv[a][:, :, c0 * P : (c0 + count) * P])
            for d in {2: range(1), len(behind) - 1: range(1, D)}.get(i, ()):
                nc.sync.dma_start(pos_sb[d][:], positions[d])

        ident = keep.tile([P, P], F32, name="ident")
        make_identity(nc, ident[:])
        small_cols = bank(0, [P, V_HALVES, P], "small_cols")
        for h, part in enumerate(v_halves):
            nc.tensor.transpose(small_cols[:, h, :], small_rows[:, part], ident[:])
        cols = keep.tile([P, V_HALVES, D + BLOCKS], F32, name="cols")
        nc.scalar.copy(cols[:], small_cols[:, :, 0 : D + BLOCKS])
        gate_sb = keep.tile([P, D, V], F32, name="gate_sb")
        turns_a_bank = 2
        for d0 in range(0, D, turns_a_bank):
            spread = bank(1 + d0 // turns_a_bank, [P, turns_a_bank, V], "spread")
            for e in range(turns_a_bank):
                for h, part in enumerate(v_halves):
                    nc.tensor.transpose(spread[:, e, part], cols[:, h, d0 + e : d0 + e + 1].to_broadcast([P, P]), ident[:])
            nc.scalar.copy(gate_sb[:, d0 : d0 + turns_a_bank, :], spread[:])

        gate_last = keep.tile([P, 1], F32, name="gate_last", tag="gate_last", align_bytes=ALIGN)
        nc.scalar.copy(gate_last[:], small_cols[:, V_HALVES - 1, D - 1 : D])

        def bias(c):
            return cols[:, 0, D + c : D + c + 1]

        def interleave(copy, grouped, planes):
            copy(grouped.rearrange("p (g i) j -> p g j i", i=2), planes.rearrange("p j (g i) -> p g j i", i=2))

        def quantize(codes, scales, grouped):
            nc.vector.quantize_mx(out=codes.bitcast(FP8X4), scales=scales, in_=grouped.rearrange("p s j -> p (s j)"))

        def operand(name, width, tag):
            codes = keep.tile([P, width], U32, name=f"{name}_codes", tag=tag, align_bytes=ALIGN)
            scales = keep.tile([P, width], U8, name=f"{name}_scales", align_bytes=ALIGN)
            return codes, scales

        w_first_grp = keep.tile([P, AHEAD * P, PACK], BF16, name="w_first_grp", align_bytes=ALIGN)
        interleave(nc.scalar.copy, w_first_grp[:], w_first[:])
        w_head = operand("w_head", AHEAD * P, "x_sb12")
        w_parts = {(0, c): (w_head, c * P) for c in range(AHEAD)}
        w_rest = operand("w_rest", len(w_raw) * P, "w_rest")
        w_grp = {}
        for i, (a, c) in enumerate(w_raw):
            w_parts[a, c] = (w_rest, i * P)
            w_grp[a, c] = keep.tile([P, P, PACK], BF16, name=f"w_grp{a}{c}", align_bytes=ALIGN)

        def interleave_w(piece):
            interleave(nc.scalar.copy, w_grp[piece][:], w_raw[piece])

        def quantize_w(piece):
            (codes, scales), m0 = w_parts[piece]
            quantize(codes[:, m0 : m0 + P], scales[:, m0 : m0 + P], w_grp[piece][:])

        half = S // 2
        s_halves = [(0, half), (half, S)]
        first_codes = keep.tile([P, S], U32, name="first_codes", align_bytes=ALIGN)
        first_scales = keep.tile([P, S], U8, name="first_scales", align_bytes=ALIGN)
        second_codes = [
            keep.tile([P, half], U32, name="second_codes0", tag="x_sb13", align_bytes=ALIGN),
            placed.tile([P, half], U32, name="second_codes1", offset=lower(behind[0]) + raw_bytes // 2, align_bytes=ALIGN),
        ]
        x_codes = {(0, 0, S): first_codes[:]}
        x_scales = {(0, 0, S): first_scales[:]}
        for h, (s0, s1) in enumerate(s_halves):
            x_codes[0, s0, s1] = first_codes[:, s0:s1]
            x_scales[0, s0, s1] = first_scales[:, s0:s1]
            x_codes[1, s0, s1] = second_codes[h][:]
            x_scales[1, s0, s1] = keep.tile([P, half], U8, name=f"second_scales{h}", align_bytes=ALIGN)[:]

        def entries(s0, s1):
            return offs_sb[:, s0 // PER_COLUMN : s1 // PER_COLUMN]

        def multiply(acc, a, c, s0, s1, closes):
            (codes, scales), m0 = w_parts[a, c]
            nc.tensor.matmul_mx(
                out=acc,
                lhsT=codes[:, m0 : m0 + P].bitcast(FP8X4),
                lhsT_scale=scales[:, m0 : m0 + P],
                rhs=x_codes[a, s0, s1].bitcast(FP8X4),
                rhs_scale=x_scales[a, s0, s1],
                start=(a == 0),
                stop=closes,
            )

        picked = [keep.tile([P, PACK, half], F32, name=f"picked{h}") for h in range(2)]
        for part, (s0, s1) in zip(picked, s_halves):
            for j in range(2):
                nc.vector.tensor_copy(part[:, j, :], x_plane[0, j].indirect(entries(s0, s1)))
                nc.scalar.activation(part[:, 2 + j, :], x_plane[0, 2 + j].indirect(entries(s0, s1)), COPY)
        grp_first = keep.tile([P, S, PACK], BF16, name="grp_first", align_bytes=ALIGN)
        for part, (s0, s1) in zip(picked, s_halves):
            interleave(nc.vector.tensor_copy, grp_first[:, s0:s1, :], part[:])
        for s0, s1 in s_halves:
            quantize(x_codes[0, s0, s1], x_scales[0, s0, s1], grp_first[:, s0:s1, :])

        runs = s_halves
        first = [bank(3 + i, [P, s1 - s0], f"first{i}") for i, (s0, s1) in enumerate(runs)]
        accs = {c: bank((6, 7, 0)[c - 1], [P, S], f"acc{c}") for c in range(1, BLOCKS)}
        picked_pair = keep.tile([P, 2, S], F32, name="picked_pair")
        grp_second = keep.tile([P, S, PACK], BF16, name="grp_second", align_bytes=ALIGN)
        nc.vector.tensor_copy(picked_pair[:, 0, :], x_plane[1, 0].indirect(offs_sb[:]))
        nc.scalar.activation(picked_pair[:, 1, :], x_plane[1, 1].indirect(offs_sb[:]), COPY)
        nc.scalar.copy(grp_second[:, :, 0:2], picked_pair[:].rearrange("p j s -> p s j"))
        nc.vector.tensor_copy(grp_second[:, :, 2], x_plane[1, 2].indirect(offs_sb[:]))
        quantize(w_head[0][:], w_head[1][:], w_first_grp[:])
        for acc, (s0, s1) in zip(first, runs):
            multiply(acc[:], 0, 0, s0, s1, False)
        for c in range(1, AHEAD):
            multiply(accs[c][:], 0, c, 0, S, False)
        own = 5 * S // 8
        last_part = keep.tile([P, S - own], BF16, name="last_part", align_bytes=ALIGN)
        nc.scalar.activation(last_part[:], x_plane[1, PACK - 1].indirect(entries(own, S)), COPY)
        nc.vector.tensor_copy(grp_second[:, 0:own, PACK - 1], x_plane[1, PACK - 1].indirect(entries(0, own)))
        nc.vector.tensor_copy(grp_second[:, own:S, PACK - 1], last_part[:])

        def quantize_x(run):
            s0, s1 = runs[run]
            quantize(x_codes[1, s0, s1], x_scales[1, s0, s1], grp_second[:, s0:s1, :])

        y_sb = [
            placed.tile([P, S], F32, name="y_sb0", offset=lower(behind[1]), align_bytes=ALIGN),
            placed.tile([P, S], F32, name="y_sb1", offset=lower(behind[-1]), align_bytes=ALIGN),
            keep.tile([P, S], F32, name="y_sb2", align_bytes=ALIGN),
            keep.tile([P, S], F32, name="y_sb3", align_bytes=ALIGN),
        ]

        def relu(c):
            nc.scalar.activation(y_sb[c][:], accs[c][:], RELU, bias=bias(c))

        def layer_piece(piece):
            a, c = piece
            interleave_w(piece)
            quantize_w(piece)
            for s0, s1 in runs if a else [(0, S)]:
                multiply(accs[c][:, s0:s1], a, c, s0, s1, a == 1 and s1 == S)

        interleave_w((1, 0))
        quantize_x(0)
        quantize_w((1, 0))
        quantize_x(1)
        for acc, (s0, s1) in zip(first, runs):
            multiply(acc[:], 1, 0, s0, s1, True)
        layer_piece((1, 1))
        for acc, (s0, s1) in zip(first, runs):
            nc.vector.tensor_scalar(y_sb[0][:, s0:s1], acc[:], bias(0), 0.0, ADD, MAX)

        late = (2, 3)
        plain_turns = (2, 3)
        prods = {}

        def place_products(members, piece):
            group = placed.tile([P, len(members), V], F32, name=f"prods{piece[0]}{piece[1]}", offset=upper(piece), align_bytes=ALIGN)
            for e, member in enumerate(members):
                prods[member] = group[:, e, :]

        def weighed(c, d):
            nc.vector.tensor_tensor(prods[c, d], y_sb[c][:].indirect(pos_sb[d][:]), gate_sb[:, d, :], MULT)

        def turn_adding(target, sources):
            for i, (e, source) in enumerate(sources):
                nc.tensor.matmul(target[:, e * P : (e + 1) * P], source, ident[:], start=(i == 0), stop=(i == len(sources) - 1), is_transpose=True)

        def add_turn(total, c, d, turns):
            for h, part in enumerate(v_halves):
                opens, closes = (d, h) == (turns[0], 0), (d, h) == (turns[-1], V_HALVES - 1)
                nc.tensor.matmul(total[:, part], prods[c, d][:, part], ident[:], start=opens, stop=closes, is_transpose=True)

        def copy_out(source, name, tag):
            target = keep.tile([P, V], F32, name=name, tag=tag, align_bytes=ALIGN)
            nc.scalar.copy(target[:], source[:])
            return target

        def turn_back(c, turned, number):
            back = bank(number, [P, V], f"back{c}")
            turn_adding(back, [(h, turned[:, part]) for h, part in enumerate(v_halves)])
            return back

        plain = {d: bank(d, [P, V_HALVES, len(late), P], f"plain{d}") for d in plain_turns}

        def fetch(c, d):
            values = keep.tile([P, V], F32, name=f"fetched{c}{d}", tag=f"fetched{c}{d}", align_bytes=ALIGN)
            nc.scalar.activation(values[:], y_sb[c][:].indirect(pos_sb[d][:]), COPY)
            for h, part in enumerate(v_halves):
                nc.tensor.transpose(plain[d][:, h, late.index(c), :], values[:, part], ident[:])

        rest = [(0, d) for d in range(2, D)] + [(1, d) for d in range(D)] + [(c, d) for d in range(2) for c in late]
        sum0 = bank(1, [P, V], "sum0")
        turns0 = (0, 2, 1, 3)
        for d, c in enumerate(late):
            layer_piece((0, c))
            place_products([(0, d)], (0, c, 1))
            weighed(0, d)
        add_turn(sum0, 0, 0, turns0)
        for c in late:
            layer_piece((1, c))
        for c in range(1, BLOCKS):
            relu(c)
        place_products(rest, behind[-1])
        for c, d in rest:
            weighed(c, d)
        for d in turns0[1:]:
            add_turn(sum0, 0, d, turns0)
        fetch(2, 2)
        sum1 = bank(6, [P, V], "sum1")
        add_turn(sum1, 1, 0, range(D))
        fetch(2, 3)
        add_turn(sum1, 1, 1, range(D))
        fetch(3, 2)
        add_turn(sum1, 1, 2, range(D))
        fetch(3, 3)
        back0 = turn_back(0, copy_out(sum0, "turned0", "fetched23"), 4)
        add_turn(sum1, 1, 3, range(D))
        def weigh(d, h, members, column):
            first_member, width = members[0], len(members) * P
            scaled = keep.tile([P, width], F32, name=f"scaled{d}{h}{first_member}", align_bytes=ALIGN)
            source = plain[d][:, h, first_member : first_member + len(members), :]
            nc.scalar.activation(scaled[:], source.rearrange("p c m -> p (c m)"), COPY, scale=column)
            return {i: scaled[:, e * P : (e + 1) * P] for e, i in enumerate(members)}

        both = range(len(late))
        back_first = bank(7, [P, len(late) * P], "back_first")
        weighed_first = [weigh(d, 0, both, cols[:, 0, d : d + 1]) for d in plain_turns]
        turn_adding(back_first, [(i, part[i]) for part in weighed_first for i in both])
        back1 = turn_back(1, copy_out(sum1, "turned1", "turned1"), 5)
        back_last = [bank((0, 1)[i], [P, P], f"back_last{i}") for i in both]
        opening = weigh(plain_turns[0], 1, both, cols[:, 1, plain_turns[0] : plain_turns[0] + 1])
        for i in both:
            nc.tensor.matmul(back_last[i][:], opening[i], ident[:], start=True, stop=False, is_transpose=True)
        for i in both:
            column = gate_last[:] if i == both[-1] else cols[:, 1, D - 1 : D]
            closing = weigh(D - 1, 1, [i], column)
            nc.tensor.matmul(back_last[i][:], closing[i], ident[:], start=False, stop=True, is_transpose=True)
        totals = keep.tile([P, 2, V], F32, name="totals", tag="gate_last", align_bytes=ALIGN)
        nc.scalar.copy(totals[:, 0, :], back0[:])
        nc.sync.dma_start(ov[0], totals[:, 0, :])
        for part in v_halves:
            nc.scalar.copy(totals[:, 1, part], back1[:, part])
            nc.sync.dma_start(ov[1][:, part], totals[:, 1, part])

        pair = keep.tile([P, len(late), V], F32, name="pair", align_bytes=ALIGN)
        for i, c in enumerate(late):
            nc.vector.tensor_tensor(pair[:, i, :], prods[c, 0], prods[c, 1], ADD)
        late_out = out.rearrange("(c p) v -> p c v", c=BLOCKS)[:, late[0] : late[-1] + 1, :]
        total = keep.tile([P, len(late), P], F32, name="total_late", align_bytes=ALIGN)
        nc.vector.tensor_tensor(total[:], pair[:, :, 0:P], back_first[:].rearrange("p (c m) -> p c m", c=len(late)), ADD)
        nc.sync.dma_start(late_out[:, :, 0:P], total[:])
        for i, c in enumerate(late):
            last = keep.tile([P, P], F32, name=f"total_last{c}", align_bytes=ALIGN)
            nc.vector.tensor_tensor(last[:], pair[:, i, P:V], back_last[i][:], ADD)
            nc.sync.dma_start(ov[c][:, P:V], last[:])
